import numpy as np
import ml_dtypes


def mxq(x, axis, fmt="e4m3"):
    dtype, down = {"e4m3": (ml_dtypes.float8_e4m3fn, 7), "e5m2": (ml_dtypes.float8_e5m2, 14)}[fmt]
    v = np.moveaxis(np.asarray(x, np.float32).astype(ml_dtypes.bfloat16).astype(np.float64), axis, -1)
    blocks = v.reshape(v.shape[:-1] + (-1, 32))
    amax = np.abs(blocks).max(-1, keepdims=True)
    byte = np.maximum(np.where(amax > 0, np.frexp(amax)[1] - 1 + 127, 0) - down, 1)
    scale = np.exp2(byte - 127.0)
    codes = (blocks / scale).astype(np.float32).astype(dtype).astype(np.float64)
    return np.moveaxis((codes * scale).reshape(v.shape), -1, axis)


WIDE = False


def mx_kscale(k):
    if not WIDE:
        return np.ones(k)
    levels = np.array([10, -10, 5, -5, 0])
    if k % 512:
        return np.exp2(np.random.permutation(np.resize(levels, k // 32))).repeat(32)
    a = np.empty((k // 512, 16))
    for p in range(k // 512):
        a[p, :8] = np.random.permutation(np.resize(levels, 8))
        for g in range(8):
            far = levels[np.abs(levels - a[p, g]) >= 10]
            a[p, g + 8] = far[np.random.randint(len(far))]
    return np.exp2(a.ravel()).repeat(32)


def f64(x):
    return np.asarray(x).astype(np.float64)


def striped(idx):
    return np.tile(idx.reshape(-1, 16).T, (8, 1)).astype(np.uint16)


def unstriped(offs):
    return offs[:16].T.reshape(-1).astype(np.int64)


K, T, E, C, N = 1536, 1280, 15, 256, 128
TOP = 3


def by_expert(wq, xq):
    return np.concatenate([wq[e].T @ xq[:, e * C:(e + 1) * C] for e in range(E)], axis=1)


def setup_inputs():
    n = np.random.standard_normal
    s = mx_kscale(K)[:, None]
    deal = np.repeat(np.arange(E), C).reshape(TOP, T)[:, np.random.permutation(T)]
    deal = np.take_along_axis(deal, np.argsort(np.random.rand(TOP, T), axis=0), axis=0)
    for _ in range(8):
        s_, t_ = np.random.permutation(T).reshape(2, -1); r = np.random.randint(TOP, size=T // 2); x, y = deal[r, s_].copy(), deal[r, t_].copy()
        ok = ~((deal[:, s_] == y).any(0) | (deal[:, t_] == x).any(0)); deal[r[ok], s_[ok]] = y[ok]; deal[r[ok], t_[ok]] = x[ok]
    order = np.lexsort((np.random.rand(TOP * T), deal.reshape(-1)))
    slot_token = order % T; pos = np.empty(TOP * T, np.int64); pos[order] = np.arange(TOP * T); pos = pos.reshape(TOP, T)
    g = np.random.uniform(0.5, 1.5, (TOP, T)); g = g / g.sum(0)
    return {
        "xT": (n((K, T)) * s).astype(np.float32),
        "w": (n((E, K, N)) / np.sqrt(K) / s[None]).astype(np.float32),
        "b": (0.3 * n((N, E))).astype(np.float32),
        "gate": np.stack([np.tile(r, (N, 1)) for r in g]).astype(np.float32),
        "offs": striped(slot_token),
        "pos1": striped(pos[0]),
        "pos2": striped(pos[1]),
        "pos3": striped(pos[2]),
    }


def reference(xT, w, b, gate, offs, pos1, pos2, pos3):
    idx = unstriped(offs)
    xq = mxq(f64(xT)[:, idx], 0, "e4m3")
    y = by_expert(mxq(f64(w), 1, "e4m3"), xq)
    y = y + np.repeat(f64(b), C, axis=1)
    return sum(f64(gate[r]) * y[:, unstriped(p)] for r, p in enumerate((pos1, pos2, pos3)))

@@ -1,0 +1,227 @@
+from contextlib import ExitStack
+
+import concourse.mybir as mybir
+
+F32 = mybir.dt.float32
+BF16 = mybir.dt.bfloat16
+U32 = mybir.dt.uint32
+U16 = mybir.dt.uint16
+U8 = mybir.dt.uint8
+FP8X4 = mybir.dt.float8_e4m3fn_x4
+IDENTITY = mybir.ActivationFunctionType.Identity
+MULT = mybir.AluOpType.mult
+ADD = mybir.AluOpType.add
+
+P = 128
+PACK = 4
+PASS_K = P * PACK
+FLOPS = 2 * 1536 * 128 * 3840
+
+TOKEN_CHUNKS = ((0, 512, 0), (512, 512, 0), (1024, 256, 0))
+WEIGHT_UNITS = 4
+X0_CHUNKS = ((0, 512, 512), (512, 512, 256), (1024, 256, 160))
+EARLY = 960
+GPSIMD_CHUNKS = (3, 6)
+LATE_AFTER = (4, 5, 7, 8, 10)
+GROUPS = (768, 768, 768, 768, 512, 256)
+OUT_CHUNKS = ((0, 512), (512, 512), (1024, 256))
+
+
+def tile_moe_tk_lin_bias_kernel(tc, xT, w, b, gate, offs, pos1, pos2, pos3, out):
+    nc = tc.nc
+    K, T = xT.shape
+    E, N = w.shape[0], w.shape[2]
+    S = offs.shape[1] * 16
+    C = S // E
+    passes = K // PASS_K
+    units = E * passes
+    x_view = xT.rearrange("(a p j) t -> a p j t", p=P, j=PACK)
+    w_view = w.rearrange("e (a p j) n -> p (e a) (j n)", p=P, j=PACK)
+
+    with ExitStack() as ctx:
+        held = ctx.enter_context(tc.tile_pool(name="held", bufs=1))
+        raws = ctx.enter_context(tc.tile_pool(name="raws", bufs=8))
+        rounds = ctx.enter_context(tc.tile_pool(name="rounds", bufs=7))
+        psum = ctx.enter_context(tc.psum_pool(name="psum", bufs=8))
+
+        offs_sb = held.tile([P, S // 16], U16, name="offs_sb")
+        pos_sb = [held.tile([P, T // 16], U16, name=f"pos{r}_sb") for r in range(3)]
+        gates = held.tile([P, 3, T], F32, name="gates")
+        x_codes = [held.tile([P, T], U32, name=f"x_codes{a}", align_bytes=64) for a in range(passes)]
+        x_scales = held.tile([P, T], U8, name="x_scales", align_bytes=64)
+        s_codes = [held.tile([P, S], U32, name=f"s_codes{a}", align_bytes=64) for a in range(passes - 1)]
+        s_scales = held.tile([P, S], U8, name="s_scales", align_bytes=64)
+        w_codes = []
+        w_scales = []
+        y = held.tile([P, S], F32, name="y")
+
+        nc.gpsimd.memset(x_scales[:], 0)
+
+        raw_x = {}
+
+        def load_x(a, token_chunks):
+            for t0, tw, vec in token_chunks:
+                raw = raws.tile([P, PACK, tw], F32, name="raw")
+                nc.sync.dma_start(raw[:], x_view[a][:, :, t0 : t0 + tw])
+                raw_x[a, t0] = raw
+
+        def quantize_x(a, chunk):
+            for t0, tw, vec in ((X0_CHUNKS if a == 0 else TOKEN_CHUNKS)[chunk],):
+                raw = raw_x[a, t0]
+                rounded = rounds.tile([P, tw, PACK], BF16, name="rounded", align_bytes=64)
+                src = raw[:].rearrange("p j (c i) -> p c j i", i=4)
+                dst = rounded[:].rearrange("p (c i) j -> p c j i", i=4)
+                cut = vec // 4
+                if vec:
+                    nc.vector.tensor_copy(dst[:, :cut], src[:, :cut])
+                if vec < tw:
+                    nc.scalar.copy(dst[:, cut:], src[:, cut:])
+                nc.vector.quantize_mx(
+                    out=x_codes[a][:, t0 : t0 + tw].bitcast(FP8X4),
+                    scales=x_scales[4 * a : P, t0 : t0 + tw],
+                    in_=rounded[:].rearrange("p t j -> p (t j)"),
+                )
+
+        raw_w = {}
+
+        def load_w(u0, n_units):
+            raw = raws.tile([P, n_units, PACK * N], F32, name="raw")
+            nc.sync.dma_start(raw[:], w_view[:, u0 : u0 + n_units, :])
+            raw_w[u0] = raw
+
+        def quantize_w(u0, n_units):
+            raw = raw_w[u0]
+            chunk = u0 // WEIGHT_UNITS
+            if chunk in LATE_AFTER:
+                rounded = held.tile([P, n_units, N, PACK], BF16, tag=f"late{chunk}", name="rounded_late", align_bytes=64)
+            else:
+                rounded = rounds.tile([P, n_units, N, PACK], BF16, name="rounded", align_bytes=64)
+            codes = held.tile([P, n_units, N], U32, name=f"w_codes{u0}", align_bytes=64)
+            scales = held.tile([P, n_units, N], U8, name=f"w_scales{u0}", align_bytes=64)
+            for i in range(n_units):
+                w_codes.append(codes[:, i, :])
+                w_scales.append(scales[:, i, :])
+            src = raw[:].rearrange("p u (j c i) -> p u c j i", j=PACK, i=4)
+            dst = rounded[:].rearrange("p u (c i) j -> p u c j i", i=4)
+            if u0 // WEIGHT_UNITS in GPSIMD_CHUNKS:
+                for i in range(n_units):
+                    nc.gpsimd.tensor_scalar(dst[:, i], src[:, i], 1.0, 0.0, MULT, ADD)
+            else:
+                nc.scalar.copy(dst, src)
+            nc.vector.quantize_mx(
+                out=codes[:].rearrange("p u n -> p (u n)").bitcast(FP8X4),
+                scales=scales[:].rearrange("p u n -> p (u n)"),
+                in_=rounded[:].rearrange("p u n j -> p (u n j)"),
+            )
+
+        def gather(dst, src, s0, sw):
+            nc.vector.tensor_copy(dst[:, s0 : s0 + sw], src[:].indirect(offs_sb[:, s0 // 16 : (s0 + sw) // 16]))
+
+        chunks = [(u0, min(WEIGHT_UNITS, units - u0)) for u0 in range(0, units, WEIGHT_UNITS)]
+        starts = [sum(GROUPS[:g]) for g in range(len(GROUPS))]
+
+        load_x(0, X0_CHUNKS[:1])
+        nc.sync.dma_start(offs_sb[:], offs)
+        load_x(0, X0_CHUNKS[1:])
+        load_x(1, TOKEN_CHUNKS)
+        for chunk in chunks[:2]:
+            load_w(*chunk)
+        load_x(2, TOKEN_CHUNKS)
+        for chunk in chunks[2:9]:
+            load_w(*chunk)
+        bias_low = raws.tile([P, 8], F32, tag="raw", name="bias_low")
+        nc.sync.dma_start(bias_low[:], b[:, 0:8])
+        for chunk in chunks[9:]:
+            load_w(*chunk)
+        bias_high = raws.tile([P, E - 8], F32, tag="raw", name="bias_high")
+        nc.sync.dma_start(bias_high[:], b[:, 8:E])
+        for tile, pos in zip(pos_sb, (pos1, pos2, pos3)):
+            nc.sync.dma_start(tile[:], pos)
+        nc.sync.dma_start(gates[:], gate.rearrange("r p t -> p r t"))
+
+        for chunk in range(3):
+            quantize_x(0, chunk)
+        made = [0]
+
+        def next_w():
+            if made[0] < len(chunks):
+                quantize_w(*chunks[made[0]])
+                made[0] += 1
+
+        for a in range(passes - 1):
+            for g in range(S // EARLY):
+                gather(s_codes[a], x_codes[a], g * EARLY, EARLY)
+                if a == 0 and g < 3:
+                    quantize_x(1, g)
+                elif a == 1 and g < 2:
+                    next_w()
+        for chunk in range(3):
+            quantize_x(2, chunk)
+
+        accs = {}
+        bank = None
+        for g, (s0, sw) in enumerate(zip(starts, GROUPS)):
+            if g < S // EARLY:
+                gather(s_scales, x_scales, g * EARLY, EARLY)
+            while made[0] <= (LATE_AFTER[g - 1] if g else 2):
+                next_w()
+            tag = f"late{LATE_AFTER[g - 1]}" if g else "early"
+            late = held.tile([P, sw], U32, tag=tag, name="late_codes", align_bytes=64)
+            nc.vector.tensor_copy(late[:], x_codes[passes - 1][:].indirect(offs_sb[:, s0 // 16 : (s0 + sw) // 16]))
+            next_w()
+            while len(w_codes) < passes * (s0 + sw) // C:
+                next_w()
+            for e in range(s0 // C, (s0 + sw) // C):
+                cols = slice(e * C, (e + 1) * C)
+                if e % 2 == 0:
+                    bank = psum.tile([P, 2, C], F32, name="bank")
+                acc = bank[:, e % 2, :]
+                words = [codes[:, cols] for codes in s_codes] + [late[:, e * C - s0 : (e + 1) * C - s0]]
+                for a in range(passes):
+                    nc.tensor.matmul_mx(
+                        out=acc,
+                        lhsT=w_codes[passes * e + a].bitcast(FP8X4),
+                        lhsT_scale=w_scales[passes * e + a],
+                        rhs=words[a].bitcast(FP8X4),
+                        rhs_scale=s_scales[4 * a : P, cols],
+                        start=(a == 0),
+                        stop=(a == passes - 1),
+                    )
+                accs[e] = acc
+        for e in range(E):
+            column = bias_low[:, e : e + 1] if e < 8 else bias_high[:, e - 8 : e - 7]
+            nc.scalar.activation(y[:, e * C : (e + 1) * C], accs[e], IDENTITY, bias=column)
+
+        terms = []
+        sums = []
+        for t0, tw in OUT_CHUNKS:
+            terms.append(raws.tile([P, 3, tw], F32, tag="raw", name="terms"))
+            sums.append(raws.tile([P, 2, tw], F32, tag="raw", name="sums"))
+
+        def weigh(i, r):
+            t0, tw = OUT_CHUNKS[i]
+            nc.vector.tensor_tensor(
+                terms[i][:, r, :], y[:].indirect(pos_sb[r][:, t0 // 16 : (t0 + tw) // 16]), gates[:, r, t0 : t0 + tw], MULT
+            )
+
+        def add(i, step):
+            t0, tw = OUT_CHUNKS[i]
+            first = terms[i][:, 0, :] if step == 0 else sums[i][:, 0, :]
+            nc.vector.tensor_tensor(sums[i][:, step, :], first, terms[i][:, step + 1, :], ADD)
+            if step == 1:
+                nc.sync.dma_start(out[:, t0 : t0 + tw], sums[i][:, 1, :])
+
+        for r in range(3):
+            weigh(0, r)
+        weigh(1, 0)
+        add(0, 0)
+        weigh(1, 1)
+        add(0, 1)
+        weigh(1, 2)
+        weigh(2, 0)
+        add(1, 0)
+        weigh(2, 1)
+        weigh(2, 2)
+        add(2, 0)
+        add(1, 1)
+        add(2, 1)

@@ -1,6 +1,7 @@
 from contextlib import ExitStack
 
 import concourse.mybir as mybir
+from concourse.masks import make_identity
 
 F32 = mybir.dt.float32
 BF16 = mybir.dt.bfloat16
@@ -20,10 +21,16 @@ FLOPS = 2 * 1536 * 128 * 3840
 TOKEN_CHUNKS = ((0, 512, 0), (512, 512, 0), (1024, 256, 0))
 WEIGHT_UNITS = 4
 X0_CHUNKS = ((0, 512, 512), (512, 512, 256), (1024, 256, 160))
-EARLY = 960
-GPSIMD_CHUNKS = (3, 6)
-LATE_AFTER = (4, 5, 7, 8, 10)
-GROUPS = (768, 768, 768, 768, 512, 256)
+PAIRED = 12
+EARLY = 1280
+EARLY_WINDOW = 1792
+LATE_WINDOW = 1408
+GPSIMD_CHUNKS = (3, 6, 9)
+BIAS_PARTS = ((0, 4, 6), (4, 8, 9), (8, 15, 12))
+SCALE_GROUPS = ((0, 1024, None), (1024, 1024, 3), (2048, 1024, 6), (3072, 768, 8))
+WORD_GROUPS = ((0, 1024, None), (1024, 1024, 4), (2048, 1024, 7), (3072, 512, 10), (3584, 256, 11))
+TURNED_CHUNK = 512
+TURNED = 1024
 OUT_CHUNKS = ((0, 512), (512, 512), (1024, 256))
 
 
@@ -40,22 +47,25 @@ def tile_moe_tk_lin_bias_kernel(tc, xT, w, b, gate, offs, pos1, pos2, pos3, out)
 
     with ExitStack() as ctx:
         held = ctx.enter_context(tc.tile_pool(name="held", bufs=1))
-        raws = ctx.enter_context(tc.tile_pool(name="raws", bufs=8))
-        rounds = ctx.enter_context(tc.tile_pool(name="rounds", bufs=7))
-        psum = ctx.enter_context(tc.psum_pool(name="psum", bufs=8))
+        raws = ctx.enter_context(tc.tile_pool(name="raws", bufs=10))
+        rounds = ctx.enter_context(tc.tile_pool(name="rounds", bufs=6))
+        psum = ctx.enter_context(tc.psum_pool(name="psum", bufs=1))
 
         offs_sb = held.tile([P, S // 16], U16, name="offs_sb")
         pos_sb = [held.tile([P, T // 16], U16, name=f"pos{r}_sb") for r in range(3)]
-        gates = held.tile([P, 3, T], F32, name="gates")
-        x_codes = [held.tile([P, T], U32, name=f"x_codes{a}", align_bytes=64) for a in range(passes)]
-        x_scales = held.tile([P, T], U8, name="x_scales", align_bytes=64)
+        ident = held.tile([P, P], F32, name="ident")
+        windows = [EARLY_WINDOW] * (passes - 1) + [LATE_WINDOW]
+        x_codes = [held.tile([P, windows[a]], U32, name=f"x_codes{a}", align_bytes=64) for a in range(passes)]
+        x_scales = held.tile([P, LATE_WINDOW], U8, name="x_scales", align_bytes=64)
         s_codes = [held.tile([P, S], U32, name=f"s_codes{a}", align_bytes=64) for a in range(passes - 1)]
-        s_scales = held.tile([P, S], U8, name="s_scales", align_bytes=64)
         w_codes = []
         w_scales = []
         y = held.tile([P, S], F32, name="y")
 
         nc.gpsimd.memset(x_scales[:], 0)
+        for codes in x_codes:
+            nc.gpsimd.memset(codes[:, T:], 0)
+        make_identity(nc, ident[:])
 
         raw_x = {}
 
@@ -83,6 +93,7 @@ def tile_moe_tk_lin_bias_kernel(tc, xT, w, b, gate, offs, pos1, pos2, pos3, out)
                 )
 
         raw_w = {}
+        lenders = [after for s0, sw, after in SCALE_GROUPS + WORD_GROUPS]
 
         def load_w(u0, n_units):
             raw = raws.tile([P, n_units, PACK * N], F32, name="raw")
@@ -92,7 +103,7 @@ def tile_moe_tk_lin_bias_kernel(tc, xT, w, b, gate, offs, pos1, pos2, pos3, out)
         def quantize_w(u0, n_units):
             raw = raw_w[u0]
             chunk = u0 // WEIGHT_UNITS
-            if chunk in LATE_AFTER:
+            if chunk in lenders:
                 rounded = held.tile([P, n_units, N, PACK], BF16, tag=f"late{chunk}", name="rounded_late", align_bytes=64)
             else:
                 rounded = rounds.tile([P, n_units, N, PACK], BF16, name="rounded", align_bytes=64)
@@ -118,7 +129,6 @@ def tile_moe_tk_lin_bias_kernel(tc, xT, w, b, gate, offs, pos1, pos2, pos3, out)
             nc.vector.tensor_copy(dst[:, s0 : s0 + sw], src[:].indirect(offs_sb[:, s0 // 16 : (s0 + sw) // 16]))
 
         chunks = [(u0, min(WEIGHT_UNITS, units - u0)) for u0 in range(0, units, WEIGHT_UNITS)]
-        starts = [sum(GROUPS[:g]) for g in range(len(GROUPS))]
 
         load_x(0, X0_CHUNKS[:1])
         nc.sync.dma_start(offs_sb[:], offs)
@@ -127,101 +137,128 @@ def tile_moe_tk_lin_bias_kernel(tc, xT, w, b, gate, offs, pos1, pos2, pos3, out)
         for chunk in chunks[:2]:
             load_w(*chunk)
         load_x(2, TOKEN_CHUNKS)
-        for chunk in chunks[2:9]:
-            load_w(*chunk)
-        bias_low = raws.tile([P, 8], F32, tag="raw", name="bias_low")
-        nc.sync.dma_start(bias_low[:], b[:, 0:8])
-        for chunk in chunks[9:]:
-            load_w(*chunk)
-        bias_high = raws.tile([P, E - 8], F32, tag="raw", name="bias_high")
-        nc.sync.dma_start(bias_high[:], b[:, 8:E])
+        loaded = 2
+        bias = []
+        for e0, e1, before in BIAS_PARTS:
+            for chunk in chunks[loaded:before]:
+                load_w(*chunk)
+            loaded = before
+            part = raws.tile([P, e1 - e0], F32, tag="raw", name="bias_part")
+            nc.sync.dma_start(part[:], b[:, e0:e1])
+            bias.extend(part[:, i : i + 1] for i in range(e1 - e0))
         for tile, pos in zip(pos_sb, (pos1, pos2, pos3)):
             nc.sync.dma_start(tile[:], pos)
-        nc.sync.dma_start(gates[:], gate.rearrange("r p t -> p r t"))
+        gates = {}
+        for t0, tw in OUT_CHUNKS:
+            gates[t0] = raws.tile([P, 3, tw], F32, tag="raw", name="gates")
+            nc.sync.dma_start(gates[t0][:], gate[:, :, t0 : t0 + tw].rearrange("r p t -> p r t"))
 
         for chunk in range(3):
             quantize_x(0, chunk)
-        made = [0]
-
-        def next_w():
-            if made[0] < len(chunks):
-                quantize_w(*chunks[made[0]])
-                made[0] += 1
-
-        for a in range(passes - 1):
-            for g in range(S // EARLY):
-                gather(s_codes[a], x_codes[a], g * EARLY, EARLY)
-                if a == 0 and g < 3:
-                    quantize_x(1, g)
-                elif a == 1 and g < 2:
-                    next_w()
+        for g in range(S // EARLY):
+            gather(s_codes[0], x_codes[0], g * EARLY, EARLY)
+        for chunk in range(3):
+            quantize_x(1, chunk)
+        for g in range(S // EARLY):
+            gather(s_codes[1], x_codes[1], g * EARLY, EARLY)
+        for chunk in chunks[:2]:
+            quantize_w(*chunk)
         for chunk in range(3):
             quantize_x(2, chunk)
 
-        accs = {}
-        bank = None
-        for g, (s0, sw) in enumerate(zip(starts, GROUPS)):
-            if g < S // EARLY:
-                gather(s_scales, x_scales, g * EARLY, EARLY)
-            while made[0] <= (LATE_AFTER[g - 1] if g else 2):
-                next_w()
-            tag = f"late{LATE_AFTER[g - 1]}" if g else "early"
-            late = held.tile([P, sw], U32, tag=tag, name="late_codes", align_bytes=64)
-            nc.vector.tensor_copy(late[:], x_codes[passes - 1][:].indirect(offs_sb[:, s0 // 16 : (s0 + sw) // 16]))
-            next_w()
-            while len(w_codes) < passes * (s0 + sw) // C:
-                next_w()
+        late = {}
+
+        def gather_late(sort, dtype, src, s0, sw, after):
+            tag = f"first_{sort}" if after is None else f"late{after}"
+            tile = held.tile([P, sw], dtype, tag=tag, name="late", align_bytes=64)
+            nc.vector.tensor_copy(tile[:], src[:].indirect(offs_sb[:, s0 // 16 : (s0 + sw) // 16]))
             for e in range(s0 // C, (s0 + sw) // C):
-                cols = slice(e * C, (e + 1) * C)
-                if e % 2 == 0:
-                    bank = psum.tile([P, 2, C], F32, name="bank")
-                acc = bank[:, e % 2, :]
-                words = [codes[:, cols] for codes in s_codes] + [late[:, e * C - s0 : (e + 1) * C - s0]]
-                for a in range(passes):
+                late[sort, e] = tile[:, e * C - s0 : (e + 1) * C - s0]
+
+        accs = {}
+        done = [0] * E
+
+        def multiply():
+            for e in range(E):
+                shares = e < PAIRED and e % 2 == 1
+                while done[e] < passes:
+                    a = done[e]
+                    ready = ("scales", e) in late and len(w_codes) > passes * e + a
+                    ready = ready and (a < passes - 1 or ("words", e) in late)
+                    if not ready or (shares and done[e - 1] < passes):
+                        break
+                    if a == 0 and e >= PAIRED:
+                        accs[e] = psum.tile([P, C], F32, tag=f"bank{(e - PAIRED // 2) % 8}", name="bank")[:]
+                    elif a == 0 and not shares:
+                        bank = psum.tile([P, 2, C], F32, tag=f"bank{e // 2}", name="bank")
+                        accs[e], accs[e + 1] = bank[:, 0, :], bank[:, 1, :]
+                    words = s_codes[a][:, e * C : (e + 1) * C] if a < passes - 1 else late["words", e]
                     nc.tensor.matmul_mx(
-                        out=acc,
+                        out=accs[e],
                         lhsT=w_codes[passes * e + a].bitcast(FP8X4),
                         lhsT_scale=w_scales[passes * e + a],
-                        rhs=words[a].bitcast(FP8X4),
-                        rhs_scale=s_scales[4 * a : P, cols],
+                        rhs=words.bitcast(FP8X4),
+                        rhs_scale=late["scales", e][4 * a : P, :],
                         start=(a == 0),
                         stop=(a == passes - 1),
                     )
-                accs[e] = acc
-        for e in range(E):
-            column = bias_low[:, e : e + 1] if e < 8 else bias_high[:, e - 8 : e - 7]
-            nc.scalar.activation(y[:, e * C : (e + 1) * C], accs[e], IDENTITY, bias=column)
+                    done[e] += 1
 
-        terms = []
-        sums = []
-        for t0, tw in OUT_CHUNKS:
-            terms.append(raws.tile([P, 3, tw], F32, tag="raw", name="terms"))
-            sums.append(raws.tile([P, 2, tw], F32, tag="raw", name="sums"))
+        def leave(e0, e1):
+            for e in range(e0, e1):
+                nc.scalar.activation(y[:, e * C : (e + 1) * C], accs[e], IDENTITY, bias=bias[e])
 
-        def weigh(i, r):
-            t0, tw = OUT_CHUNKS[i]
+        for after in [None] + list(range(2, len(chunks))):
+            if after is not None:
+                quantize_w(*chunks[after])
+            for group in SCALE_GROUPS:
+                if group[2] == after:
+                    gather_late("scales", U8, x_scales, *group)
+            multiply()
+            for group in WORD_GROUPS:
+                if group[2] == after:
+                    gather_late("words", U32, x_codes[passes - 1], *group)
+            multiply()
+            for e0, e1, before in BIAS_PARTS:
+                if before - 1 == after:
+                    leave(e0, e1)
+
+        per = TURNED_CHUNK // P
+        pair = 2
+
+        def weigh(terms, r, t0, tw):
             nc.vector.tensor_tensor(
-                terms[i][:, r, :], y[:].indirect(pos_sb[r][:, t0 // 16 : (t0 + tw) // 16]), gates[:, r, t0 : t0 + tw], MULT
+                terms[:, r, :], y[:].indirect(pos_sb[r][:, t0 // 16 : (t0 + tw) // 16]), gates[t0][:, r, :], MULT
             )
 
-        def add(i, step):
-            t0, tw = OUT_CHUNKS[i]
-            first = terms[i][:, 0, :] if step == 0 else sums[i][:, 0, :]
-            nc.vector.tensor_tensor(sums[i][:, step, :], first, terms[i][:, step + 1, :], ADD)
-            if step == 1:
-                nc.sync.dma_start(out[:, t0 : t0 + tw], sums[i][:, 1, :])
+        for i in range(TURNED // TURNED_CHUNK):
+            t0 = i * TURNED_CHUNK
+            terms = raws.tile([P, 3, TURNED_CHUNK], F32, tag="raw", name="terms")
+            turned = raws.tile([P, per, P], F32, tag="raw", name="turned")
+            result = raws.tile([P, per, P], F32, tag="raw", name="result")
+            summed = [psum.tile([P, P], F32, tag=f"bank{(per * i + c) % 8}", name="summed") for c in range(per)]
+            for r in range(3):
+                weigh(terms, r, t0, TURNED_CHUNK)
+                for c in range(per):
+                    nc.tensor.matmul(
+                        summed[c][:], terms[:, r, c * P : (c + 1) * P], ident[:], start=(r == 0), stop=(r == 2), is_transpose=True
+                    )
+            back = [psum.tile([P, P], F32, tag=f"bank{(per * (i + 1) + c) % 8}", name="back") for c in range(per)]
+            for c in range(per):
+                nc.scalar.copy(turned[:, c, :], summed[c][:])
+                nc.tensor.transpose(back[c][:], turned[:, c, :], ident[:])
+            for c0 in range(0, per, pair):
+                for c in range(c0, c0 + pair):
+                    nc.scalar.copy(result[:, c, :], back[c][:])
+                nc.sync.dma_start(
+                    out[:, t0 + c0 * P : t0 + (c0 + pair) * P], result[:, c0 : c0 + pair, :].rearrange("p c m -> p (c m)")
+                )
 
+        rest = T - TURNED
+        terms = raws.tile([P, 3, rest], F32, tag="raw", name="terms")
+        sums = raws.tile([P, 2, rest], F32, tag="raw", name="sums")
         for r in range(3):
-            weigh(0, r)
-        weigh(1, 0)
-        add(0, 0)
-        weigh(1, 1)
-        add(0, 1)
-        weigh(1, 2)
-        weigh(2, 0)
-        add(1, 0)
-        weigh(2, 1)
-        weigh(2, 2)
-        add(2, 0)
-        add(1, 1)
-        add(2, 1)
+            weigh(terms, r, TURNED, rest)
+        nc.vector.tensor_tensor(sums[:, 0, :], terms[:, 0, :], terms[:, 1, :], ADD)
+        nc.vector.tensor_tensor(sums[:, 1, :], sums[:, 0, :], terms[:, 2, :], ADD)
+        nc.sync.dma_start(out[:, TURNED:T], sums[:, 1, :])

@@ -18,14 +18,14 @@ PACK = 4
 PASS_K = P * PACK
 FLOPS = 2 * 1536 * 128 * 3840
 
-TOKEN_CHUNKS = ((0, 512, 0), (512, 512, 0), (1024, 256, 0))
+TOKEN_CHUNKS = ((0, 256, 0), (256, 512, 0), (768, 512, 0))
 WEIGHT_UNITS = 4
 X0_CHUNKS = ((0, 512, 512), (512, 512, 256), (1024, 256, 160))
 PAIRED = 12
 EARLY = 1280
 EARLY_WINDOW = 1792
 LATE_WINDOW = 1408
-GPSIMD_CHUNKS = (3, 6, 9)
+VECTOR_CHUNKS = (9,)
 BIAS_PARTS = ((0, 4, 6), (4, 8, 9), (8, 15, 12))
 SCALE_GROUPS = ((0, 1024, None), (1024, 1024, 3), (2048, 1024, 6), (3072, 768, 8))
 WORD_GROUPS = ((0, 1024, None), (1024, 1024, 4), (2048, 1024, 7), (3072, 512, 10), (3584, 256, 11))
@@ -114,9 +114,8 @@ def tile_moe_tk_lin_bias_kernel(tc, xT, w, b, gate, offs, pos1, pos2, pos3, out)
                 w_scales.append(scales[:, i, :])
             src = raw[:].rearrange("p u (j c i) -> p u c j i", j=PACK, i=4)
             dst = rounded[:].rearrange("p u (c i) j -> p u c j i", i=4)
-            if u0 // WEIGHT_UNITS in GPSIMD_CHUNKS:
-                for i in range(n_units):
-                    nc.gpsimd.tensor_scalar(dst[:, i], src[:, i], 1.0, 0.0, MULT, ADD)
+            if chunk in VECTOR_CHUNKS:
+                nc.vector.tensor_copy(dst, src)
             else:
                 nc.scalar.copy(dst, src)
             nc.vector.quantize_mx(

@@ -19,16 +19,15 @@ PASS_K = P * PACK
 FLOPS = 2 * 1536 * 128 * 3840
 
 TOKEN_CHUNKS = ((0, 256, 0), (256, 512, 0), (768, 512, 0))
-WEIGHT_UNITS = 4
+WEIGHT_CHUNKS = (4,) * 10 + (2, 2, 1)
 X0_CHUNKS = ((0, 512, 512), (512, 512, 256), (1024, 256, 160))
 PAIRED = 12
 EARLY = 1280
 EARLY_WINDOW = 1792
 LATE_WINDOW = 1408
-VECTOR_CHUNKS = (9,)
-BIAS_PARTS = ((0, 4, 6), (4, 8, 9), (8, 15, 12))
-SCALE_GROUPS = ((0, 1024, None), (1024, 1024, 3), (2048, 1024, 6), (3072, 768, 8))
-WORD_GROUPS = ((0, 1024, None), (1024, 1024, 4), (2048, 1024, 7), (3072, 512, 10), (3584, 256, 11))
+BIAS_PARTS = ((0, 4, 6), (4, 8, 9), (8, 15, 13))
+SCALE_GROUPS = ((0, 1024, None), (1024, 1024, 2), (2048, 1024, 4), (3072, 768, 7))
+WORD_GROUPS = ((0, 1024, None), (1024, 1024, 3), (2048, 1024, 6), (3072, 512, 9), (3584, 256, 11))
 TURNED_CHUNK = 512
 TURNED = 1024
 OUT_CHUNKS = ((0, 512), (512, 512), (1024, 256))
@@ -41,7 +40,6 @@ def tile_moe_tk_lin_bias_kernel(tc, xT, w, b, gate, offs, pos1, pos2, pos3, out)
     S = offs.shape[1] * 16
     C = S // E
     passes = K // PASS_K
-    units = E * passes
     x_view = xT.rearrange("(a p j) t -> a p j t", p=P, j=PACK)
     w_view = w.rearrange("e (a p j) n -> p (e a) (j n)", p=P, j=PACK)
 
@@ -102,7 +100,7 @@ def tile_moe_tk_lin_bias_kernel(tc, xT, w, b, gate, offs, pos1, pos2, pos3, out)
 
         def quantize_w(u0, n_units):
             raw = raw_w[u0]
-            chunk = u0 // WEIGHT_UNITS
+            chunk = chunks.index((u0, n_units))
             if chunk in lenders:
                 rounded = held.tile([P, n_units, N, PACK], BF16, tag=f"late{chunk}", name="rounded_late", align_bytes=64)
             else:
@@ -114,10 +112,7 @@ def tile_moe_tk_lin_bias_kernel(tc, xT, w, b, gate, offs, pos1, pos2, pos3, out)
                 w_scales.append(scales[:, i, :])
             src = raw[:].rearrange("p u (j c i) -> p u c j i", j=PACK, i=4)
             dst = rounded[:].rearrange("p u (c i) j -> p u c j i", i=4)
-            if chunk in VECTOR_CHUNKS:
-                nc.vector.tensor_copy(dst, src)
-            else:
-                nc.scalar.copy(dst, src)
+            nc.scalar.copy(dst, src)
             nc.vector.quantize_mx(
                 out=codes[:].rearrange("p u n -> p (u n)").bitcast(FP8X4),
                 scales=scales[:].rearrange("p u n -> p (u n)"),
@@ -127,7 +122,7 @@ def tile_moe_tk_lin_bias_kernel(tc, xT, w, b, gate, offs, pos1, pos2, pos3, out)
         def gather(dst, src, s0, sw):
             nc.vector.tensor_copy(dst[:, s0 : s0 + sw], src[:].indirect(offs_sb[:, s0 // 16 : (s0 + sw) // 16]))
 
-        chunks = [(u0, min(WEIGHT_UNITS, units - u0)) for u0 in range(0, units, WEIGHT_UNITS)]
+        chunks = [(sum(WEIGHT_CHUNKS[:i]), n) for i, n in enumerate(WEIGHT_CHUNKS)]
 
         load_x(0, X0_CHUNKS[:1])
         nc.sync.dma_start(offs_sb[:], offs)
@@ -242,7 +237,7 @@ def tile_moe_tk_lin_bias_kernel(tc, xT, w, b, gate, offs, pos1, pos2, pos3, out)
                     nc.tensor.matmul(
                         summed[c][:], terms[:, r, c * P : (c + 1) * P], ident[:], start=(r == 0), stop=(r == 2), is_transpose=True
                     )
-            back = [psum.tile([P, P], F32, tag=f"bank{(per * (i + 1) + c) % 8}", name="back") for c in range(per)]
+            back = [psum.tile([P, P], F32, tag=f"bank{(per * i + c) % 8}", name="back") for c in range(per)]
             for c in range(per):
                 nc.scalar.copy(turned[:, c, :], summed[c][:])
                 nc.tensor.transpose(back[c][:], turned[:, c, :], ident[:])

@@ -20,7 +20,7 @@ FLOPS = 2 * 1536 * 128 * 3840
 
 TOKEN_CHUNKS = ((0, 256, 0), (256, 512, 0), (768, 512, 0))
 WEIGHT_CHUNKS = (4,) * 10 + (2, 2, 1)
-X0_CHUNKS = ((0, 512, 512), (512, 512, 256), (1024, 256, 160))
+X0_CHUNKS = ((0, 512, 512), (512, 512, 344), (1024, 256, 128))
 PAIRED = 12
 EARLY = 1280
 EARLY_WINDOW = 1792
@@ -51,7 +51,6 @@ def tile_moe_tk_lin_bias_kernel(tc, xT, w, b, gate, offs, pos1, pos2, pos3, out)
 
         offs_sb = held.tile([P, S // 16], U16, name="offs_sb")
         pos_sb = [held.tile([P, T // 16], U16, name=f"pos{r}_sb") for r in range(3)]
-        ident = held.tile([P, P], F32, name="ident")
         windows = [EARLY_WINDOW] * (passes - 1) + [LATE_WINDOW]
         x_codes = [held.tile([P, windows[a]], U32, name=f"x_codes{a}", align_bytes=64) for a in range(passes)]
         x_scales = held.tile([P, LATE_WINDOW], U8, name="x_scales", align_bytes=64)
@@ -60,10 +59,9 @@ def tile_moe_tk_lin_bias_kernel(tc, xT, w, b, gate, offs, pos1, pos2, pos3, out)
         w_scales = []
         y = held.tile([P, S], F32, name="y")
 
-        nc.gpsimd.memset(x_scales[:], 0)
+        nc.vector.memset(x_scales[:].bitcast(U32), 0)
         for codes in x_codes:
-            nc.gpsimd.memset(codes[:, T:], 0)
-        make_identity(nc, ident[:])
+            nc.vector.memset(codes[:, T:], 0)
 
         raw_x = {}
 
@@ -76,7 +74,10 @@ def tile_moe_tk_lin_bias_kernel(tc, xT, w, b, gate, offs, pos1, pos2, pos3, out)
         def quantize_x(a, chunk):
             for t0, tw, vec in ((X0_CHUNKS if a == 0 else TOKEN_CHUNKS)[chunk],):
                 raw = raw_x[a, t0]
-                rounded = rounds.tile([P, tw, PACK], BF16, name="rounded", align_bytes=64)
+                if (a, chunk) == (0, 2):
+                    rounded = held.tile([P, tw, PACK], BF16, tag="ident", name="rounded_last", align_bytes=64)
+                else:
+                    rounded = rounds.tile([P, tw, PACK], BF16, name="rounded", align_bytes=64)
                 src = raw[:].rearrange("p j (c i) -> p c j i", i=4)
                 dst = rounded[:].rearrange("p (c i) j -> p c j i", i=4)
                 cut = vec // 4
@@ -149,6 +150,8 @@ def tile_moe_tk_lin_bias_kernel(tc, xT, w, b, gate, offs, pos1, pos2, pos3, out)
 
         for chunk in range(3):
             quantize_x(0, chunk)
+        ident = held.tile([P, P], F32, tag="ident", name="ident", align_bytes=64)
+        make_identity(nc, ident[:])
         for g in range(S // EARLY):
             gather(s_codes[0], x_codes[0], g * EARLY, EARLY)
         for chunk in range(3):

@@ -15,247 +15,251 @@ ADD = mybir.AluOpType.add
 
 P = 128
 PACK = 4
-PASS_K = P * PACK
+TOP = 3
+STRIPE = 16
+RUN = 4
 FLOPS = 2 * 1536 * 128 * 3840
 
-TOKEN_CHUNKS = ((0, 256, 0), (256, 512, 0), (768, 512, 0))
-WEIGHT_CHUNKS = (4,) * 10 + (2, 2, 1)
-X0_CHUNKS = ((0, 512, 512), (512, 512, 344), (1024, 256, 128))
+FIRST_PIECES = ((0, 512, 512), (512, 512, 344), (1024, 256, 128))
+LATER_PIECES = ((0, 256, 0), (256, 512, 0), (768, 512, 0))
+WEIGHT_PIECES = (4,) * 10 + (2, 2, 1)
+EARLY_GATHER, EARLY_WINDOW, LATE_WINDOW = 1280, 1792, 1408
+SCALE_GATHERS = ((0, 1024, 1), (1024, 1024, 3), (2048, 1024, 5), (3072, 768, 7))
+WORD_GATHERS = ((0, 1024, 2), (1024, 1024, 4), (2048, 1024, 6), (3072, 512, 9), (3584, 256, 11))
+BIAS_PARTS = ((0, 4, 7), (4, 8, 10), (8, 15, 13))
 PAIRED = 12
-EARLY = 1280
-EARLY_WINDOW = 1792
-LATE_WINDOW = 1408
-BIAS_PARTS = ((0, 4, 6), (4, 8, 9), (8, 15, 13))
-SCALE_GROUPS = ((0, 1024, None), (1024, 1024, 2), (2048, 1024, 4), (3072, 768, 7))
-WORD_GROUPS = ((0, 1024, None), (1024, 1024, 3), (2048, 1024, 6), (3072, 512, 9), (3584, 256, 11))
-TURNED_CHUNK = 512
-TURNED = 1024
-OUT_CHUNKS = ((0, 512), (512, 512), (1024, 256))
+BUFFERS = 13
+OUT_PIECES = ((0, 512), (512, 384), (896, 384))
+BANKS_A_PIECE = 4
+STORE_BLOCKS = 2
 
 
 def tile_moe_tk_lin_bias_kernel(tc, xT, w, b, gate, offs, pos1, pos2, pos3, out):
     nc = tc.nc
     K, T = xT.shape
     E, N = w.shape[0], w.shape[2]
-    S = offs.shape[1] * 16
+    S = offs.shape[1] * STRIPE
     C = S // E
-    passes = K // PASS_K
+    passes = K // (P * PACK)
     x_view = xT.rearrange("(a p j) t -> a p j t", p=P, j=PACK)
     w_view = w.rearrange("e (a p j) n -> p (e a) (j n)", p=P, j=PACK)
+    weight_pieces = [(sum(WEIGHT_PIECES[:i]), count) for i, count in enumerate(WEIGHT_PIECES)]
+    lenders = sorted(piece for s0, slots, piece in SCALE_GATHERS + WORD_GATHERS)
 
     with ExitStack() as ctx:
         held = ctx.enter_context(tc.tile_pool(name="held", bufs=1))
-        raws = ctx.enter_context(tc.tile_pool(name="raws", bufs=10))
-        rounds = ctx.enter_context(tc.tile_pool(name="rounds", bufs=6))
+        loads = ctx.enter_context(tc.tile_pool(name="loads", bufs=1))
+        rounds = ctx.enter_context(tc.tile_pool(name="rounds", bufs=8))
         psum = ctx.enter_context(tc.psum_pool(name="psum", bufs=1))
 
-        offs_sb = held.tile([P, S // 16], U16, name="offs_sb")
-        pos_sb = [held.tile([P, T // 16], U16, name=f"pos{r}_sb") for r in range(3)]
+        offs_sb = held.tile([P, S // STRIPE], U16, name="offs_sb")
+        pos_sb = [held.tile([P, T // STRIPE], U16, name=f"pos{r}_sb") for r in range(TOP)]
         windows = [EARLY_WINDOW] * (passes - 1) + [LATE_WINDOW]
-        x_codes = [held.tile([P, windows[a]], U32, name=f"x_codes{a}", align_bytes=64) for a in range(passes)]
-        x_scales = held.tile([P, LATE_WINDOW], U8, name="x_scales", align_bytes=64)
-        s_codes = [held.tile([P, S], U32, name=f"s_codes{a}", align_bytes=64) for a in range(passes - 1)]
-        w_codes = []
-        w_scales = []
+        token_words = [held.tile([P, windows[a]], U32, name=f"token_words{a}", align_bytes=64) for a in range(passes)]
+        token_scales = held.tile([P, LATE_WINDOW], U8, name="token_scales", align_bytes=64)
+        slot_words = [held.tile([P, S], U32, name="slot_words0", align_bytes=64)]
         y = held.tile([P, S], F32, name="y")
 
-        nc.vector.memset(x_scales[:].bitcast(U32), 0)
-        for codes in x_codes:
-            nc.vector.memset(codes[:, T:], 0)
+        nc.vector.memset(token_scales[:].bitcast(U32), 0)
+        for words in token_words:
+            nc.vector.memset(words[:, T:], 0)
+
+        free = [f"buffer{i}" for i in range(BUFFERS)]
+
+        def take(keep=False):
+            tag = free.pop(0)
+            if not keep:
+                free.append(tag)
+            return tag
 
         raw_x = {}
+        raw_w = {}
+        buffer_of = {}
 
-        def load_x(a, token_chunks):
-            for t0, tw, vec in token_chunks:
-                raw = raws.tile([P, PACK, tw], F32, name="raw")
-                nc.sync.dma_start(raw[:], x_view[a][:, :, t0 : t0 + tw])
-                raw_x[a, t0] = raw
+        def load_x(a, pieces):
+            for t0, tokens, on_vector in pieces:
+                raw_x[a, t0] = loads.tile([P, PACK, tokens], F32, tag=take(), name="raw_x", align_bytes=64)
+                nc.sync.dma_start(raw_x[a, t0][:], x_view[a][:, :, t0 : t0 + tokens])
 
-        def quantize_x(a, chunk):
-            for t0, tw, vec in ((X0_CHUNKS if a == 0 else TOKEN_CHUNKS)[chunk],):
-                raw = raw_x[a, t0]
-                if (a, chunk) == (0, 2):
-                    rounded = held.tile([P, tw, PACK], BF16, tag="ident", name="rounded_last", align_bytes=64)
+        def load_w(piece):
+            m0, count = weight_pieces[piece]
+            buffer_of[piece] = take(keep=piece in lenders) if piece else "first_weights"
+            raw_w[piece] = loads.tile([P, count, PACK * N], F32, tag=buffer_of[piece], name="raw_w", align_bytes=64)
+            nc.sync.dma_start(raw_w[piece][:], w_view[:, m0 : m0 + count, :])
+
+        load_x(0, FIRST_PIECES[:1])
+        nc.sync.dma_start(offs_sb[:], offs)
+        load_x(0, FIRST_PIECES[1:])
+        load_x(1, LATER_PIECES)
+        load_w(0)
+        load_x(2, LATER_PIECES)
+        loaded = 1
+        bias = []
+        for e0, e1, before in BIAS_PARTS:
+            for piece in range(loaded, before):
+                load_w(piece)
+            loaded = before
+            part = held.tile([P, e1 - e0], F32, name=f"bias{e0}")
+            nc.sync.dma_start(part[:], b[:, e0:e1])
+            bias.extend(part[:, i : i + 1] for i in range(e1 - e0))
+        for pos_tile, pos in zip(pos_sb, (pos1, pos2, pos3)):
+            nc.sync.dma_start(pos_tile[:], pos)
+        gates = {}
+        for t0, tokens in OUT_PIECES:
+            gates[t0] = loads.tile([P, TOP, tokens], F32, tag=take(keep=True), name="gates", align_bytes=64)
+            nc.sync.dma_start(gates[t0][:], gate[:, :, t0 : t0 + tokens].rearrange("r p t -> p r t"))
+
+        def quantize_x(a, pieces):
+            for t0, tokens, on_vector in pieces:
+                if (a, t0) == (0, FIRST_PIECES[-1][0]):
+                    rounded = held.tile([P, tokens, PACK], BF16, tag="identity", name="rounded_last", align_bytes=64)
                 else:
-                    rounded = rounds.tile([P, tw, PACK], BF16, name="rounded", align_bytes=64)
-                src = raw[:].rearrange("p j (c i) -> p c j i", i=4)
-                dst = rounded[:].rearrange("p (c i) j -> p c j i", i=4)
-                cut = vec // 4
-                if vec:
+                    rounded = rounds.tile([P, tokens, PACK], BF16, name="rounded", align_bytes=64)
+                src = raw_x[a, t0][:].rearrange("p j (c i) -> p c j i", i=RUN)
+                dst = rounded[:].rearrange("p (c i) j -> p c j i", i=RUN)
+                cut = on_vector // RUN
+                if on_vector:
                     nc.vector.tensor_copy(dst[:, :cut], src[:, :cut])
-                if vec < tw:
+                if on_vector < tokens:
                     nc.scalar.copy(dst[:, cut:], src[:, cut:])
                 nc.vector.quantize_mx(
-                    out=x_codes[a][:, t0 : t0 + tw].bitcast(FP8X4),
-                    scales=x_scales[4 * a : P, t0 : t0 + tw],
+                    out=token_words[a][:, t0 : t0 + tokens].bitcast(FP8X4),
+                    scales=token_scales[4 * a : P, t0 : t0 + tokens],
                     in_=rounded[:].rearrange("p t j -> p (t j)"),
                 )
 
-        raw_w = {}
-        lenders = [after for s0, sw, after in SCALE_GROUPS + WORD_GROUPS]
+        w_words = []
+        w_scales = []
 
-        def load_w(u0, n_units):
-            raw = raws.tile([P, n_units, PACK * N], F32, name="raw")
-            nc.sync.dma_start(raw[:], w_view[:, u0 : u0 + n_units, :])
-            raw_w[u0] = raw
-
-        def quantize_w(u0, n_units):
-            raw = raw_w[u0]
-            chunk = chunks.index((u0, n_units))
-            if chunk in lenders:
-                rounded = held.tile([P, n_units, N, PACK], BF16, tag=f"late{chunk}", name="rounded_late", align_bytes=64)
-            else:
-                rounded = rounds.tile([P, n_units, N, PACK], BF16, name="rounded", align_bytes=64)
-            codes = held.tile([P, n_units, N], U32, name=f"w_codes{u0}", align_bytes=64)
-            scales = held.tile([P, n_units, N], U8, name=f"w_scales{u0}", align_bytes=64)
-            for i in range(n_units):
-                w_codes.append(codes[:, i, :])
-                w_scales.append(scales[:, i, :])
-            src = raw[:].rearrange("p u (j c i) -> p u c j i", j=PACK, i=4)
-            dst = rounded[:].rearrange("p u (c i) j -> p u c j i", i=4)
-            nc.scalar.copy(dst, src)
+        def quantize_w(piece):
+            m0, count = weight_pieces[piece]
+            rounded = rounds.tile([P, count, N, PACK], BF16, name="rounded", align_bytes=64)
+            words = held.tile([P, count, N], U32, name=f"w_words{m0}", align_bytes=64)
+            scales = held.tile([P, count, N], U8, name=f"w_scales{m0}", align_bytes=64)
+            w_words.extend(words[:, i, :] for i in range(count))
+            w_scales.extend(scales[:, i, :] for i in range(count))
+            nc.scalar.copy(
+                rounded[:].rearrange("p m (c i) j -> p m c j i", i=RUN),
+                raw_w[piece][:].rearrange("p m (j c i) -> p m c j i", j=PACK, i=RUN),
+            )
             nc.vector.quantize_mx(
-                out=codes[:].rearrange("p u n -> p (u n)").bitcast(FP8X4),
-                scales=scales[:].rearrange("p u n -> p (u n)"),
-                in_=rounded[:].rearrange("p u n j -> p (u n j)"),
+                out=words[:].rearrange("p m n -> p (m n)").bitcast(FP8X4),
+                scales=scales[:].rearrange("p m n -> p (m n)"),
+                in_=rounded[:].rearrange("p m n j -> p (m n j)"),
             )
 
-        def gather(dst, src, s0, sw):
-            nc.vector.tensor_copy(dst[:, s0 : s0 + sw], src[:].indirect(offs_sb[:, s0 // 16 : (s0 + sw) // 16]))
+        def gather(dst, window, s0, slots):
+            nc.vector.tensor_copy(dst, window[:].indirect(offs_sb[:, s0 // STRIPE : (s0 + slots) // STRIPE]))
 
-        chunks = [(sum(WEIGHT_CHUNKS[:i]), n) for i, n in enumerate(WEIGHT_CHUNKS)]
+        def gather_early(a):
+            for s0 in range(0, S, EARLY_GATHER):
+                gather(slot_words[a][:, s0 : s0 + EARLY_GATHER], token_words[a], s0, EARLY_GATHER)
 
-        load_x(0, X0_CHUNKS[:1])
-        nc.sync.dma_start(offs_sb[:], offs)
-        load_x(0, X0_CHUNKS[1:])
-        load_x(1, TOKEN_CHUNKS)
-        for chunk in chunks[:2]:
-            load_w(*chunk)
-        load_x(2, TOKEN_CHUNKS)
-        loaded = 2
-        bias = []
-        for e0, e1, before in BIAS_PARTS:
-            for chunk in chunks[loaded:before]:
-                load_w(*chunk)
-            loaded = before
-            part = raws.tile([P, e1 - e0], F32, tag="raw", name="bias_part")
-            nc.sync.dma_start(part[:], b[:, e0:e1])
-            bias.extend(part[:, i : i + 1] for i in range(e1 - e0))
-        for tile, pos in zip(pos_sb, (pos1, pos2, pos3)):
-            nc.sync.dma_start(tile[:], pos)
-        gates = {}
-        for t0, tw in OUT_CHUNKS:
-            gates[t0] = raws.tile([P, 3, tw], F32, tag="raw", name="gates")
-            nc.sync.dma_start(gates[t0][:], gate[:, :, t0 : t0 + tw].rearrange("r p t -> p r t"))
-
-        for chunk in range(3):
-            quantize_x(0, chunk)
-        ident = held.tile([P, P], F32, tag="ident", name="ident", align_bytes=64)
+        quantize_x(0, FIRST_PIECES)
+        ident = held.tile([P, P], F32, tag="identity", name="ident", align_bytes=64)
         make_identity(nc, ident[:])
-        for g in range(S // EARLY):
-            gather(s_codes[0], x_codes[0], g * EARLY, EARLY)
-        for chunk in range(3):
-            quantize_x(1, chunk)
-        for g in range(S // EARLY):
-            gather(s_codes[1], x_codes[1], g * EARLY, EARLY)
-        for chunk in chunks[:2]:
-            quantize_w(*chunk)
-        for chunk in range(3):
-            quantize_x(2, chunk)
+        gather_early(0)
+        quantize_x(1, LATER_PIECES)
+        quantize_w(0)
+        slot_words.append(loads.tile([P, S], U32, tag=buffer_of[0], name="slot_words1", align_bytes=64))
+        gather_early(1)
+        quantize_x(2, LATER_PIECES)
 
-        late = {}
+        slot_scales = {}
+        last_words = {}
 
-        def gather_late(sort, dtype, src, s0, sw, after):
-            tag = f"first_{sort}" if after is None else f"late{after}"
-            tile = held.tile([P, sw], dtype, tag=tag, name="late", align_bytes=64)
-            nc.vector.tensor_copy(tile[:], src[:].indirect(offs_sb[:, s0 // 16 : (s0 + sw) // 16]))
-            for e in range(s0 // C, (s0 + sw) // C):
-                late[sort, e] = tile[:, e * C - s0 : (e + 1) * C - s0]
+        def gather_late(by_expert, dtype, window, s0, slots, piece):
+            gathered = loads.tile([P, slots], dtype, tag=buffer_of[piece], name="gathered", align_bytes=64)
+            gather(gathered[:], window, s0, slots)
+            for e in range(s0 // C, (s0 + slots) // C):
+                by_expert[e] = gathered[:, e * C - s0 : (e + 1) * C - s0]
 
-        accs = {}
-        done = [0] * E
+        products = {}
+        passes_done = [0] * E
 
         def multiply():
             for e in range(E):
-                shares = e < PAIRED and e % 2 == 1
-                while done[e] < passes:
-                    a = done[e]
-                    ready = ("scales", e) in late and len(w_codes) > passes * e + a
-                    ready = ready and (a < passes - 1 or ("words", e) in late)
-                    if not ready or (shares and done[e - 1] < passes):
+                second_in_bank = e < PAIRED and e % 2 == 1
+                while passes_done[e] < passes:
+                    a = passes_done[e]
+                    ready = e in slot_scales and len(w_words) > passes * e + a and (a < passes - 1 or e in last_words)
+                    if not ready or (second_in_bank and passes_done[e - 1] < passes):
                         break
                     if a == 0 and e >= PAIRED:
-                        accs[e] = psum.tile([P, C], F32, tag=f"bank{(e - PAIRED // 2) % 8}", name="bank")[:]
-                    elif a == 0 and not shares:
+                        products[e] = psum.tile([P, C], F32, tag=f"bank{(e - PAIRED // 2) % 8}", name="bank")[:]
+                    elif a == 0 and not second_in_bank:
                         bank = psum.tile([P, 2, C], F32, tag=f"bank{e // 2}", name="bank")
-                        accs[e], accs[e + 1] = bank[:, 0, :], bank[:, 1, :]
-                    words = s_codes[a][:, e * C : (e + 1) * C] if a < passes - 1 else late["words", e]
+                        products[e], products[e + 1] = bank[:, 0, :], bank[:, 1, :]
+                    moving = slot_words[a][:, e * C : (e + 1) * C] if a < passes - 1 else last_words[e]
                     nc.tensor.matmul_mx(
-                        out=accs[e],
-                        lhsT=w_codes[passes * e + a].bitcast(FP8X4),
+                        out=products[e],
+                        lhsT=w_words[passes * e + a].bitcast(FP8X4),
                         lhsT_scale=w_scales[passes * e + a],
-                        rhs=words.bitcast(FP8X4),
-                        rhs_scale=late["scales", e][4 * a : P, :],
+                        rhs=moving.bitcast(FP8X4),
+                        rhs_scale=slot_scales[e][4 * a : P, :],
                         start=(a == 0),
                         stop=(a == passes - 1),
                     )
-                    done[e] += 1
+                    passes_done[e] += 1
 
-        def leave(e0, e1):
-            for e in range(e0, e1):
-                nc.scalar.activation(y[:, e * C : (e + 1) * C], accs[e], IDENTITY, bias=bias[e])
-
-        for after in [None] + list(range(2, len(chunks))):
-            if after is not None:
-                quantize_w(*chunks[after])
-            for group in SCALE_GROUPS:
-                if group[2] == after:
-                    gather_late("scales", U8, x_scales, *group)
+        for piece in range(1, len(weight_pieces)):
+            quantize_w(piece)
+            for s0, slots, lender in SCALE_GATHERS:
+                if lender == piece:
+                    gather_late(slot_scales, U8, token_scales, s0, slots, piece)
             multiply()
-            for group in WORD_GROUPS:
-                if group[2] == after:
-                    gather_late("words", U32, x_codes[passes - 1], *group)
+            for s0, slots, lender in WORD_GATHERS:
+                if lender == piece:
+                    gather_late(last_words, U32, token_words[passes - 1], s0, slots, piece)
             multiply()
             for e0, e1, before in BIAS_PARTS:
-                if before - 1 == after:
-                    leave(e0, e1)
+                if before - 1 == piece:
+                    for e in range(e0, e1):
+                        nc.scalar.activation(y[:, e * C : (e + 1) * C], products[e], IDENTITY, bias=bias[e])
 
-        per = TURNED_CHUNK // P
-        pair = 2
+        free.extend(buffer_of[piece] for piece in lenders)
 
-        def weigh(terms, r, t0, tw):
-            nc.vector.tensor_tensor(
-                terms[:, r, :], y[:].indirect(pos_sb[r][:, t0 // 16 : (t0 + tw) // 16]), gates[t0][:, r, :], MULT
-            )
+        def weigh(terms, r, t0, c0, c1):
+            entries = pos_sb[r][:, (t0 + c0) // STRIPE : (t0 + c1) // STRIPE]
+            nc.vector.tensor_tensor(terms[:, r, c0:c1], y[:].indirect(entries), gates[t0][:, r, c0:c1], MULT)
 
-        for i in range(TURNED // TURNED_CHUNK):
-            t0 = i * TURNED_CHUNK
-            terms = raws.tile([P, 3, TURNED_CHUNK], F32, tag="raw", name="terms")
-            turned = raws.tile([P, per, P], F32, tag="raw", name="turned")
-            result = raws.tile([P, per, P], F32, tag="raw", name="result")
-            summed = [psum.tile([P, P], F32, tag=f"bank{(per * i + c) % 8}", name="summed") for c in range(per)]
-            for r in range(3):
-                weigh(terms, r, t0, TURNED_CHUNK)
-                for c in range(per):
+        for i, (t0, tokens) in enumerate(OUT_PIECES[:-1]):
+            blocks = tokens // P
+            tags = [f"bank{BANKS_A_PIECE * i + c}" for c in range(blocks)]
+            terms = loads.tile([P, TOP, tokens], F32, tag=take(), name="terms", align_bytes=64)
+            turned = loads.tile([P, blocks, P], F32, tag=take(), name="turned", align_bytes=64)
+            result = loads.tile([P, blocks, P], F32, tag=take(), name="result", align_bytes=64)
+            summed = [psum.tile([P, P], F32, tag=tag, name="summed") for tag in tags]
+            for r in range(TOP):
+                weigh(terms, r, t0, 0, tokens)
+                for c in range(blocks):
                     nc.tensor.matmul(
-                        summed[c][:], terms[:, r, c * P : (c + 1) * P], ident[:], start=(r == 0), stop=(r == 2), is_transpose=True
+                        summed[c][:],
+                        terms[:, r, c * P : (c + 1) * P],
+                        ident[:],
+                        start=(r == 0),
+                        stop=(r == TOP - 1),
+                        is_transpose=True,
                     )
-            back = [psum.tile([P, P], F32, tag=f"bank{(per * i + c) % 8}", name="back") for c in range(per)]
-            for c in range(per):
+            back = [psum.tile([P, P], F32, tag=tag, name="back") for tag in tags]
+            for c in range(blocks):
                 nc.scalar.copy(turned[:, c, :], summed[c][:])
                 nc.tensor.transpose(back[c][:], turned[:, c, :], ident[:])
-            for c0 in range(0, per, pair):
-                for c in range(c0, c0 + pair):
+            for c0 in range(0, blocks, STORE_BLOCKS):
+                c1 = min(c0 + STORE_BLOCKS, blocks)
+                for c in range(c0, c1):
                     nc.scalar.copy(result[:, c, :], back[c][:])
-                nc.sync.dma_start(
-                    out[:, t0 + c0 * P : t0 + (c0 + pair) * P], result[:, c0 : c0 + pair, :].rearrange("p c m -> p (c m)")
-                )
+                nc.scalar.dma_start(out[:, t0 + c0 * P : t0 + c1 * P], result[:, c0:c1, :].rearrange("p c m -> p (c m)"))
 
-        rest = T - TURNED
-        terms = raws.tile([P, 3, rest], F32, tag="raw", name="terms")
-        sums = raws.tile([P, 2, rest], F32, tag="raw", name="sums")
-        for r in range(3):
-            weigh(terms, r, TURNED, rest)
+        t0, tokens = OUT_PIECES[-1]
+        cut = tokens - P
+        terms = loads.tile([P, TOP, tokens], F32, tag=take(), name="terms", align_bytes=64)
+        sums = loads.tile([P, 2, tokens], F32, tag=take(), name="sums", align_bytes=64)
+        weigh(terms, 0, t0, 0, tokens)
+        weigh(terms, 1, t0, 0, tokens)
+        weigh(terms, 2, t0, 0, cut)
         nc.vector.tensor_tensor(sums[:, 0, :], terms[:, 0, :], terms[:, 1, :], ADD)
-        nc.vector.tensor_tensor(sums[:, 1, :], sums[:, 0, :], terms[:, 2, :], ADD)
-        nc.sync.dma_start(out[:, TURNED:T], sums[:, 1, :])
+        weigh(terms, 2, t0, cut, tokens)
+        for c0, c1 in ((0, cut), (cut, tokens)):
+            nc.vector.tensor_tensor(sums[:, 1, c0:c1], sums[:, 0, c0:c1], terms[:, 2, c0:c1], ADD)
+            nc.sync.dma_start(out[:, t0 + c0 : t0 + c1], sums[:, 1, c0:c1])

@@ -20,7 +20,7 @@ STRIPE = 16
 RUN = 4
 FLOPS = 2 * 1536 * 128 * 3840
 
-FIRST_PIECES = ((0, 512, 512), (512, 512, 344), (1024, 256, 128))
+FIRST_PIECES = ((0, 512, 512), (512, 512, 256), (1024, 256, 128))
 LATER_PIECES = ((0, 256, 0), (256, 512, 0), (768, 512, 0))
 WEIGHT_PIECES = (4,) * 10 + (2, 2, 1)
 EARLY_GATHER, EARLY_WINDOW, LATE_WINDOW = 1280, 1792, 1408
@@ -60,9 +60,7 @@ def tile_moe_tk_lin_bias_kernel(tc, xT, w, b, gate, offs, pos1, pos2, pos3, out)
         slot_words = [held.tile([P, S], U32, name="slot_words0", align_bytes=64)]
         y = held.tile([P, S], F32, name="y")
 
-        nc.vector.memset(token_scales[:].bitcast(U32), 0)
-        for words in token_words:
-            nc.vector.memset(words[:, T:], 0)
+        nc.vector.memset(token_scales[:, :T].bitcast(U32), 0)
 
         free = [f"buffer{i}" for i in range(BUFFERS)]
 
@@ -87,9 +85,8 @@ def tile_moe_tk_lin_bias_kernel(tc, xT, w, b, gate, offs, pos1, pos2, pos3, out)
             raw_w[piece] = loads.tile([P, count, PACK * N], F32, tag=buffer_of[piece], name="raw_w", align_bytes=64)
             nc.sync.dma_start(raw_w[piece][:], w_view[:, m0 : m0 + count, :])
 
-        load_x(0, FIRST_PIECES[:1])
+        load_x(0, FIRST_PIECES)
         nc.sync.dma_start(offs_sb[:], offs)
-        load_x(0, FIRST_PIECES[1:])
         load_x(1, LATER_PIECES)
         load_w(0)
         load_x(2, LATER_PIECES)
@@ -109,24 +106,29 @@ def tile_moe_tk_lin_bias_kernel(tc, xT, w, b, gate, offs, pos1, pos2, pos3, out)
             gates[t0] = loads.tile([P, TOP, tokens], F32, tag=take(keep=True), name="gates", align_bytes=64)
             nc.sync.dma_start(gates[t0][:], gate[:, :, t0 : t0 + tokens].rearrange("r p t -> p r t"))
 
+        rounded_x = {}
+
+        def round_x(a, t0, tokens, on_vector):
+            rounded_x[a, t0] = rounds.tile([P, tokens, PACK], BF16, name="rounded", align_bytes=64)
+            src = raw_x[a, t0][:].rearrange("p j (c i) -> p c j i", i=RUN)
+            dst = rounded_x[a, t0][:].rearrange("p (c i) j -> p c j i", i=RUN)
+            cut = on_vector // RUN
+            if on_vector:
+                nc.vector.tensor_copy(dst[:, :cut], src[:, :cut])
+            if on_vector < tokens:
+                nc.scalar.copy(dst[:, cut:], src[:, cut:])
+
+        def quantize_tokens(a, t0, c0, c1):
+            nc.vector.quantize_mx(
+                out=token_words[a][:, t0 + c0 : t0 + c1].bitcast(FP8X4),
+                scales=token_scales[4 * a : P, t0 + c0 : t0 + c1],
+                in_=rounded_x[a, t0][:, c0:c1, :].rearrange("p t j -> p (t j)"),
+            )
+
         def quantize_x(a, pieces):
             for t0, tokens, on_vector in pieces:
-                if (a, t0) == (0, FIRST_PIECES[-1][0]):
-                    rounded = held.tile([P, tokens, PACK], BF16, tag="identity", name="rounded_last", align_bytes=64)
-                else:
-                    rounded = rounds.tile([P, tokens, PACK], BF16, name="rounded", align_bytes=64)
-                src = raw_x[a, t0][:].rearrange("p j (c i) -> p c j i", i=RUN)
-                dst = rounded[:].rearrange("p (c i) j -> p c j i", i=RUN)
-                cut = on_vector // RUN
-                if on_vector:
-                    nc.vector.tensor_copy(dst[:, :cut], src[:, :cut])
-                if on_vector < tokens:
-                    nc.scalar.copy(dst[:, cut:], src[:, cut:])
-                nc.vector.quantize_mx(
-                    out=token_words[a][:, t0 : t0 + tokens].bitcast(FP8X4),
-                    scales=token_scales[4 * a : P, t0 : t0 + tokens],
-                    in_=rounded[:].rearrange("p t j -> p (t j)"),
-                )
+                round_x(a, t0, tokens, on_vector)
+                quantize_tokens(a, t0, 0, tokens)
 
         w_words = []
         w_scales = []
@@ -155,9 +157,15 @@ def tile_moe_tk_lin_bias_kernel(tc, xT, w, b, gate, offs, pos1, pos2, pos3, out)
             for s0 in range(0, S, EARLY_GATHER):
                 gather(slot_words[a][:, s0 : s0 + EARLY_GATHER], token_words[a], s0, EARLY_GATHER)
 
-        quantize_x(0, FIRST_PIECES)
-        ident = held.tile([P, P], F32, tag="identity", name="ident", align_bytes=64)
+        ident = held.tile([P, P], F32, name="ident", align_bytes=64)
         make_identity(nc, ident[:])
+        first, second, third = FIRST_PIECES
+        quantize_x(0, [first])
+        round_x(0, *second)
+        quantize_tokens(0, second[0], 0, second[2])
+        round_x(0, *third)
+        quantize_tokens(0, second[0], second[2], second[1])
+        quantize_tokens(0, third[0], 0, third[1])
         gather_early(0)
         quantize_x(1, LATER_PIECES)
         quantize_w(0)
@@ -176,6 +184,7 @@ def tile_moe_tk_lin_bias_kernel(tc, xT, w, b, gate, offs, pos1, pos2, pos3, out)
 
         products = {}
         passes_done = [0] * E
+        last_half = []
 
         def multiply():
             for e in range(E):
@@ -191,15 +200,21 @@ def tile_moe_tk_lin_bias_kernel(tc, xT, w, b, gate, offs, pos1, pos2, pos3, out)
                         bank = psum.tile([P, 2, C], F32, tag=f"bank{e // 2}", name="bank")
                         products[e], products[e + 1] = bank[:, 0, :], bank[:, 1, :]
                     moving = slot_words[a][:, e * C : (e + 1) * C] if a < passes - 1 else last_words[e]
-                    nc.tensor.matmul_mx(
-                        out=products[e],
-                        lhsT=w_words[passes * e + a].bitcast(FP8X4),
-                        lhsT_scale=w_scales[passes * e + a],
-                        rhs=moving.bitcast(FP8X4),
-                        rhs_scale=slot_scales[e][4 * a : P, :],
-                        start=(a == 0),
-                        stop=(a == passes - 1),
-                    )
+                    if a == 0 and e == E - 1:
+                        last_half.append(psum.tile([P, C // 2], F32, tag="bank1", name="bank")[:])
+                    parts = [(products[e], 0, C)]
+                    if e == E - 1:
+                        parts = [(products[e][:, : C // 2], 0, C // 2), (last_half[0], C // 2, C)]
+                    for dst, c0, c1 in parts:
+                        nc.tensor.matmul_mx(
+                            out=dst,
+                            lhsT=w_words[passes * e + a].bitcast(FP8X4),
+                            lhsT_scale=w_scales[passes * e + a],
+                            rhs=moving[:, c0:c1].bitcast(FP8X4),
+                            rhs_scale=slot_scales[e][4 * a : P, c0:c1],
+                            start=(a == 0),
+                            stop=(a == passes - 1),
+                        )
                     passes_done[e] += 1
 
         for piece in range(1, len(weight_pieces)):
@@ -215,7 +230,12 @@ def tile_moe_tk_lin_bias_kernel(tc, xT, w, b, gate, offs, pos1, pos2, pos3, out)
             for e0, e1, before in BIAS_PARTS:
                 if before - 1 == piece:
                     for e in range(e0, e1):
-                        nc.scalar.activation(y[:, e * C : (e + 1) * C], products[e], IDENTITY, bias=bias[e])
+                        if e < E - 1:
+                            nc.scalar.activation(y[:, e * C : (e + 1) * C], products[e], IDENTITY, bias=bias[e])
+                        else:
+                            mid = e * C + C // 2
+                            nc.scalar.activation(y[:, e * C : mid], products[e][:, : C // 2], IDENTITY, bias=bias[e])
+                            nc.scalar.activation(y[:, mid:], last_half[0], IDENTITY, bias=bias[e])
 
         free.extend(buffer_of[piece] for piece in lenders)
 

@@ -24,8 +24,8 @@ FIRST_PIECES = ((0, 512, 512), (512, 512, 256), (1024, 256, 128))
 LATER_PIECES = ((0, 256, 0), (256, 512, 0), (768, 512, 0))
 WEIGHT_PIECES = (4,) * 10 + (2, 2, 1)
 EARLY_GATHER, EARLY_WINDOW, LATE_WINDOW = 1280, 1792, 1408
-SCALE_GATHERS = ((0, 1024, 1), (1024, 1024, 3), (2048, 1024, 5), (3072, 768, 7))
-WORD_GATHERS = ((0, 1024, 2), (1024, 1024, 4), (2048, 1024, 6), (3072, 512, 9), (3584, 256, 11))
+SCALE_GATHERS = ((0, 1024, 1), (1024, 1024, 3), (2048, 1024, 5), (3072, 768, 8))
+WORD_GATHERS = ((0, 1024, 2), (1024, 1024, 4), (2048, 1024, 6), (3072, 512, 10), (3584, 256, 11))
 BIAS_PARTS = ((0, 4, 7), (4, 8, 10), (8, 15, 13))
 PAIRED = 12
 BUFFERS = 13

@@ -10,6 +10,7 @@ U16 = mybir.dt.uint16
 U8 = mybir.dt.uint8
 FP8X4 = mybir.dt.float8_e4m3fn_x4
 IDENTITY = mybir.ActivationFunctionType.Identity
+COPY = mybir.ActivationFunctionType.Copy
 MULT = mybir.AluOpType.mult
 ADD = mybir.AluOpType.add
 
@@ -29,9 +30,10 @@ WORD_GATHERS = ((0, 1024, 2), (1024, 1024, 4), (2048, 1024, 6), (3072, 512, 10),
 BIAS_PARTS = ((0, 4, 7), (4, 8, 10), (8, 15, 13))
 PAIRED = 12
 BUFFERS = 13
-OUT_PIECES = ((0, 512), (512, 384), (896, 384))
-BANKS_A_PIECE = 4
-STORE_BLOCKS = 2
+VECTOR_PIECE = (896, 384)
+BANK_BLOCKS = 4
+LEAD = 3
+FINISH_GROUPS = ((0, 2, 0), (2, 4, 1), (4, 6, 6), (6, 7, 7))
 
 
 def tile_moe_tk_lin_bias_kernel(tc, xT, w, b, gate, offs, pos1, pos2, pos3, out):
@@ -61,6 +63,10 @@ def tile_moe_tk_lin_bias_kernel(tc, xT, w, b, gate, offs, pos1, pos2, pos3, out)
         y = held.tile([P, S], F32, name="y")
 
         nc.vector.memset(token_scales[:, :T].bitcast(U32), 0)
+        shared_blocks = VECTOR_PIECE[0] // P
+        gate_rows = held.tile([P, P], F32, name="gate_rows", align_bytes=64)
+        gate_columns = held.tile([P, (TOP - 1) * shared_blocks], F32, name="gate_columns")
+        nc.vector.memset(gate_rows[:], 0.0)
 
         free = [f"buffer{i}" for i in range(BUFFERS)]
 
@@ -90,6 +96,9 @@ def tile_moe_tk_lin_bias_kernel(tc, xT, w, b, gate, offs, pos1, pos2, pos3, out)
         load_x(1, LATER_PIECES)
         load_w(0)
         load_x(2, LATER_PIECES)
+        for r in range(1, TOP):
+            rows = gate_rows[(r - 1) * shared_blocks : r * shared_blocks, :]
+            nc.sync.dma_start(rows, gate[r, 0, : shared_blocks * P].rearrange("(c t) -> c t", t=P))
         loaded = 1
         bias = []
         for e0, e1, before in BIAS_PARTS:
@@ -101,10 +110,11 @@ def tile_moe_tk_lin_bias_kernel(tc, xT, w, b, gate, offs, pos1, pos2, pos3, out)
             bias.extend(part[:, i : i + 1] for i in range(e1 - e0))
         for pos_tile, pos in zip(pos_sb, (pos1, pos2, pos3)):
             nc.sync.dma_start(pos_tile[:], pos)
-        gates = {}
-        for t0, tokens in OUT_PIECES:
-            gates[t0] = loads.tile([P, TOP, tokens], F32, tag=take(keep=True), name="gates", align_bytes=64)
-            nc.sync.dma_start(gates[t0][:], gate[:, :, t0 : t0 + tokens].rearrange("r p t -> p r t"))
+        t0, tokens = VECTOR_PIECE
+        first_gates = loads.tile([P, t0], F32, tag=take(keep=True), name="first_gates", align_bytes=64)
+        nc.sync.dma_start(first_gates[:], gate[0, :, :t0])
+        gates = loads.tile([P, TOP, tokens], F32, tag=take(keep=True), name="gates", align_bytes=64)
+        nc.sync.dma_start(gates[:], gate[:, :, t0:].rearrange("r p t -> p r t"))
 
         rounded_x = {}
 
@@ -173,6 +183,10 @@ def tile_moe_tk_lin_bias_kernel(tc, xT, w, b, gate, offs, pos1, pos2, pos3, out)
         gather_early(1)
         quantize_x(2, LATER_PIECES)
 
+        gates_turned = psum.tile([P, P], F32, tag="bank7", name="gates_turned")
+        nc.tensor.transpose(gates_turned[:], gate_rows[:], ident[:])
+        nc.scalar.copy(gate_columns[:], gates_turned[:, : (TOP - 1) * shared_blocks])
+
         slot_scales = {}
         last_words = {}
 
@@ -239,47 +253,55 @@ def tile_moe_tk_lin_bias_kernel(tc, xT, w, b, gate, offs, pos1, pos2, pos3, out)
 
         free.extend(buffer_of[piece] for piece in lenders)
 
-        def weigh(terms, r, t0, c0, c1):
-            entries = pos_sb[r][:, (t0 + c0) // STRIPE : (t0 + c1) // STRIPE]
-            nc.vector.tensor_tensor(terms[:, r, c0:c1], y[:].indirect(entries), gates[t0][:, r, c0:c1], MULT)
+        def entries(r, t0, tokens):
+            return pos_sb[r][:, t0 // STRIPE : (t0 + tokens) // STRIPE]
 
-        for i, (t0, tokens) in enumerate(OUT_PIECES[:-1]):
-            blocks = tokens // P
-            tags = [f"bank{BANKS_A_PIECE * i + c}" for c in range(blocks)]
-            terms = loads.tile([P, TOP, tokens], F32, tag=take(), name="terms", align_bytes=64)
-            turned = loads.tile([P, blocks, P], F32, tag=take(), name="turned", align_bytes=64)
-            result = loads.tile([P, blocks, P], F32, tag=take(), name="result", align_bytes=64)
-            summed = [psum.tile([P, P], F32, tag=tag, name="summed") for tag in tags]
-            for r in range(TOP):
-                weigh(terms, r, t0, 0, tokens)
-                for c in range(blocks):
+        t0, tokens = VECTOR_PIECE
+        turned = {}
+        weighed = {}
+        for r in range(1, TOP):
+            plain = loads.tile([P, t0], F32, tag=take(), name="plain", align_bytes=64)
+            nc.scalar.activation(plain[:], y[:].indirect(entries(r, 0, t0)), COPY)
+            weighed[r] = loads.tile([P, shared_blocks, P], F32, tag=take(), name="weighed", align_bytes=64)
+            for c0 in range(0, shared_blocks, BANK_BLOCKS):
+                c1 = min(c0 + BANK_BLOCKS, shared_blocks)
+                bank = psum.tile([P, c1 - c0, P], F32, tag=f"bank{2 * r + c0 // BANK_BLOCKS}", name="turned")
+                for c in range(c0, c1):
+                    turned[r, c] = bank[:, c - c0, :]
+                    nc.tensor.transpose(turned[r, c], plain[:, c * P : (c + 1) * P], ident[:])
+
+        def weigh_turned(r, c):
+            column = (r - 1) * shared_blocks + c
+            nc.scalar.activation(weighed[r][:, c, :], turned[r, c], COPY, scale=gate_columns[:, column : column + 1])
+
+        terms = loads.tile([P, TOP, tokens], F32, tag=take(), name="terms", align_bytes=64)
+        sums = loads.tile([P, 2, tokens], F32, tag=take(), name="sums", align_bytes=64)
+        first = loads.tile([P, t0], F32, tag=take(), name="first", align_bytes=64)
+        result = loads.tile([P, t0], F32, tag=take(), name="result", align_bytes=64)
+        for r in range(TOP):
+            nc.vector.tensor_tensor(terms[:, r, :], y[:].indirect(entries(r, t0, tokens)), gates[:, r, :], MULT)
+        nc.vector.tensor_tensor(sums[:, 0, :], terms[:, 0, :], terms[:, 1, :], ADD)
+        nc.vector.tensor_tensor(first[:], y[:].indirect(entries(0, 0, t0)), first_gates[:], MULT)
+        nc.vector.tensor_tensor(sums[:, 1, :], sums[:, 0, :], terms[:, 2, :], ADD)
+        nc.sync.dma_start(out[:, t0:], sums[:, 1, :])
+
+        for c in range(LEAD):
+            weigh_turned(1, c)
+        for c0, c1, bank in FINISH_GROUPS:
+            back = psum.tile([P, c1 - c0, P], F32, tag=f"bank{bank}", name="back")
+            for c in range(c0, c1):
+                if c >= LEAD:
+                    weigh_turned(1, c)
+                weigh_turned(2, c)
+                for r in range(1, TOP):
                     nc.tensor.matmul(
-                        summed[c][:],
-                        terms[:, r, c * P : (c + 1) * P],
+                        back[:, c - c0, :],
+                        weighed[r][:, c, :],
                         ident[:],
-                        start=(r == 0),
+                        start=(r == 1),
                         stop=(r == TOP - 1),
                         is_transpose=True,
                     )
-            back = [psum.tile([P, P], F32, tag=tag, name="back") for tag in tags]
-            for c in range(blocks):
-                nc.scalar.copy(turned[:, c, :], summed[c][:])
-                nc.tensor.transpose(back[c][:], turned[:, c, :], ident[:])
-            for c0 in range(0, blocks, STORE_BLOCKS):
-                c1 = min(c0 + STORE_BLOCKS, blocks)
-                for c in range(c0, c1):
-                    nc.scalar.copy(result[:, c, :], back[c][:])
-                nc.scalar.dma_start(out[:, t0 + c0 * P : t0 + c1 * P], result[:, c0:c1, :].rearrange("p c m -> p (c m)"))
-
-        t0, tokens = OUT_PIECES[-1]
-        cut = tokens - P
-        terms = loads.tile([P, TOP, tokens], F32, tag=take(), name="terms", align_bytes=64)
-        sums = loads.tile([P, 2, tokens], F32, tag=take(), name="sums", align_bytes=64)
-        weigh(terms, 0, t0, 0, tokens)
-        weigh(terms, 1, t0, 0, tokens)
-        weigh(terms, 2, t0, 0, cut)
-        nc.vector.tensor_tensor(sums[:, 0, :], terms[:, 0, :], terms[:, 1, :], ADD)
-        weigh(terms, 2, t0, cut, tokens)
-        for c0, c1 in ((0, cut), (cut, tokens)):
-            nc.vector.tensor_tensor(sums[:, 1, c0:c1], sums[:, 0, c0:c1], terms[:, 2, c0:c1], ADD)
-            nc.sync.dma_start(out[:, t0 + c0 : t0 + c1], sums[:, 1, c0:c1])
+            columns = slice(c0 * P, c1 * P)
+            nc.vector.tensor_tensor(result[:, columns], back[:].rearrange("p c m -> p (c m)"), first[:, columns], ADD)
+            nc.sync.dma_start(out[:, columns], result[:, columns])

@@ -30,10 +30,7 @@ WORD_GATHERS = ((0, 1024, 2), (1024, 1024, 4), (2048, 1024, 6), (3072, 512, 10),
 BIAS_PARTS = ((0, 4, 7), (4, 8, 10), (8, 15, 13))
 PAIRED = 12
 BUFFERS = 13
-VECTOR_PIECE = (896, 384)
-BANK_BLOCKS = 4
-LEAD = 3
-FINISH_GROUPS = ((0, 2, 0), (2, 4, 1), (4, 6, 6), (6, 7, 7))
+SCALAR_FROM = (10, 4, 3)
 
 
 def tile_moe_tk_lin_bias_kernel(tc, xT, w, b, gate, offs, pos1, pos2, pos3, out):
@@ -63,9 +60,10 @@ def tile_moe_tk_lin_bias_kernel(tc, xT, w, b, gate, offs, pos1, pos2, pos3, out)
         y = held.tile([P, S], F32, name="y")
 
         nc.vector.memset(token_scales[:, :T].bitcast(U32), 0)
-        shared_blocks = VECTOR_PIECE[0] // P
+        blocks = T // P
+        turned_terms = [(r, c) for r in range(TOP) for c in range(SCALAR_FROM[r], blocks)]
         gate_rows = held.tile([P, P], F32, name="gate_rows", align_bytes=64)
-        gate_columns = held.tile([P, (TOP - 1) * shared_blocks], F32, name="gate_columns")
+        gate_columns = held.tile([P, len(turned_terms)], F32, name="gate_columns")
         nc.vector.memset(gate_rows[:], 0.0)
 
         free = [f"buffer{i}" for i in range(BUFFERS)]
@@ -97,8 +95,9 @@ def tile_moe_tk_lin_bias_kernel(tc, xT, w, b, gate, offs, pos1, pos2, pos3, out)
         load_w(0)
         load_x(2, LATER_PIECES)
         for r in range(1, TOP):
-            rows = gate_rows[(r - 1) * shared_blocks : r * shared_blocks, :]
-            nc.sync.dma_start(rows, gate[r, 0, : shared_blocks * P].rearrange("(c t) -> c t", t=P))
+            row = turned_terms.index((r, SCALAR_FROM[r]))
+            rows = gate_rows[row : row + blocks - SCALAR_FROM[r], :]
+            nc.sync.dma_start(rows, gate[r, 0, SCALAR_FROM[r] * P :].rearrange("(c t) -> c t", t=P))
         loaded = 1
         bias = []
         for e0, e1, before in BIAS_PARTS:
@@ -110,11 +109,10 @@ def tile_moe_tk_lin_bias_kernel(tc, xT, w, b, gate, offs, pos1, pos2, pos3, out)
             bias.extend(part[:, i : i + 1] for i in range(e1 - e0))
         for pos_tile, pos in zip(pos_sb, (pos1, pos2, pos3)):
             nc.sync.dma_start(pos_tile[:], pos)
-        t0, tokens = VECTOR_PIECE
-        first_gates = loads.tile([P, t0], F32, tag=take(keep=True), name="first_gates", align_bytes=64)
-        nc.sync.dma_start(first_gates[:], gate[0, :, :t0])
-        gates = loads.tile([P, TOP, tokens], F32, tag=take(keep=True), name="gates", align_bytes=64)
-        nc.sync.dma_start(gates[:], gate[:, :, t0:].rearrange("r p t -> p r t"))
+        gates = []
+        for r in range(TOP):
+            gates.append(loads.tile([P, SCALAR_FROM[r] * P], F32, tag=take(keep=True), name="gates", align_bytes=64))
+            nc.sync.dma_start(gates[r][:], gate[r, :, : SCALAR_FROM[r] * P])
 
         rounded_x = {}
 
@@ -185,7 +183,7 @@ def tile_moe_tk_lin_bias_kernel(tc, xT, w, b, gate, offs, pos1, pos2, pos3, out)
 
         gates_turned = psum.tile([P, P], F32, tag="bank7", name="gates_turned")
         nc.tensor.transpose(gates_turned[:], gate_rows[:], ident[:])
-        nc.scalar.copy(gate_columns[:], gates_turned[:, : (TOP - 1) * shared_blocks])
+        nc.scalar.copy(gate_columns[:], gates_turned[:, : len(turned_terms)])
 
         slot_scales = {}
         last_words = {}
@@ -253,55 +251,73 @@ def tile_moe_tk_lin_bias_kernel(tc, xT, w, b, gate, offs, pos1, pos2, pos3, out)
 
         free.extend(buffer_of[piece] for piece in lenders)
 
-        def entries(r, t0, tokens):
-            return pos_sb[r][:, t0 // STRIPE : (t0 + tokens) // STRIPE]
+        def entries(r, c0, c1):
+            return pos_sb[r][:, c0 * P // STRIPE : c1 * P // STRIPE]
 
-        t0, tokens = VECTOR_PIECE
         turned = {}
         weighed = {}
-        for r in range(1, TOP):
-            plain = loads.tile([P, t0], F32, tag=take(), name="plain", align_bytes=64)
-            nc.scalar.activation(plain[:], y[:].indirect(entries(r, 0, t0)), COPY)
-            weighed[r] = loads.tile([P, shared_blocks, P], F32, tag=take(), name="weighed", align_bytes=64)
-            for c0 in range(0, shared_blocks, BANK_BLOCKS):
-                c1 = min(c0 + BANK_BLOCKS, shared_blocks)
-                bank = psum.tile([P, c1 - c0, P], F32, tag=f"bank{2 * r + c0 // BANK_BLOCKS}", name="turned")
-                for c in range(c0, c1):
-                    turned[r, c] = bank[:, c - c0, :]
-                    nc.tensor.transpose(turned[r, c], plain[:, c * P : (c + 1) * P], ident[:])
+        so_far = {}
 
-        def weigh_turned(r, c):
-            column = (r - 1) * shared_blocks + c
-            nc.scalar.activation(weighed[r][:, c, :], turned[r, c], COPY, scale=gate_columns[:, column : column + 1])
+        def fetch(r, c0, c1, bank, tag):
+            plain = loads.tile([P, c1 - c0, P], F32, tag=tag, name="plain", align_bytes=64)
+            nc.scalar.activation(plain[:].rearrange("p c t -> p (c t)"), y[:].indirect(entries(r, c0, c1)), COPY)
+            tile = psum.tile([P, c1 - c0, P], F32, tag=f"bank{bank}", name="turned")
+            for c in range(c0, c1):
+                turned[r, c] = tile[:, c - c0, :]
+                nc.tensor.transpose(turned[r, c], plain[:, c - c0, :], ident[:])
 
-        terms = loads.tile([P, TOP, tokens], F32, tag=take(), name="terms", align_bytes=64)
-        sums = loads.tile([P, 2, tokens], F32, tag=take(), name="sums", align_bytes=64)
-        first = loads.tile([P, t0], F32, tag=take(), name="first", align_bytes=64)
-        result = loads.tile([P, t0], F32, tag=take(), name="result", align_bytes=64)
-        for r in range(TOP):
-            nc.vector.tensor_tensor(terms[:, r, :], y[:].indirect(entries(r, t0, tokens)), gates[:, r, :], MULT)
-        nc.vector.tensor_tensor(sums[:, 0, :], terms[:, 0, :], terms[:, 1, :], ADD)
-        nc.vector.tensor_tensor(first[:], y[:].indirect(entries(0, 0, t0)), first_gates[:], MULT)
-        nc.vector.tensor_tensor(sums[:, 1, :], sums[:, 0, :], terms[:, 2, :], ADD)
-        nc.sync.dma_start(out[:, t0:], sums[:, 1, :])
-
-        for c in range(LEAD):
-            weigh_turned(1, c)
-        for c0, c1, bank in FINISH_GROUPS:
+        def turn_back(c0, c1, bank, tag):
+            tile = loads.tile([P, c1 - c0, TOP - 1, P], F32, tag=tag, name="weighed", align_bytes=64)
             back = psum.tile([P, c1 - c0, P], F32, tag=f"bank{bank}", name="back")
             for c in range(c0, c1):
-                if c >= LEAD:
-                    weigh_turned(1, c)
-                weigh_turned(2, c)
-                for r in range(1, TOP):
+                present = [r for r in range(1, TOP) if c >= SCALAR_FROM[r]]
+                for r in present:
+                    column = turned_terms.index((r, c))
+                    nc.scalar.activation(
+                        tile[:, c - c0, r - 1, :], turned[r, c], COPY, scale=gate_columns[:, column : column + 1]
+                    )
                     nc.tensor.matmul(
                         back[:, c - c0, :],
-                        weighed[r][:, c, :],
+                        tile[:, c - c0, r - 1, :],
                         ident[:],
-                        start=(r == 1),
-                        stop=(r == TOP - 1),
+                        start=(r == present[0]),
+                        stop=(r == present[-1]),
                         is_transpose=True,
                     )
-            columns = slice(c0 * P, c1 * P)
-            nc.vector.tensor_tensor(result[:, columns], back[:].rearrange("p c m -> p (c m)"), first[:, columns], ADD)
-            nc.sync.dma_start(out[:, columns], result[:, columns])
+            return back[:].rearrange("p c m -> p (c m)")
+
+        def weigh(r, c0, c1, term):
+            nc.vector.tensor_tensor(term, y[:].indirect(entries(r, c0, c1)), gates[r][:, c0 * P : c1 * P], MULT)
+            return term
+
+        def finish(c0, c1, one, other):
+            nc.vector.tensor_tensor(result[:, c0 * P : c1 * P], one, other, ADD)
+            nc.sync.dma_start(out[:, c0 * P : c1 * P], result[:, c0 * P : c1 * P])
+
+        ring = [take(keep=True) for i in range(3)]
+        early_tag = take(keep=True)
+        fetch(2, 3, 6, 2, ring[0])
+        fetch(1, 4, 7, 3, ring[1])
+        fetch(2, 6, 8, 4, ring[2])
+        back4 = turn_back(4, 6, 7, early_tag)
+        back3 = turn_back(3, 4, 0, take())
+        fetch(1, 7, 10, 5, ring[0])
+        fetch(2, 8, 10, 6, ring[1])
+        back6 = turn_back(6, 8, 1, take())
+        back8 = turn_back(8, 10, 2, take())
+
+        result = loads.tile([P, T], F32, tag=take(), name="result", align_bytes=64)
+        terms = loads.tile([P, 13 * P], F32, tag=take(), name="terms", align_bytes=64)
+        pair = loads.tile([P, 4 * P], F32, tag=take(), name="pair", align_bytes=64)
+        term0 = weigh(0, 0, 4, terms[:, : 4 * P])
+        term1 = weigh(1, 0, 4, terms[:, 4 * P : 8 * P])
+        term2 = weigh(2, 0, 3, terms[:, 8 * P : 11 * P])
+        nc.vector.tensor_tensor(pair[:], term0, term1, ADD)
+        first4 = weigh(0, 4, 6, terms[:, 11 * P :])
+        finish(0, 3, pair[:, : 3 * P], term2)
+        finish(4, 6, back4, first4)
+        first6 = loads.tile([P, 4 * P], F32, tag=early_tag, name="first6", align_bytes=64)
+        weigh(0, 6, 10, first6[:])
+        finish(3, 4, back3, pair[:, 3 * P :])
+        finish(6, 8, back6, first6[:, : 2 * P])
+        finish(8, 10, back8, first6[:, 2 * P :])

@@ -30,7 +30,7 @@ WORD_GATHERS = ((0, 1024, 2), (1024, 1024, 4), (2048, 1024, 6), (3072, 512, 10),
 BIAS_PARTS = ((0, 4, 7), (4, 8, 10), (8, 15, 13))
 PAIRED = 12
 BUFFERS = 13
-SCALAR_FROM = (10, 4, 3)
+SCALAR_FROM = (6, 6, 5)
 
 
 def tile_moe_tk_lin_bias_kernel(tc, xT, w, b, gate, offs, pos1, pos2, pos3, out):
@@ -94,7 +94,7 @@ def tile_moe_tk_lin_bias_kernel(tc, xT, w, b, gate, offs, pos1, pos2, pos3, out)
         load_x(1, LATER_PIECES)
         load_w(0)
         load_x(2, LATER_PIECES)
-        for r in range(1, TOP):
+        for r in range(TOP):
             row = turned_terms.index((r, SCALAR_FROM[r]))
             rows = gate_rows[row : row + blocks - SCALAR_FROM[r], :]
             nc.sync.dma_start(rows, gate[r, 0, SCALAR_FROM[r] * P :].rearrange("(c t) -> c t", t=P))
@@ -255,8 +255,6 @@ def tile_moe_tk_lin_bias_kernel(tc, xT, w, b, gate, offs, pos1, pos2, pos3, out)
             return pos_sb[r][:, c0 * P // STRIPE : c1 * P // STRIPE]
 
         turned = {}
-        weighed = {}
-        so_far = {}
 
         def fetch(r, c0, c1, bank, tag):
             plain = loads.tile([P, c1 - c0, P], F32, tag=tag, name="plain", align_bytes=64)
@@ -266,25 +264,10 @@ def tile_moe_tk_lin_bias_kernel(tc, xT, w, b, gate, offs, pos1, pos2, pos3, out)
                 turned[r, c] = tile[:, c - c0, :]
                 nc.tensor.transpose(turned[r, c], plain[:, c - c0, :], ident[:])
 
-        def turn_back(c0, c1, bank, tag):
-            tile = loads.tile([P, c1 - c0, TOP - 1, P], F32, tag=tag, name="weighed", align_bytes=64)
-            back = psum.tile([P, c1 - c0, P], F32, tag=f"bank{bank}", name="back")
-            for c in range(c0, c1):
-                present = [r for r in range(1, TOP) if c >= SCALAR_FROM[r]]
-                for r in present:
-                    column = turned_terms.index((r, c))
-                    nc.scalar.activation(
-                        tile[:, c - c0, r - 1, :], turned[r, c], COPY, scale=gate_columns[:, column : column + 1]
-                    )
-                    nc.tensor.matmul(
-                        back[:, c - c0, :],
-                        tile[:, c - c0, r - 1, :],
-                        ident[:],
-                        start=(r == present[0]),
-                        stop=(r == present[-1]),
-                        is_transpose=True,
-                    )
-            return back[:].rearrange("p c m -> p (c m)")
+        def weigh_turned(r, c, back, start, stop):
+            column = turned_terms.index((r, c))
+            nc.scalar.activation(weighed[:, column, :], turned[r, c], COPY, scale=gate_columns[:, column : column + 1])
+            nc.tensor.matmul(back, weighed[:, column, :], ident[:], start=start, stop=stop, is_transpose=True)
 
         def weigh(r, c0, c1, term):
             nc.vector.tensor_tensor(term, y[:].indirect(entries(r, c0, c1)), gates[r][:, c0 * P : c1 * P], MULT)
@@ -294,30 +277,44 @@ def tile_moe_tk_lin_bias_kernel(tc, xT, w, b, gate, offs, pos1, pos2, pos3, out)
             nc.vector.tensor_tensor(result[:, c0 * P : c1 * P], one, other, ADD)
             nc.sync.dma_start(out[:, c0 * P : c1 * P], result[:, c0 * P : c1 * P])
 
-        ring = [take(keep=True) for i in range(3)]
-        early_tag = take(keep=True)
-        fetch(2, 3, 6, 2, ring[0])
-        fetch(1, 4, 7, 3, ring[1])
-        fetch(2, 6, 8, 4, ring[2])
-        back4 = turn_back(4, 6, 7, early_tag)
-        back3 = turn_back(3, 4, 0, take())
-        fetch(1, 7, 10, 5, ring[0])
-        fetch(2, 8, 10, 6, ring[1])
-        back6 = turn_back(6, 8, 1, take())
-        back8 = turn_back(8, 10, 2, take())
+        def hand_out(c0, c1, back, queue):
+            nc.scalar.copy(result[:, c0 * P : c1 * P], back)
+            queue.dma_start(out[:, c0 * P : c1 * P], result[:, c0 * P : c1 * P])
 
         result = loads.tile([P, T], F32, tag=take(), name="result", align_bytes=64)
-        terms = loads.tile([P, 13 * P], F32, tag=take(), name="terms", align_bytes=64)
-        pair = loads.tile([P, 4 * P], F32, tag=take(), name="pair", align_bytes=64)
-        term0 = weigh(0, 0, 4, terms[:, : 4 * P])
-        term1 = weigh(1, 0, 4, terms[:, 4 * P : 8 * P])
-        term2 = weigh(2, 0, 3, terms[:, 8 * P : 11 * P])
-        nc.vector.tensor_tensor(pair[:], term0, term1, ADD)
-        first4 = weigh(0, 4, 6, terms[:, 11 * P :])
-        finish(0, 3, pair[:, : 3 * P], term2)
-        finish(4, 6, back4, first4)
-        first6 = loads.tile([P, 4 * P], F32, tag=early_tag, name="first6", align_bytes=64)
-        weigh(0, 6, 10, first6[:])
-        finish(3, 4, back3, pair[:, 3 * P :])
-        finish(6, 8, back6, first6[:, : 2 * P])
-        finish(8, 10, back8, first6[:, 2 * P :])
+        weighed = loads.tile([P, len(turned_terms), P], F32, tag=take(), name="weighed", align_bytes=64)
+        ring = [take(keep=True) for i in range(4)]
+        fetch(2, 5, 8, 2, ring[0])
+        fetch(1, 6, 8, 3, ring[1])
+        fetch(0, 6, 8, 4, ring[2])
+        fetch(2, 8, 10, 5, ring[3])
+        back5 = psum.tile([P, P], F32, tag="bank0", name="back")
+        weigh_turned(2, 5, back5[:], True, True)
+        back6 = psum.tile([P, 2, P], F32, tag="bank1", name="back")
+        for c in (6, 7):
+            for r in (2, 1, 0):
+                weigh_turned(r, c, back6[:, c - 6, :], r == 2, r == 0)
+        fetch(1, 8, 10, 6, ring[1])
+        fetch(0, 8, 10, 7, ring[2])
+        back8 = psum.tile([P, P], F32, tag="bank2", name="back")
+        back9 = psum.tile([P, P], F32, tag="bank3", name="back")
+        for r in (2, 1, 0):
+            weigh_turned(r, 8, back8[:], r == 2, r == 0)
+            weigh_turned(r, 9, back9[:], r == 2, r == 0)
+
+        terms01 = loads.tile([P, 2, 6 * P], F32, tag=take(), name="terms01", align_bytes=64)
+        term2 = loads.tile([P, 5 * P], F32, tag=take(), name="term2", align_bytes=64)
+        pair = loads.tile([P, 6 * P], F32, tag=take(), name="pair", align_bytes=64)
+        weigh(0, 0, 6, terms01[:, 0, :])
+        weigh(1, 0, 6, terms01[:, 1, :])
+        weigh(2, 0, 3, term2[:, : 3 * P])
+        nc.vector.tensor_tensor(pair[:], terms01[:, 0, :], terms01[:, 1, :], ADD)
+        weigh(2, 3, 5, term2[:, 3 * P :])
+        hand_out(6, 8, back6[:].rearrange("p c m -> p (c m)"), nc.sync)
+        finish(0, 3, pair[:, : 3 * P], term2[:, : 3 * P])
+        nc.vector.tensor_tensor(result[:, 5 * P : 6 * P], back5[:], pair[:, 5 * P :], ADD)
+        nc.scalar.copy(result[:, 8 * P : 9 * P], back8[:])
+        nc.scalar.copy(result[:, 9 * P :], back9[:])
+        nc.scalar.dma_start(out[:, 8 * P :], result[:, 8 * P :])
+        nc.vector.tensor_tensor(result[:, 3 * P : 5 * P], pair[:, 3 * P : 5 * P], term2[:, 3 * P :], ADD)
+        nc.sync.dma_start(out[:, 3 * P : 6 * P], result[:, 3 * P : 6 * P])

@@ -30,7 +30,7 @@ WORD_GATHERS = ((0, 1024, 2), (1024, 1024, 4), (2048, 1024, 6), (3072, 512, 10),
 BIAS_PARTS = ((0, 4, 7), (4, 8, 10), (8, 15, 13))
 PAIRED = 12
 BUFFERS = 13
-SCALAR_FROM = (6, 6, 5)
+SCALAR_FROM = (6, 6, 6)
 
 
 def tile_moe_tk_lin_bias_kernel(tc, xT, w, b, gate, offs, pos1, pos2, pos3, out):
@@ -266,8 +266,8 @@ def tile_moe_tk_lin_bias_kernel(tc, xT, w, b, gate, offs, pos1, pos2, pos3, out)
 
         def weigh_turned(r, c, back, start, stop):
             column = turned_terms.index((r, c))
-            nc.scalar.activation(weighed[:, column, :], turned[r, c], COPY, scale=gate_columns[:, column : column + 1])
-            nc.tensor.matmul(back, weighed[:, column, :], ident[:], start=start, stop=stop, is_transpose=True)
+            nc.scalar.activation(weighed[r, c], turned[r, c], COPY, scale=gate_columns[:, column : column + 1])
+            nc.tensor.matmul(back, weighed[r, c], ident[:], start=start, stop=stop, is_transpose=True)
 
         def weigh(r, c0, c1, term):
             nc.vector.tensor_tensor(term, y[:].indirect(entries(r, c0, c1)), gates[r][:, c0 * P : c1 * P], MULT)
@@ -282,39 +282,55 @@ def tile_moe_tk_lin_bias_kernel(tc, xT, w, b, gate, offs, pos1, pos2, pos3, out)
             queue.dma_start(out[:, c0 * P : c1 * P], result[:, c0 * P : c1 * P])
 
         result = loads.tile([P, T], F32, tag=take(), name="result", align_bytes=64)
-        weighed = loads.tile([P, len(turned_terms), P], F32, tag=take(), name="weighed", align_bytes=64)
+        weighed = {}
+
+        def room_for_weighed(c0, c1, tag):
+            tile = loads.tile([P, TOP, c1 - c0, P], F32, tag=tag, name="weighed", align_bytes=64)
+            for r in range(TOP):
+                for c in range(c0, c1):
+                    weighed[r, c] = tile[:, r, c - c0, :]
+
+        room_for_weighed(6, 8, take())
         ring = [take(keep=True) for i in range(4)]
-        fetch(2, 5, 8, 2, ring[0])
+        fetch(2, 6, 10, 2, ring[0])
         fetch(1, 6, 8, 3, ring[1])
         fetch(0, 6, 8, 4, ring[2])
-        fetch(2, 8, 10, 5, ring[3])
-        back5 = psum.tile([P, P], F32, tag="bank0", name="back")
-        weigh_turned(2, 5, back5[:], True, True)
+        fetch(1, 8, 10, 6, ring[3])
         back6 = psum.tile([P, 2, P], F32, tag="bank1", name="back")
         for c in (6, 7):
             for r in (2, 1, 0):
                 weigh_turned(r, c, back6[:, c - 6, :], r == 2, r == 0)
-        fetch(1, 8, 10, 6, ring[1])
         fetch(0, 8, 10, 7, ring[2])
-        back8 = psum.tile([P, P], F32, tag="bank2", name="back")
-        back9 = psum.tile([P, P], F32, tag="bank3", name="back")
+        room_for_weighed(8, 10, ring[3])
+        back8 = psum.tile([P, P], F32, tag="bank0", name="back")
+        back9 = psum.tile([P, P], F32, tag="bank5", name="back")
         for r in (2, 1, 0):
             weigh_turned(r, 8, back8[:], r == 2, r == 0)
             weigh_turned(r, 9, back9[:], r == 2, r == 0)
 
         terms01 = loads.tile([P, 2, 6 * P], F32, tag=take(), name="terms01", align_bytes=64)
-        term2 = loads.tile([P, 5 * P], F32, tag=take(), name="term2", align_bytes=64)
+        term2 = loads.tile([P, 6 * P], F32, tag=take(), name="term2", align_bytes=64)
         pair = loads.tile([P, 6 * P], F32, tag=take(), name="pair", align_bytes=64)
+
+        def add_pair(c0, c1):
+            columns = slice(c0 * P, c1 * P)
+            nc.vector.tensor_tensor(pair[:, columns], terms01[:, 0, columns], terms01[:, 1, columns], ADD)
+
+        def last(c0, c1):
+            finish(c0, c1, pair[:, c0 * P : c1 * P], term2[:, c0 * P : c1 * P])
+
         weigh(0, 0, 6, terms01[:, 0, :])
-        weigh(1, 0, 6, terms01[:, 1, :])
+        weigh(1, 0, 3, terms01[:, 1, : 3 * P])
         weigh(2, 0, 3, term2[:, : 3 * P])
-        nc.vector.tensor_tensor(pair[:], terms01[:, 0, :], terms01[:, 1, :], ADD)
-        weigh(2, 3, 5, term2[:, 3 * P :])
+        add_pair(0, 3)
+        weigh(1, 3, 6, terms01[:, 1, 3 * P :])
+        last(0, 3)
         hand_out(6, 8, back6[:].rearrange("p c m -> p (c m)"), nc.sync)
-        finish(0, 3, pair[:, : 3 * P], term2[:, : 3 * P])
-        nc.vector.tensor_tensor(result[:, 5 * P : 6 * P], back5[:], pair[:, 5 * P :], ADD)
+        add_pair(3, 6)
+        weigh(2, 3, 5, term2[:, 3 * P : 5 * P])
+        weigh(2, 5, 6, term2[:, 5 * P :])
+        last(3, 5)
         nc.scalar.copy(result[:, 8 * P : 9 * P], back8[:])
         nc.scalar.copy(result[:, 9 * P :], back9[:])
         nc.scalar.dma_start(out[:, 8 * P :], result[:, 8 * P :])
-        nc.vector.tensor_tensor(result[:, 3 * P : 5 * P], pair[:, 3 * P : 5 * P], term2[:, 3 * P :], ADD)
-        nc.sync.dma_start(out[:, 3 * P : 6 * P], result[:, 3 * P : 6 * P])
+        last(5, 6)

@@ -24,13 +24,25 @@ FLOPS = 2 * 1536 * 128 * 3840
 FIRST_PIECES = ((0, 512, 512), (512, 512, 256), (1024, 256, 128))
 LATER_PIECES = ((0, 256, 0), (256, 512, 0), (768, 512, 0))
 WEIGHT_PIECES = (4,) * 10 + (2, 2, 1)
-EARLY_GATHER, EARLY_WINDOW, LATE_WINDOW = 1280, 1792, 1408
-SCALE_GATHERS = ((0, 1024, 1), (1024, 1024, 3), (2048, 1024, 5), (3072, 768, 8))
-WORD_GATHERS = ((0, 1024, 2), (1024, 1024, 4), (2048, 1024, 6), (3072, 512, 10), (3584, 256, 11))
+WINDOWS = (1792, 1792, 1408)
+SCALES = 3
+FREE_GATHERS = (((0, 0, 1280), (0, 1280, 1280), (0, 2560, 768)), ((1, 0, 1280), (1, 1280, 1280)), ())
+SPACERS = (None, (0, 3328, 512), (1, 2560, 1280))
+BEHIND_WEIGHTS = {
+    0: (SCALES, 0, 1024),
+    1: (2, 0, 1024),
+    2: (SCALES, 1024, 1024),
+    3: (2, 1024, 1024),
+    5: (SCALES, 2048, 1024),
+    6: (2, 2048, 1024),
+    8: (SCALES, 3072, 768),
+    10: (2, 3072, 512),
+    11: (2, 3584, 256),
+}
 BIAS_PARTS = ((0, 4, 7), (4, 8, 10), (8, 15, 13))
 PAIRED = 12
 BUFFERS = 13
-SCALAR_FROM = (6, 6, 6)
+VECTOR_BLOCKS = 6
 
 
 def tile_moe_tk_lin_bias_kernel(tc, xT, w, b, gate, offs, pos1, pos2, pos3, out):
@@ -40,10 +52,13 @@ def tile_moe_tk_lin_bias_kernel(tc, xT, w, b, gate, offs, pos1, pos2, pos3, out)
     S = offs.shape[1] * STRIPE
     C = S // E
     passes = K // (P * PACK)
+    blocks = T // P
+    scalar_blocks = blocks - VECTOR_BLOCKS
+    vector_tokens = VECTOR_BLOCKS * P
     x_view = xT.rearrange("(a p j) t -> a p j t", p=P, j=PACK)
     w_view = w.rearrange("e (a p j) n -> p (e a) (j n)", p=P, j=PACK)
+    token_pieces = [FIRST_PIECES] + [LATER_PIECES] * (passes - 1)
     weight_pieces = [(sum(WEIGHT_PIECES[:i]), count) for i, count in enumerate(WEIGHT_PIECES)]
-    lenders = sorted(piece for s0, slots, piece in SCALE_GATHERS + WORD_GATHERS)
 
     with ExitStack() as ctx:
         held = ctx.enter_context(tc.tile_pool(name="held", bufs=1))
@@ -51,68 +66,59 @@ def tile_moe_tk_lin_bias_kernel(tc, xT, w, b, gate, offs, pos1, pos2, pos3, out)
         rounds = ctx.enter_context(tc.tile_pool(name="rounds", bufs=8))
         psum = ctx.enter_context(tc.psum_pool(name="psum", bufs=1))
 
+        def bank(number, shape):
+            return psum.tile(shape, F32, tag=f"bank{number}", name="bank")
+
         offs_sb = held.tile([P, S // STRIPE], U16, name="offs_sb")
         pos_sb = [held.tile([P, T // STRIPE], U16, name=f"pos{r}_sb") for r in range(TOP)]
-        windows = [EARLY_WINDOW] * (passes - 1) + [LATE_WINDOW]
-        token_words = [held.tile([P, windows[a]], U32, name=f"token_words{a}", align_bytes=64) for a in range(passes)]
-        token_scales = held.tile([P, LATE_WINDOW], U8, name="token_scales", align_bytes=64)
-        slot_words = [held.tile([P, S], U32, name="slot_words0", align_bytes=64)]
+        windows = [held.tile([P, WINDOWS[a]], U32, name=f"token_words{a}", align_bytes=64) for a in range(passes)]
+        token_scales = held.tile([P, WINDOWS[-1]], U8, name="token_scales", align_bytes=64)
+        windows.append(token_scales)
         y = held.tile([P, S], F32, name="y")
+        gates = held.tile([P, TOP, vector_tokens], F32, name="gates")
+        gate_rows = held.tile([P, P], F32, name="gate_rows", align_bytes=64)
+        gate_columns = held.tile([P, TOP * scalar_blocks], F32, name="gate_columns")
+        ident = held.tile([P, P], F32, name="ident", align_bytes=64)
 
         nc.vector.memset(token_scales[:, :T].bitcast(U32), 0)
-        blocks = T // P
-        turned_terms = [(r, c) for r in range(TOP) for c in range(SCALAR_FROM[r], blocks)]
-        gate_rows = held.tile([P, P], F32, name="gate_rows", align_bytes=64)
-        gate_columns = held.tile([P, len(turned_terms)], F32, name="gate_columns")
         nc.vector.memset(gate_rows[:], 0.0)
+        make_identity(nc, ident[:])
 
         free = [f"buffer{i}" for i in range(BUFFERS)]
+        lent = []
 
         def take(keep=False):
             tag = free.pop(0)
-            if not keep:
-                free.append(tag)
+            (lent if keep else free).append(tag)
             return tag
 
         raw_x = {}
-        raw_w = {}
-        buffer_of = {}
-
-        def load_x(a, pieces):
-            for t0, tokens, on_vector in pieces:
-                raw_x[a, t0] = loads.tile([P, PACK, tokens], F32, tag=take(), name="raw_x", align_bytes=64)
+        spacer_buffer = {}
+        for a in range(passes):
+            for t0, tokens, on_vector in token_pieces[a]:
+                spacer_buffer[a] = take(keep=a > 0 and t0 + tokens == T)
+                raw_x[a, t0] = loads.tile([P, PACK, tokens], F32, tag=spacer_buffer[a], name="raw_x", align_bytes=64)
                 nc.sync.dma_start(raw_x[a, t0][:], x_view[a][:, :, t0 : t0 + tokens])
-
-        def load_w(piece):
-            m0, count = weight_pieces[piece]
-            buffer_of[piece] = take(keep=piece in lenders) if piece else "first_weights"
-            raw_w[piece] = loads.tile([P, count, PACK * N], F32, tag=buffer_of[piece], name="raw_w", align_bytes=64)
-            nc.sync.dma_start(raw_w[piece][:], w_view[:, m0 : m0 + count, :])
-
-        load_x(0, FIRST_PIECES)
-        nc.sync.dma_start(offs_sb[:], offs)
-        load_x(1, LATER_PIECES)
-        load_w(0)
-        load_x(2, LATER_PIECES)
+            if a == 0:
+                nc.sync.dma_start(offs_sb[:], offs)
         for r in range(TOP):
-            row = turned_terms.index((r, SCALAR_FROM[r]))
-            rows = gate_rows[row : row + blocks - SCALAR_FROM[r], :]
-            nc.sync.dma_start(rows, gate[r, 0, SCALAR_FROM[r] * P :].rearrange("(c t) -> c t", t=P))
-        loaded = 1
+            rows = gate_rows[r * scalar_blocks : (r + 1) * scalar_blocks, :]
+            nc.sync.dma_start(rows, gate[r, 0, vector_tokens:].rearrange("(c t) -> c t", t=P))
+        raw_w = {}
+        weight_buffer = {}
         bias = []
-        for e0, e1, before in BIAS_PARTS:
-            for piece in range(loaded, before):
-                load_w(piece)
-            loaded = before
-            part = held.tile([P, e1 - e0], F32, name=f"bias{e0}")
-            nc.sync.dma_start(part[:], b[:, e0:e1])
-            bias.extend(part[:, i : i + 1] for i in range(e1 - e0))
+        for piece, (m0, count) in enumerate(weight_pieces):
+            weight_buffer[piece] = take(keep=piece in BEHIND_WEIGHTS)
+            raw_w[piece] = loads.tile([P, count, PACK * N], F32, tag=weight_buffer[piece], name="raw_w", align_bytes=64)
+            nc.sync.dma_start(raw_w[piece][:], w_view[:, m0 : m0 + count, :])
+            for e0, e1, before in BIAS_PARTS:
+                if before - 1 == piece:
+                    part = held.tile([P, e1 - e0], F32, name=f"bias{e0}")
+                    nc.sync.dma_start(part[:], b[:, e0:e1])
+                    bias.extend(part[:, i : i + 1] for i in range(e1 - e0))
         for pos_tile, pos in zip(pos_sb, (pos1, pos2, pos3)):
             nc.sync.dma_start(pos_tile[:], pos)
-        gates = []
-        for r in range(TOP):
-            gates.append(loads.tile([P, SCALAR_FROM[r] * P], F32, tag=take(keep=True), name="gates", align_bytes=64))
-            nc.sync.dma_start(gates[r][:], gate[r, :, : SCALAR_FROM[r] * P])
+        nc.sync.dma_start(gates[:], gate[:, :, :vector_tokens].rearrange("r p t -> p r t"))
 
         rounded_x = {}
 
@@ -128,15 +134,40 @@ def tile_moe_tk_lin_bias_kernel(tc, xT, w, b, gate, offs, pos1, pos2, pos3, out)
 
         def quantize_tokens(a, t0, c0, c1):
             nc.vector.quantize_mx(
-                out=token_words[a][:, t0 + c0 : t0 + c1].bitcast(FP8X4),
+                out=windows[a][:, t0 + c0 : t0 + c1].bitcast(FP8X4),
                 scales=token_scales[4 * a : P, t0 + c0 : t0 + c1],
                 in_=rounded_x[a, t0][:, c0:c1, :].rearrange("p t j -> p (t j)"),
             )
 
-        def quantize_x(a, pieces):
-            for t0, tokens, on_vector in pieces:
-                round_x(a, t0, tokens, on_vector)
-                quantize_tokens(a, t0, 0, tokens)
+        by_expert = {}
+
+        def gather(sort, s0, slots, pool, tag):
+            dtype = U8 if sort == SCALES else U32
+            gathered = pool.tile([P, slots], dtype, tag=tag, name="gathered", align_bytes=64)
+            nc.vector.tensor_copy(gathered[:], windows[sort][:].indirect(offs_sb[:, s0 // STRIPE : (s0 + slots) // STRIPE]))
+            for e in range(s0 // C, (s0 + slots) // C):
+                by_expert[sort, e] = gathered[:, e * C - s0 : (e + 1) * C - s0]
+
+        first, second, third = FIRST_PIECES
+        round_x(0, *first)
+        quantize_tokens(0, first[0], 0, first[1])
+        round_x(0, *second)
+        quantize_tokens(0, second[0], 0, second[2])
+        round_x(0, *third)
+        quantize_tokens(0, second[0], second[2], second[1])
+        quantize_tokens(0, third[0], 0, third[1])
+        for a in range(passes):
+            if a > 0:
+                for t0, tokens, on_vector in token_pieces[a]:
+                    round_x(a, t0, tokens, on_vector)
+                    quantize_tokens(a, t0, 0, tokens)
+                gather(*SPACERS[a], loads, spacer_buffer[a])
+            for sort, s0, slots in FREE_GATHERS[a]:
+                gather(sort, s0, slots, held, f"words{sort}_{s0}")
+
+        gates_turned = bank(7, [P, P])
+        nc.tensor.transpose(gates_turned[:], gate_rows[:], ident[:])
+        nc.scalar.copy(gate_columns[:], gates_turned[:, : TOP * scalar_blocks])
 
         w_words = []
         w_scales = []
@@ -158,131 +189,66 @@ def tile_moe_tk_lin_bias_kernel(tc, xT, w, b, gate, offs, pos1, pos2, pos3, out)
                 in_=rounded[:].rearrange("p m n j -> p (m n j)"),
             )
 
-        def gather(dst, window, s0, slots):
-            nc.vector.tensor_copy(dst, window[:].indirect(offs_sb[:, s0 // STRIPE : (s0 + slots) // STRIPE]))
-
-        def gather_early(a):
-            for s0 in range(0, S, EARLY_GATHER):
-                gather(slot_words[a][:, s0 : s0 + EARLY_GATHER], token_words[a], s0, EARLY_GATHER)
-
-        ident = held.tile([P, P], F32, name="ident", align_bytes=64)
-        make_identity(nc, ident[:])
-        first, second, third = FIRST_PIECES
-        quantize_x(0, [first])
-        round_x(0, *second)
-        quantize_tokens(0, second[0], 0, second[2])
-        round_x(0, *third)
-        quantize_tokens(0, second[0], second[2], second[1])
-        quantize_tokens(0, third[0], 0, third[1])
-        gather_early(0)
-        quantize_x(1, LATER_PIECES)
-        quantize_w(0)
-        slot_words.append(loads.tile([P, S], U32, tag=buffer_of[0], name="slot_words1", align_bytes=64))
-        gather_early(1)
-        quantize_x(2, LATER_PIECES)
-
-        gates_turned = psum.tile([P, P], F32, tag="bank7", name="gates_turned")
-        nc.tensor.transpose(gates_turned[:], gate_rows[:], ident[:])
-        nc.scalar.copy(gate_columns[:], gates_turned[:, : len(turned_terms)])
-
-        slot_scales = {}
-        last_words = {}
-
-        def gather_late(by_expert, dtype, window, s0, slots, piece):
-            gathered = loads.tile([P, slots], dtype, tag=buffer_of[piece], name="gathered", align_bytes=64)
-            gather(gathered[:], window, s0, slots)
-            for e in range(s0 // C, (s0 + slots) // C):
-                by_expert[e] = gathered[:, e * C - s0 : (e + 1) * C - s0]
-
         products = {}
         passes_done = [0] * E
-        last_half = []
+
+        def open_product(e):
+            if e == E - 1:
+                products[e] = [(bank(i, [P, C // 2])[:], i * C // 2, (i + 1) * C // 2) for i in range(2)]
+            elif e >= PAIRED:
+                products[e] = [(bank(e - PAIRED // 2, [P, C])[:], 0, C)]
+            elif e % 2 == 0:
+                pair_bank = bank(e // 2, [P, 2, C])
+                products[e], products[e + 1] = [(pair_bank[:, 0, :], 0, C)], [(pair_bank[:, 1, :], 0, C)]
 
         def multiply():
             for e in range(E):
                 second_in_bank = e < PAIRED and e % 2 == 1
                 while passes_done[e] < passes:
                     a = passes_done[e]
-                    ready = e in slot_scales and len(w_words) > passes * e + a and (a < passes - 1 or e in last_words)
+                    ready = (SCALES, e) in by_expert and (a, e) in by_expert and len(w_words) > passes * e + a
                     if not ready or (second_in_bank and passes_done[e - 1] < passes):
                         break
-                    if a == 0 and e >= PAIRED:
-                        products[e] = psum.tile([P, C], F32, tag=f"bank{(e - PAIRED // 2) % 8}", name="bank")[:]
-                    elif a == 0 and not second_in_bank:
-                        bank = psum.tile([P, 2, C], F32, tag=f"bank{e // 2}", name="bank")
-                        products[e], products[e + 1] = bank[:, 0, :], bank[:, 1, :]
-                    moving = slot_words[a][:, e * C : (e + 1) * C] if a < passes - 1 else last_words[e]
-                    if a == 0 and e == E - 1:
-                        last_half.append(psum.tile([P, C // 2], F32, tag="bank1", name="bank")[:])
-                    parts = [(products[e], 0, C)]
-                    if e == E - 1:
-                        parts = [(products[e][:, : C // 2], 0, C // 2), (last_half[0], C // 2, C)]
-                    for dst, c0, c1 in parts:
+                    if a == 0:
+                        open_product(e)
+                    for dst, c0, c1 in products[e]:
                         nc.tensor.matmul_mx(
                             out=dst,
                             lhsT=w_words[passes * e + a].bitcast(FP8X4),
                             lhsT_scale=w_scales[passes * e + a],
-                            rhs=moving[:, c0:c1].bitcast(FP8X4),
-                            rhs_scale=slot_scales[e][4 * a : P, c0:c1],
+                            rhs=by_expert[a, e][:, c0:c1].bitcast(FP8X4),
+                            rhs_scale=by_expert[SCALES, e][4 * a : P, c0:c1],
                             start=(a == 0),
                             stop=(a == passes - 1),
                         )
                     passes_done[e] += 1
 
-        for piece in range(1, len(weight_pieces)):
+        for piece in range(len(weight_pieces)):
             quantize_w(piece)
-            for s0, slots, lender in SCALE_GATHERS:
-                if lender == piece:
-                    gather_late(slot_scales, U8, token_scales, s0, slots, piece)
-            multiply()
-            for s0, slots, lender in WORD_GATHERS:
-                if lender == piece:
-                    gather_late(last_words, U32, token_words[passes - 1], s0, slots, piece)
+            if piece in BEHIND_WEIGHTS:
+                gather(*BEHIND_WEIGHTS[piece], loads, weight_buffer[piece])
             multiply()
             for e0, e1, before in BIAS_PARTS:
                 if before - 1 == piece:
                     for e in range(e0, e1):
-                        if e < E - 1:
-                            nc.scalar.activation(y[:, e * C : (e + 1) * C], products[e], IDENTITY, bias=bias[e])
-                        else:
-                            mid = e * C + C // 2
-                            nc.scalar.activation(y[:, e * C : mid], products[e][:, : C // 2], IDENTITY, bias=bias[e])
-                            nc.scalar.activation(y[:, mid:], last_half[0], IDENTITY, bias=bias[e])
+                        for product, c0, c1 in products[e]:
+                            nc.scalar.activation(y[:, e * C + c0 : e * C + c1], product, IDENTITY, bias=bias[e])
 
-        free.extend(buffer_of[piece] for piece in lenders)
+        free.extend(lent)
 
         def entries(r, c0, c1):
             return pos_sb[r][:, c0 * P // STRIPE : c1 * P // STRIPE]
 
         turned = {}
+        weighed = {}
 
-        def fetch(r, c0, c1, bank, tag):
+        def fetch(r, c0, c1, number, tag):
             plain = loads.tile([P, c1 - c0, P], F32, tag=tag, name="plain", align_bytes=64)
             nc.scalar.activation(plain[:].rearrange("p c t -> p (c t)"), y[:].indirect(entries(r, c0, c1)), COPY)
-            tile = psum.tile([P, c1 - c0, P], F32, tag=f"bank{bank}", name="turned")
+            tile = bank(number, [P, c1 - c0, P])
             for c in range(c0, c1):
                 turned[r, c] = tile[:, c - c0, :]
                 nc.tensor.transpose(turned[r, c], plain[:, c - c0, :], ident[:])
-
-        def weigh_turned(r, c, back, start, stop):
-            column = turned_terms.index((r, c))
-            nc.scalar.activation(weighed[r, c], turned[r, c], COPY, scale=gate_columns[:, column : column + 1])
-            nc.tensor.matmul(back, weighed[r, c], ident[:], start=start, stop=stop, is_transpose=True)
-
-        def weigh(r, c0, c1, term):
-            nc.vector.tensor_tensor(term, y[:].indirect(entries(r, c0, c1)), gates[r][:, c0 * P : c1 * P], MULT)
-            return term
-
-        def finish(c0, c1, one, other):
-            nc.vector.tensor_tensor(result[:, c0 * P : c1 * P], one, other, ADD)
-            nc.sync.dma_start(out[:, c0 * P : c1 * P], result[:, c0 * P : c1 * P])
-
-        def hand_out(c0, c1, back, queue):
-            nc.scalar.copy(result[:, c0 * P : c1 * P], back)
-            queue.dma_start(out[:, c0 * P : c1 * P], result[:, c0 * P : c1 * P])
-
-        result = loads.tile([P, T], F32, tag=take(), name="result", align_bytes=64)
-        weighed = {}
 
         def room_for_weighed(c0, c1, tag):
             tile = loads.tile([P, TOP, c1 - c0, P], F32, tag=tag, name="weighed", align_bytes=64)
@@ -290,47 +256,61 @@ def tile_moe_tk_lin_bias_kernel(tc, xT, w, b, gate, offs, pos1, pos2, pos3, out)
                 for c in range(c0, c1):
                     weighed[r, c] = tile[:, r, c - c0, :]
 
-        room_for_weighed(6, 8, take())
+        def weigh_turned(r, c, back):
+            column = r * scalar_blocks + c - VECTOR_BLOCKS
+            nc.scalar.activation(weighed[r, c], turned[r, c], COPY, scale=gate_columns[:, column : column + 1])
+            nc.tensor.matmul(back, weighed[r, c], ident[:], start=(r == 2), stop=(r == 0), is_transpose=True)
+
         ring = [take(keep=True) for i in range(4)]
+        room_for_weighed(6, 7, take())
         fetch(2, 6, 10, 2, ring[0])
         fetch(1, 6, 8, 3, ring[1])
         fetch(0, 6, 8, 4, ring[2])
         fetch(1, 8, 10, 6, ring[3])
-        back6 = psum.tile([P, 2, P], F32, tag="bank1", name="back")
-        for c in (6, 7):
-            for r in (2, 1, 0):
-                weigh_turned(r, c, back6[:, c - 6, :], r == 2, r == 0)
-        fetch(0, 8, 10, 7, ring[2])
-        room_for_weighed(8, 10, ring[3])
-        back8 = psum.tile([P, P], F32, tag="bank0", name="back")
-        back9 = psum.tile([P, P], F32, tag="bank5", name="back")
+        back6 = bank(1, [P, 2, P])
         for r in (2, 1, 0):
-            weigh_turned(r, 8, back8[:], r == 2, r == 0)
-            weigh_turned(r, 9, back9[:], r == 2, r == 0)
+            weigh_turned(r, 6, back6[:, 0, :])
+        fetch(0, 8, 10, 7, ring[2])
+        room_for_weighed(7, 10, ring[3])
+        for r in (2, 1, 0):
+            weigh_turned(r, 7, back6[:, 1, :])
+        back8 = bank(0, [P, P])
+        back9 = bank(5, [P, P])
+        for r in (2, 1, 0):
+            weigh_turned(r, 8, back8[:])
+            weigh_turned(r, 9, back9[:])
+        handed = loads.tile([P, 4 * P], F32, tag=ring[2], name="handed", align_bytes=64)
+        nc.scalar.copy(handed[:, : 2 * P], back6[:].rearrange("p c m -> p (c m)"))
+        nc.scalar.dma_start(out[:, 6 * P : 8 * P], handed[:, : 2 * P])
+        nc.scalar.copy(handed[:, 2 * P : 3 * P], back8[:])
+        nc.scalar.copy(handed[:, 3 * P :], back9[:])
+        nc.scalar.dma_start(out[:, 8 * P :], handed[:, 2 * P :])
 
-        terms01 = loads.tile([P, 2, 6 * P], F32, tag=take(), name="terms01", align_bytes=64)
-        term2 = loads.tile([P, 6 * P], F32, tag=take(), name="term2", align_bytes=64)
-        pair = loads.tile([P, 6 * P], F32, tag=take(), name="pair", align_bytes=64)
+        terms = [loads.tile([P, vector_tokens], F32, tag=take(), name="term", align_bytes=64) for r in range(TOP)]
+        pair = loads.tile([P, vector_tokens], F32, tag=take(), name="pair", align_bytes=64)
+        result = loads.tile([P, vector_tokens], F32, tag=take(), name="result", align_bytes=64)
+
+        def weigh(r, c0, c1):
+            columns = slice(c0 * P, c1 * P)
+            nc.vector.tensor_tensor(terms[r][:, columns], y[:].indirect(entries(r, c0, c1)), gates[:, r, columns], MULT)
 
         def add_pair(c0, c1):
             columns = slice(c0 * P, c1 * P)
-            nc.vector.tensor_tensor(pair[:, columns], terms01[:, 0, columns], terms01[:, 1, columns], ADD)
+            nc.vector.tensor_tensor(pair[:, columns], terms[0][:, columns], terms[1][:, columns], ADD)
 
-        def last(c0, c1):
-            finish(c0, c1, pair[:, c0 * P : c1 * P], term2[:, c0 * P : c1 * P])
+        def finish(c0, c1):
+            columns = slice(c0 * P, c1 * P)
+            nc.vector.tensor_tensor(result[:, columns], pair[:, columns], terms[2][:, columns], ADD)
+            nc.sync.dma_start(out[:, columns], result[:, columns])
 
-        weigh(0, 0, 6, terms01[:, 0, :])
-        weigh(1, 0, 3, terms01[:, 1, : 3 * P])
-        weigh(2, 0, 3, term2[:, : 3 * P])
+        weigh(0, 0, 6)
+        weigh(1, 0, 3)
+        weigh(2, 0, 3)
         add_pair(0, 3)
-        weigh(1, 3, 6, terms01[:, 1, 3 * P :])
-        last(0, 3)
-        hand_out(6, 8, back6[:].rearrange("p c m -> p (c m)"), nc.sync)
+        weigh(1, 3, 6)
+        finish(0, 3)
         add_pair(3, 6)
-        weigh(2, 3, 5, term2[:, 3 * P : 5 * P])
-        weigh(2, 5, 6, term2[:, 5 * P :])
-        last(3, 5)
-        nc.scalar.copy(result[:, 8 * P : 9 * P], back8[:])
-        nc.scalar.copy(result[:, 9 * P :], back9[:])
-        nc.scalar.dma_start(out[:, 8 * P :], result[:, 8 * P :])
-        last(5, 6)
+        weigh(2, 3, 5)
+        weigh(2, 5, 6)
+        finish(3, 5)
+        finish(5, 6)

@@ -21,7 +21,7 @@ STRIPE = 16
 RUN = 4
 FLOPS = 2 * 1536 * 128 * 3840
 
-FIRST_PIECES = ((0, 512, 512), (512, 512, 256), (1024, 256, 128))
+FIRST_PIECES = ((0, 768, 384), (768, 384, 256), (1152, 128, 64))
 LATER_PIECES = ((0, 256, 0), (256, 512, 0), (768, 512, 0))
 WEIGHT_PIECES = (4,) * 10 + (2, 2, 1)
 WINDOWS = (1792, 1792, 1408)
@@ -120,23 +120,19 @@ def tile_moe_tk_lin_bias_kernel(tc, xT, w, b, gate, offs, pos1, pos2, pos3, out)
             nc.sync.dma_start(pos_tile[:], pos)
         nc.sync.dma_start(gates[:], gate[:, :, :vector_tokens].rearrange("r p t -> p r t"))
 
-        rounded_x = {}
+        def room_for_rounded(tokens):
+            return rounds.tile([P, tokens, PACK], BF16, name="rounded", align_bytes=64)[:]
 
-        def round_x(a, t0, tokens, on_vector):
-            rounded_x[a, t0] = rounds.tile([P, tokens, PACK], BF16, name="rounded", align_bytes=64)
-            src = raw_x[a, t0][:].rearrange("p j (c i) -> p c j i", i=RUN)
-            dst = rounded_x[a, t0][:].rearrange("p (c i) j -> p c j i", i=RUN)
-            cut = on_vector // RUN
-            if on_vector:
-                nc.vector.tensor_copy(dst[:, :cut], src[:, :cut])
-            if on_vector < tokens:
-                nc.scalar.copy(dst[:, cut:], src[:, cut:])
+        def round_x(copy, a, t0, c0, c1, rounded):
+            src = raw_x[a, t0][:, :, c0:c1].rearrange("p j (c i) -> p c j i", i=RUN)
+            copy(rounded.rearrange("p (c i) j -> p c j i", i=RUN), src)
+            return (a, t0 + c0, t0 + c1, rounded)
 
-        def quantize_tokens(a, t0, c0, c1):
+        def quantize_tokens(a, t0, t1, rounded):
             nc.vector.quantize_mx(
-                out=windows[a][:, t0 + c0 : t0 + c1].bitcast(FP8X4),
-                scales=token_scales[4 * a : P, t0 + c0 : t0 + c1],
-                in_=rounded_x[a, t0][:, c0:c1, :].rearrange("p t j -> p (t j)"),
+                out=windows[a][:, t0:t1].bitcast(FP8X4),
+                scales=token_scales[4 * a : P, t0:t1],
+                in_=rounded.rearrange("p t j -> p (t j)"),
             )
 
         by_expert = {}
@@ -148,19 +144,32 @@ def tile_moe_tk_lin_bias_kernel(tc, xT, w, b, gate, offs, pos1, pos2, pos3, out)
             for e in range(s0 // C, (s0 + slots) // C):
                 by_expert[sort, e] = gathered[:, e * C - s0 : (e + 1) * C - s0]
 
+        def share(t0, tokens, on_vector):
+            by_vector = round_x(nc.vector.tensor_copy, 0, t0, 0, on_vector, room_for_rounded(on_vector))
+            by_scalar = round_x(nc.scalar.copy, 0, t0, on_vector, tokens, room_for_rounded(tokens - on_vector))
+            return by_vector, by_scalar
+
         first, second, third = FIRST_PIECES
-        round_x(0, *first)
-        quantize_tokens(0, first[0], 0, first[1])
-        round_x(0, *second)
-        quantize_tokens(0, second[0], 0, second[2])
-        round_x(0, *third)
-        quantize_tokens(0, second[0], second[2], second[1])
-        quantize_tokens(0, third[0], 0, third[1])
+        t0, tokens, on_vector = first
+        cut = tokens - P
+        by_vector = round_x(nc.vector.tensor_copy, 0, t0, 0, on_vector, room_for_rounded(on_vector))
+        early = round_x(nc.scalar.copy, 0, t0, on_vector, cut, room_for_rounded(cut - on_vector))
+        late = round_x(nc.scalar.copy, 0, t0, cut, tokens, room_for_rounded(P))
+        quantize_tokens(*early)
+        quantize_tokens(*by_vector)
+        quantize_tokens(*late)
+        by_vector, by_scalar = share(*second)
+        quantize_tokens(*by_scalar)
+        t0, tokens, on_vector = third
+        last = room_for_rounded(tokens)
+        round_x(nc.vector.tensor_copy, 0, t0, 0, on_vector, last[:, :on_vector, :])
+        round_x(nc.scalar.copy, 0, t0, on_vector, tokens, last[:, on_vector:, :])
+        quantize_tokens(*by_vector)
+        quantize_tokens(0, t0, t0 + tokens, last)
         for a in range(passes):
             if a > 0:
                 for t0, tokens, on_vector in token_pieces[a]:
-                    round_x(a, t0, tokens, on_vector)
-                    quantize_tokens(a, t0, 0, tokens)
+                    quantize_tokens(*round_x(nc.scalar.copy, a, t0, 0, tokens, room_for_rounded(tokens)))
                 gather(*SPACERS[a], loads, spacer_buffer[a])
             for sort, s0, slots in FREE_GATHERS[a]:
                 gather(sort, s0, slots, held, f"words{sort}_{s0}")

@@ -43,6 +43,7 @@ BIAS_PARTS = ((0, 4, 7), (4, 8, 10), (8, 15, 13))
 PAIRED = 12
 BUFFERS = 13
 VECTOR_BLOCKS = 6
+FETCHES = ((2, 6, 8), (1, 6, 8), (0, 6, 8), (2, 8, 10), (1, 8, 9), (0, 8, 9), (1, 9, 10), (0, 9, 10))
 
 
 def tile_moe_tk_lin_bias_kernel(tc, xT, w, b, gate, offs, pos1, pos2, pos3, out):
@@ -161,11 +162,11 @@ def tile_moe_tk_lin_bias_kernel(tc, xT, w, b, gate, offs, pos1, pos2, pos3, out)
         by_vector, by_scalar = share(*second)
         quantize_tokens(*by_scalar)
         t0, tokens, on_vector = third
-        last = room_for_rounded(tokens)
-        round_x(nc.vector.tensor_copy, 0, t0, 0, on_vector, last[:, :on_vector, :])
-        round_x(nc.scalar.copy, 0, t0, on_vector, tokens, last[:, on_vector:, :])
+        tail = room_for_rounded(tokens)
+        round_x(nc.vector.tensor_copy, 0, t0, 0, on_vector, tail[:, :on_vector, :])
+        round_x(nc.scalar.copy, 0, t0, on_vector, tokens, tail[:, on_vector:, :])
         quantize_tokens(*by_vector)
-        quantize_tokens(0, t0, t0 + tokens, last)
+        quantize_tokens(0, t0, t0 + tokens, tail)
         for a in range(passes):
             if a > 0:
                 for t0, tokens, on_vector in token_pieces[a]:
@@ -249,51 +250,41 @@ def tile_moe_tk_lin_bias_kernel(tc, xT, w, b, gate, offs, pos1, pos2, pos3, out)
             return pos_sb[r][:, c0 * P // STRIPE : c1 * P // STRIPE]
 
         turned = {}
-        weighed = {}
+        ring = [take(keep=True) for i in range(3)]
+        weighed = loads.tile([P, TOP, scalar_blocks, P], F32, tag=take(), name="weighed", align_bytes=64)
+        back = {c: bank(4 + c - VECTOR_BLOCKS, [P, P]) for c in range(VECTOR_BLOCKS, blocks)}
 
-        def fetch(r, c0, c1, number, tag):
-            plain = loads.tile([P, c1 - c0, P], F32, tag=tag, name="plain", align_bytes=64)
+        def fetch(step):
+            r, c0, c1 = FETCHES[step]
+            plain = loads.tile([P, c1 - c0, P], F32, tag=ring[step % len(ring)], name="plain", align_bytes=64)
             nc.scalar.activation(plain[:].rearrange("p c t -> p (c t)"), y[:].indirect(entries(r, c0, c1)), COPY)
-            tile = bank(number, [P, c1 - c0, P])
+            tile = bank(step % 4, [P, c1 - c0, P])
             for c in range(c0, c1):
                 turned[r, c] = tile[:, c - c0, :]
                 nc.tensor.transpose(turned[r, c], plain[:, c - c0, :], ident[:])
 
-        def room_for_weighed(c0, c1, tag):
-            tile = loads.tile([P, TOP, c1 - c0, P], F32, tag=tag, name="weighed", align_bytes=64)
-            for r in range(TOP):
-                for c in range(c0, c1):
-                    weighed[r, c] = tile[:, r, c - c0, :]
+        def weigh_turned(step):
+            r, c0, c1 = FETCHES[step]
+            for c in range(c0, c1):
+                column = r * scalar_blocks + c - VECTOR_BLOCKS
+                term = weighed[:, r, c - VECTOR_BLOCKS, :]
+                nc.scalar.activation(term, turned[r, c], COPY, scale=gate_columns[:, column : column + 1])
+                nc.tensor.matmul(back[c][:], term, ident[:], start=(r == 2), stop=(r == 0), is_transpose=True)
 
-        def weigh_turned(r, c, back):
-            column = r * scalar_blocks + c - VECTOR_BLOCKS
-            nc.scalar.activation(weighed[r, c], turned[r, c], COPY, scale=gate_columns[:, column : column + 1])
-            nc.tensor.matmul(back, weighed[r, c], ident[:], start=(r == 2), stop=(r == 0), is_transpose=True)
-
-        ring = [take(keep=True) for i in range(4)]
-        room_for_weighed(6, 7, take())
-        fetch(2, 6, 10, 2, ring[0])
-        fetch(1, 6, 8, 3, ring[1])
-        fetch(0, 6, 8, 4, ring[2])
-        fetch(1, 8, 10, 6, ring[3])
-        back6 = bank(1, [P, 2, P])
-        for r in (2, 1, 0):
-            weigh_turned(r, 6, back6[:, 0, :])
-        fetch(0, 8, 10, 7, ring[2])
-        room_for_weighed(7, 10, ring[3])
-        for r in (2, 1, 0):
-            weigh_turned(r, 7, back6[:, 1, :])
-        back8 = bank(0, [P, P])
-        back9 = bank(5, [P, P])
-        for r in (2, 1, 0):
-            weigh_turned(r, 8, back8[:])
-            weigh_turned(r, 9, back9[:])
-        handed = loads.tile([P, 4 * P], F32, tag=ring[2], name="handed", align_bytes=64)
-        nc.scalar.copy(handed[:, : 2 * P], back6[:].rearrange("p c m -> p (c m)"))
-        nc.scalar.dma_start(out[:, 6 * P : 8 * P], handed[:, : 2 * P])
-        nc.scalar.copy(handed[:, 2 * P : 3 * P], back8[:])
-        nc.scalar.copy(handed[:, 3 * P :], back9[:])
-        nc.scalar.dma_start(out[:, 8 * P :], handed[:, 2 * P :])
+        last = len(FETCHES) - 1
+        for step in range(last + len(ring)):
+            if step >= len(ring):
+                weigh_turned(step - len(ring))
+            if step <= last:
+                fetch(step)
+        handed = loads.tile([P, scalar_blocks, P], F32, tag=ring[(last - 1) % len(ring)], name="handed", align_bytes=64)
+        for c in (6, 7):
+            nc.scalar.copy(handed[:, c - VECTOR_BLOCKS, :], back[c][:])
+        weigh_turned(last)
+        nc.scalar.copy(handed[:, 2, :], back[8][:])
+        nc.scalar.dma_start(out[:, 6 * P : 9 * P], handed[:, :3, :].rearrange("p c t -> p (c t)"))
+        nc.scalar.copy(handed[:, 3, :], back[9][:])
+        nc.scalar.dma_start(out[:, 9 * P :], handed[:, 3, :])
 
         terms = [loads.tile([P, vector_tokens], F32, tag=take(), name="term", align_bytes=64) for r in range(TOP)]
         pair = loads.tile([P, vector_tokens], F32, tag=take(), name="pair", align_bytes=64)

@@ -21,10 +21,12 @@ STRIPE = 16
 RUN = 4
 FLOPS = 2 * 1536 * 128 * 3840
 
-FIRST_PIECES = ((0, 768, 384), (768, 384, 256), (1152, 128, 64))
-LATER_PIECES = ((0, 256, 0), (256, 512, 0), (768, 512, 0))
+LOW_ON_VECTOR = 704
+FIRST_UNITS = (256, 512, 256, 256)
+HIGH_PIECES = ((512, 256), (512, 256), (256, 192))
+LATER_PIECES = (256, 512, 512)
 WEIGHT_PIECES = (4,) * 10 + (2, 2, 1)
-WINDOWS = (1792, 1792, 1408)
+WINDOWS = (1792, 1792, 1408, 1408)
 SCALES = 3
 FREE_GATHERS = (((0, 0, 1280), (0, 1280, 1280), (0, 2560, 768)), ((1, 0, 1280), (1, 1280, 1280)), ())
 SPACERS = (None, (0, 3328, 512), (1, 2560, 1280))
@@ -39,11 +41,12 @@ BEHIND_WEIGHTS = {
     10: (2, 3072, 512),
     11: (2, 3584, 256),
 }
-BIAS_PARTS = ((0, 4, 7), (4, 8, 10), (8, 15, 13))
+BIAS_BEHIND = {6: (0, 4), 9: (4, 8), 12: (8, 15)}
 PAIRED = 12
 BUFFERS = 13
 VECTOR_BLOCKS = 6
 FETCHES = ((2, 6, 8), (1, 6, 8), (0, 6, 8), (2, 8, 10), (1, 8, 9), (0, 8, 9), (1, 9, 10), (0, 9, 10))
+LAG = 3
 
 
 def tile_moe_tk_lin_bias_kernel(tc, xT, w, b, gate, offs, pos1, pos2, pos3, out):
@@ -58,8 +61,9 @@ def tile_moe_tk_lin_bias_kernel(tc, xT, w, b, gate, offs, pos1, pos2, pos3, out)
     vector_tokens = VECTOR_BLOCKS * P
     x_view = xT.rearrange("(a p j) t -> a p j t", p=P, j=PACK)
     w_view = w.rearrange("e (a p j) n -> p (e a) (j n)", p=P, j=PACK)
-    token_pieces = [FIRST_PIECES] + [LATER_PIECES] * (passes - 1)
-    weight_pieces = [(sum(WEIGHT_PIECES[:i]), count) for i, count in enumerate(WEIGHT_PIECES)]
+
+    def spans(widths):
+        return [(sum(widths[:i]), width) for i, width in enumerate(widths)]
 
     with ExitStack() as ctx:
         held = ctx.enter_context(tc.tile_pool(name="held", bufs=1))
@@ -73,10 +77,8 @@ def tile_moe_tk_lin_bias_kernel(tc, xT, w, b, gate, offs, pos1, pos2, pos3, out)
         offs_sb = held.tile([P, S // STRIPE], U16, name="offs_sb")
         pos_sb = [held.tile([P, T // STRIPE], U16, name=f"pos{r}_sb") for r in range(TOP)]
         windows = [held.tile([P, WINDOWS[a]], U32, name=f"token_words{a}", align_bytes=64) for a in range(passes)]
-        token_scales = held.tile([P, WINDOWS[-1]], U8, name="token_scales", align_bytes=64)
+        token_scales = held.tile([P, WINDOWS[SCALES]], U8, name="token_scales", align_bytes=64)
         windows.append(token_scales)
-        y = held.tile([P, S], F32, name="y")
-        gates = held.tile([P, TOP, vector_tokens], F32, name="gates")
         gate_rows = held.tile([P, P], F32, name="gate_rows", align_bytes=64)
         gate_columns = held.tile([P, TOP * scalar_blocks], F32, name="gate_columns")
         ident = held.tile([P, P], F32, name="ident", align_bytes=64)
@@ -93,46 +95,11 @@ def tile_moe_tk_lin_bias_kernel(tc, xT, w, b, gate, offs, pos1, pos2, pos3, out)
             (lent if keep else free).append(tag)
             return tag
 
-        raw_x = {}
-        spacer_buffer = {}
-        for a in range(passes):
-            for t0, tokens, on_vector in token_pieces[a]:
-                spacer_buffer[a] = take(keep=a > 0 and t0 + tokens == T)
-                raw_x[a, t0] = loads.tile([P, PACK, tokens], F32, tag=spacer_buffer[a], name="raw_x", align_bytes=64)
-                nc.sync.dma_start(raw_x[a, t0][:], x_view[a][:, :, t0 : t0 + tokens])
-            if a == 0:
-                nc.sync.dma_start(offs_sb[:], offs)
-        for r in range(TOP):
-            rows = gate_rows[r * scalar_blocks : (r + 1) * scalar_blocks, :]
-            nc.sync.dma_start(rows, gate[r, 0, vector_tokens:].rearrange("(c t) -> c t", t=P))
-        raw_w = {}
-        weight_buffer = {}
-        bias = []
-        for piece, (m0, count) in enumerate(weight_pieces):
-            weight_buffer[piece] = take(keep=piece in BEHIND_WEIGHTS)
-            raw_w[piece] = loads.tile([P, count, PACK * N], F32, tag=weight_buffer[piece], name="raw_w", align_bytes=64)
-            nc.sync.dma_start(raw_w[piece][:], w_view[:, m0 : m0 + count, :])
-            for e0, e1, before in BIAS_PARTS:
-                if before - 1 == piece:
-                    part = held.tile([P, e1 - e0], F32, name=f"bias{e0}")
-                    nc.sync.dma_start(part[:], b[:, e0:e1])
-                    bias.extend(part[:, i : i + 1] for i in range(e1 - e0))
-        for pos_tile, pos in zip(pos_sb, (pos1, pos2, pos3)):
-            nc.sync.dma_start(pos_tile[:], pos)
-        nc.sync.dma_start(gates[:], gate[:, :, :vector_tokens].rearrange("r p t -> p r t"))
-
-        def room_for_rounded(tokens):
-            return rounds.tile([P, tokens, PACK], BF16, name="rounded", align_bytes=64)[:]
-
-        def round_x(copy, a, t0, c0, c1, rounded):
-            src = raw_x[a, t0][:, :, c0:c1].rearrange("p j (c i) -> p c j i", i=RUN)
-            copy(rounded.rearrange("p (c i) j -> p c j i", i=RUN), src)
-            return (a, t0 + c0, t0 + c1, rounded)
-
-        def quantize_tokens(a, t0, t1, rounded):
+        def quantize_tokens(a, t0, rounded):
+            columns = slice(t0, t0 + rounded.shape[1])
             nc.vector.quantize_mx(
-                out=windows[a][:, t0:t1].bitcast(FP8X4),
-                scales=token_scales[4 * a : P, t0:t1],
+                out=windows[a][:, columns].bitcast(FP8X4),
+                scales=token_scales[4 * a : P, columns],
                 in_=rounded.rearrange("p t j -> p (t j)"),
             )
 
@@ -145,32 +112,51 @@ def tile_moe_tk_lin_bias_kernel(tc, xT, w, b, gate, offs, pos1, pos2, pos3, out)
             for e in range(s0 // C, (s0 + slots) // C):
                 by_expert[sort, e] = gathered[:, e * C - s0 : (e + 1) * C - s0]
 
-        def share(t0, tokens, on_vector):
-            by_vector = round_x(nc.vector.tensor_copy, 0, t0, 0, on_vector, room_for_rounded(on_vector))
-            by_scalar = round_x(nc.scalar.copy, 0, t0, on_vector, tokens, room_for_rounded(tokens - on_vector))
-            return by_vector, by_scalar
+        low = held.tile([P, 2, T], F32, tag="y", name="low", align_bytes=64)
+        nc.sync.dma_start(low[:], x_view[0][:, 0:2, :])
+        high = []
+        for t0, tokens in spans([tokens for tokens, on_vector in HIGH_PIECES]):
+            raw = loads.tile([P, 2, tokens], F32, tag=take(), name="high", align_bytes=64)
+            nc.sync.dma_start(raw[:], x_view[0][:, 2:4, t0 : t0 + tokens])
+            high.append((t0, raw))
+        nc.sync.dma_start(offs_sb[:], offs)
+        raw_x = {}
+        spacer_buffer = {}
+        for a in range(1, passes):
+            for t0, tokens in spans(LATER_PIECES):
+                spacer_buffer[a] = take(keep=t0 + tokens == T)
+                raw_x[a, t0] = loads.tile([P, PACK, tokens], F32, tag=spacer_buffer[a], name="raw_x", align_bytes=64)
+                nc.sync.dma_start(raw_x[a, t0][:], x_view[a][:, :, t0 : t0 + tokens])
+        for r in range(TOP):
+            rows = gate_rows[r * scalar_blocks : (r + 1) * scalar_blocks, :]
+            nc.sync.dma_start(rows, gate[r, 0, vector_tokens:].rearrange("(c t) -> c t", t=P))
 
-        first, second, third = FIRST_PIECES
-        t0, tokens, on_vector = first
-        cut = tokens - P
-        by_vector = round_x(nc.vector.tensor_copy, 0, t0, 0, on_vector, room_for_rounded(on_vector))
-        early = round_x(nc.scalar.copy, 0, t0, on_vector, cut, room_for_rounded(cut - on_vector))
-        late = round_x(nc.scalar.copy, 0, t0, cut, tokens, room_for_rounded(P))
-        quantize_tokens(*early)
-        quantize_tokens(*by_vector)
-        quantize_tokens(*late)
-        by_vector, by_scalar = share(*second)
-        quantize_tokens(*by_scalar)
-        t0, tokens, on_vector = third
-        tail = room_for_rounded(tokens)
-        round_x(nc.vector.tensor_copy, 0, t0, 0, on_vector, tail[:, :on_vector, :])
-        round_x(nc.scalar.copy, 0, t0, on_vector, tokens, tail[:, on_vector:, :])
-        quantize_tokens(*by_vector)
-        quantize_tokens(0, t0, t0 + tokens, tail)
+        first = held.tile([P, T, PACK], BF16, tag="gates", name="first", align_bytes=64)
+
+        def round_half(copy, half, t0, src):
+            dst = first[:, t0 : t0 + src.shape[2], 2 * half : 2 * half + 2]
+            copy(dst.rearrange("p (c i) e -> p c e i", i=RUN), src.rearrange("p e (c i) -> p c e i", i=RUN))
+
+        round_half(nc.vector.tensor_copy, 0, 0, low[:, :, :LOW_ON_VECTOR])
+        round_half(nc.scalar.copy, 0, LOW_ON_VECTOR, low[:, :, LOW_ON_VECTOR:])
+        units = spans(FIRST_UNITS)
+        for (t0, raw), (tokens, on_vector) in zip(high, HIGH_PIECES):
+            round_half(nc.vector.tensor_copy, 1, t0, raw[:, :, :on_vector])
+            round_half(nc.scalar.copy, 1, t0 + on_vector, raw[:, :, on_vector:])
+            if t0 == 0:
+                quantize_tokens(0, 0, first[:, : units[0][1], :])
+        for t0, tokens in units[1:]:
+            quantize_tokens(0, t0, first[:, t0 : t0 + tokens, :])
+
+        def interleave(dst, src):
+            nc.scalar.copy(dst.rearrange("p m (c i) j -> p m c j i", i=RUN), src.rearrange("p m j (c i) -> p m c j i", i=RUN))
+
         for a in range(passes):
             if a > 0:
-                for t0, tokens, on_vector in token_pieces[a]:
-                    quantize_tokens(*round_x(nc.scalar.copy, a, t0, 0, tokens, room_for_rounded(tokens)))
+                for t0, tokens in spans(LATER_PIECES):
+                    rounded = rounds.tile([P, 1, tokens, PACK], BF16, name="rounded", align_bytes=64)
+                    interleave(rounded[:], raw_x[a, t0][:].unsqueeze(1))
+                    quantize_tokens(a, t0, rounded[:, 0])
                 gather(*SPACERS[a], loads, spacer_buffer[a])
             for sort, s0, slots in FREE_GATHERS[a]:
                 gather(sort, s0, slots, held, f"words{sort}_{s0}")
@@ -179,26 +165,9 @@ def tile_moe_tk_lin_bias_kernel(tc, xT, w, b, gate, offs, pos1, pos2, pos3, out)
         nc.tensor.transpose(gates_turned[:], gate_rows[:], ident[:])
         nc.scalar.copy(gate_columns[:], gates_turned[:, : TOP * scalar_blocks])
 
+        y = held.tile([P, S], F32, tag="y", name="y", align_bytes=64)
         w_words = []
         w_scales = []
-
-        def quantize_w(piece):
-            m0, count = weight_pieces[piece]
-            rounded = rounds.tile([P, count, N, PACK], BF16, name="rounded", align_bytes=64)
-            words = held.tile([P, count, N], U32, name=f"w_words{m0}", align_bytes=64)
-            scales = held.tile([P, count, N], U8, name=f"w_scales{m0}", align_bytes=64)
-            w_words.extend(words[:, i, :] for i in range(count))
-            w_scales.extend(scales[:, i, :] for i in range(count))
-            nc.scalar.copy(
-                rounded[:].rearrange("p m (c i) j -> p m c j i", i=RUN),
-                raw_w[piece][:].rearrange("p m (j c i) -> p m c j i", j=PACK, i=RUN),
-            )
-            nc.vector.quantize_mx(
-                out=words[:].rearrange("p m n -> p (m n)").bitcast(FP8X4),
-                scales=scales[:].rearrange("p m n -> p (m n)"),
-                in_=rounded[:].rearrange("p m n j -> p (m n j)"),
-            )
-
         products = {}
         passes_done = [0] * E
 
@@ -233,16 +202,36 @@ def tile_moe_tk_lin_bias_kernel(tc, xT, w, b, gate, offs, pos1, pos2, pos3, out)
                         )
                     passes_done[e] += 1
 
-        for piece in range(len(weight_pieces)):
-            quantize_w(piece)
+        for piece, (m0, count) in enumerate(spans(WEIGHT_PIECES)):
+            buffer = take(keep=piece in BEHIND_WEIGHTS)
+            raw = loads.tile([P, count, PACK, N], F32, tag=buffer, name="raw_w", align_bytes=64)
+            nc.sync.dma_start(raw[:].rearrange("p m j n -> p m (j n)"), w_view[:, m0 : m0 + count, :])
+            rounded = rounds.tile([P, count, N, PACK], BF16, name="rounded", align_bytes=64)
+            words = held.tile([P, count, N], U32, name=f"w_words{m0}", align_bytes=64)
+            scales = held.tile([P, count, N], U8, name=f"w_scales{m0}", align_bytes=64)
+            w_words.extend(words[:, i, :] for i in range(count))
+            w_scales.extend(scales[:, i, :] for i in range(count))
+            interleave(rounded[:], raw[:])
+            nc.vector.quantize_mx(
+                out=words[:].rearrange("p m n -> p (m n)").bitcast(FP8X4),
+                scales=scales[:].rearrange("p m n -> p (m n)"),
+                in_=rounded[:].rearrange("p m n j -> p (m n j)"),
+            )
             if piece in BEHIND_WEIGHTS:
-                gather(*BEHIND_WEIGHTS[piece], loads, weight_buffer[piece])
+                gather(*BEHIND_WEIGHTS[piece], loads, buffer)
             multiply()
-            for e0, e1, before in BIAS_PARTS:
-                if before - 1 == piece:
-                    for e in range(e0, e1):
-                        for product, c0, c1 in products[e]:
-                            nc.scalar.activation(y[:, e * C + c0 : e * C + c1], product, IDENTITY, bias=bias[e])
+            if piece in BIAS_BEHIND:
+                e0, e1 = BIAS_BEHIND[piece]
+                bias = held.tile([P, e1 - e0], F32, name=f"bias{e0}")
+                nc.sync.dma_start(bias[:], b[:, e0:e1])
+                for e in range(e0, e1):
+                    for product, c0, c1 in products[e]:
+                        nc.scalar.activation(y[:, e * C + c0 : e * C + c1], product, IDENTITY, bias=bias[:, e - e0 : e - e0 + 1])
+
+        for pos_tile, pos in zip(pos_sb, (pos1, pos2, pos3)):
+            nc.sync.dma_start(pos_tile[:], pos)
+        gates = held.tile([P, TOP, vector_tokens], F32, tag="gates", name="gates", align_bytes=64)
+        nc.sync.dma_start(gates[:], gate[:, :, :vector_tokens].rearrange("r p t -> p r t"))
 
         free.extend(lent)
 
@@ -250,13 +239,13 @@ def tile_moe_tk_lin_bias_kernel(tc, xT, w, b, gate, offs, pos1, pos2, pos3, out)
             return pos_sb[r][:, c0 * P // STRIPE : c1 * P // STRIPE]
 
         turned = {}
-        ring = [take(keep=True) for i in range(3)]
+        ring = [take(keep=True) for i in range(LAG)]
         weighed = loads.tile([P, TOP, scalar_blocks, P], F32, tag=take(), name="weighed", align_bytes=64)
         back = {c: bank(4 + c - VECTOR_BLOCKS, [P, P]) for c in range(VECTOR_BLOCKS, blocks)}
 
         def fetch(step):
             r, c0, c1 = FETCHES[step]
-            plain = loads.tile([P, c1 - c0, P], F32, tag=ring[step % len(ring)], name="plain", align_bytes=64)
+            plain = loads.tile([P, c1 - c0, P], F32, tag=ring[step % LAG], name="plain", align_bytes=64)
             nc.scalar.activation(plain[:].rearrange("p c t -> p (c t)"), y[:].indirect(entries(r, c0, c1)), COPY)
             tile = bank(step % 4, [P, c1 - c0, P])
             for c in range(c0, c1):
@@ -272,12 +261,12 @@ def tile_moe_tk_lin_bias_kernel(tc, xT, w, b, gate, offs, pos1, pos2, pos3, out)
                 nc.tensor.matmul(back[c][:], term, ident[:], start=(r == 2), stop=(r == 0), is_transpose=True)
 
         last = len(FETCHES) - 1
-        for step in range(last + len(ring)):
-            if step >= len(ring):
-                weigh_turned(step - len(ring))
+        for step in range(last + LAG):
+            if step >= LAG:
+                weigh_turned(step - LAG)
             if step <= last:
                 fetch(step)
-        handed = loads.tile([P, scalar_blocks, P], F32, tag=ring[(last - 1) % len(ring)], name="handed", align_bytes=64)
+        handed = loads.tile([P, scalar_blocks, P], F32, tag=ring[(last - 1) % LAG], name="handed", align_bytes=64)
         for c in (6, 7):
             nc.scalar.copy(handed[:, c - VECTOR_BLOCKS, :], back[c][:])
         weigh_turned(last)

@@ -21,29 +21,13 @@ STRIPE = 16
 RUN = 4
 FLOPS = 2 * 1536 * 128 * 3840
 
+BERTH = 8192
 LOW_ON_VECTOR = 704
 FIRST_UNITS = (256, 512, 256, 256)
 HIGH_PIECES = ((512, 256), (512, 256), (256, 192))
-LATER_PIECES = (256, 512, 512)
-WEIGHT_PIECES = (4,) * 10 + (2, 2, 1)
-WINDOWS = (1792, 1792, 1408, 1408)
+PLANE = (4, 0, 8)
 SCALES = 3
-FREE_GATHERS = (((0, 0, 1280), (0, 1280, 1280), (0, 2560, 768)), ((1, 0, 1280), (1, 1280, 1280)), ())
-SPACERS = (None, (0, 3328, 512), (1, 2560, 1280))
-BEHIND_WEIGHTS = {
-    0: (SCALES, 0, 1024),
-    1: (2, 0, 1024),
-    2: (SCALES, 1024, 1024),
-    3: (2, 1024, 1024),
-    5: (SCALES, 2048, 1024),
-    6: (2, 2048, 1024),
-    8: (SCALES, 3072, 768),
-    10: (2, 3072, 512),
-    11: (2, 3584, 256),
-}
-BIAS_BEHIND = {6: (0, 4), 9: (4, 8), 12: (8, 15)}
-PAIRED = 12
-BUFFERS = 13
+SCALE_WINDOW = 1792
 VECTOR_BLOCKS = 6
 FETCHES = ((2, 6, 8), (1, 6, 8), (0, 6, 8), (2, 8, 10), (1, 8, 9), (0, 8, 9), (1, 9, 10), (0, 9, 10))
 LAG = 3
@@ -67,18 +51,20 @@ def tile_moe_tk_lin_bias_kernel(tc, xT, w, b, gate, offs, pos1, pos2, pos3, out)
 
     with ExitStack() as ctx:
         held = ctx.enter_context(tc.tile_pool(name="held", bufs=1))
-        loads = ctx.enter_context(tc.tile_pool(name="loads", bufs=1))
-        rounds = ctx.enter_context(tc.tile_pool(name="rounds", bufs=8))
+        quay = ctx.enter_context(tc.tile_pool(name="quay", bufs=1))
+        rounds = ctx.enter_context(tc.tile_pool(name="rounds", bufs=1))
         psum = ctx.enter_context(tc.psum_pool(name="psum", bufs=1))
 
         def bank(number, shape):
             return psum.tile(shape, F32, tag=f"bank{number}", name="bank")
 
+        def berth(pool, name, shape, dtype, number, byte=0):
+            return pool.tile(shape, dtype, name=name, align_bytes=64, offset=number * BERTH + byte)
+
         offs_sb = held.tile([P, S // STRIPE], U16, name="offs_sb")
         pos_sb = [held.tile([P, T // STRIPE], U16, name=f"pos{r}_sb") for r in range(TOP)]
-        windows = [held.tile([P, WINDOWS[a]], U32, name=f"token_words{a}", align_bytes=64) for a in range(passes)]
-        token_scales = held.tile([P, WINDOWS[SCALES]], U8, name="token_scales", align_bytes=64)
-        windows.append(token_scales)
+        token_words = held.tile([P, (passes - 1) * T + S], U32, name="token_words", align_bytes=64)
+        token_scales = held.tile([P, SCALE_WINDOW], U8, name="token_scales", align_bytes=64)
         gate_rows = held.tile([P, P], F32, name="gate_rows", align_bytes=64)
         gate_columns = held.tile([P, TOP * scalar_blocks], F32, name="gate_columns")
         ident = held.tile([P, P], F32, name="ident", align_bytes=64)
@@ -87,46 +73,48 @@ def tile_moe_tk_lin_bias_kernel(tc, xT, w, b, gate, offs, pos1, pos2, pos3, out)
         nc.vector.memset(gate_rows[:], 0.0)
         make_identity(nc, ident[:])
 
-        free = [f"buffer{i}" for i in range(BUFFERS)]
-        lent = []
-
-        def take(keep=False):
-            tag = free.pop(0)
-            (lent if keep else free).append(tag)
-            return tag
-
         def quantize_tokens(a, t0, rounded):
-            columns = slice(t0, t0 + rounded.shape[1])
+            tokens = rounded.shape[1]
+            first_word = (passes - 1 - a) * T + t0
             nc.vector.quantize_mx(
-                out=windows[a][:, columns].bitcast(FP8X4),
-                scales=token_scales[4 * a : P, columns],
+                out=token_words[:, first_word : first_word + tokens].bitcast(FP8X4),
+                scales=token_scales[PLANE[a] : P, t0 : t0 + tokens],
                 in_=rounded.rearrange("p t j -> p (t j)"),
             )
 
         by_expert = {}
 
-        def gather(sort, s0, slots, pool, tag):
+        def gather(sort, s0, slots, number=None, byte=0):
+            name = f"gathered{sort}_{s0}"
             dtype = U8 if sort == SCALES else U32
-            gathered = pool.tile([P, slots], dtype, tag=tag, name="gathered", align_bytes=64)
-            nc.vector.tensor_copy(gathered[:], windows[sort][:].indirect(offs_sb[:, s0 // STRIPE : (s0 + slots) // STRIPE]))
-            for e in range(s0 // C, (s0 + slots) // C):
-                by_expert[sort, e] = gathered[:, e * C - s0 : (e + 1) * C - s0]
+            if number is None:
+                gathered = held.tile([P, slots], dtype, name=name, align_bytes=64)
+            else:
+                gathered = berth(quay, name, [P, slots], dtype, number, byte)
+            if sort == SCALES:
+                window = token_scales[:]
+            else:
+                first_word = (passes - 1 - sort) * T
+                window = token_words[:, first_word : first_word + (S if slots > T else SCALE_WINDOW)]
+            nc.vector.tensor_copy(gathered[:], window.indirect(offs_sb[:, s0 // STRIPE : (s0 + slots) // STRIPE]))
+            for h in range(s0 // P, (s0 + slots) // P):
+                by_expert[sort, h] = (gathered, s0)
+
+        def interleave(dst, src):
+            nc.scalar.copy(dst.rearrange("p m (c i) j -> p m c j i", i=RUN), src.rearrange("p m j (c i) -> p m c j i", i=RUN))
 
         low = held.tile([P, 2, T], F32, tag="y", name="low", align_bytes=64)
         nc.sync.dma_start(low[:], x_view[0][:, 0:2, :])
         high = []
-        for t0, tokens in spans([tokens for tokens, on_vector in HIGH_PIECES]):
-            raw = loads.tile([P, 2, tokens], F32, tag=take(), name="high", align_bytes=64)
+        for i, (t0, tokens) in enumerate(spans([tokens for tokens, on_vector in HIGH_PIECES])):
+            raw = berth(quay, f"high{i}", [P, 2, tokens], F32, 0, i * BERTH // 2)
             nc.sync.dma_start(raw[:], x_view[0][:, 2:4, t0 : t0 + tokens])
             high.append((t0, raw))
         nc.sync.dma_start(offs_sb[:], offs)
-        raw_x = {}
-        spacer_buffer = {}
-        for a in range(1, passes):
-            for t0, tokens in spans(LATER_PIECES):
-                spacer_buffer[a] = take(keep=t0 + tokens == T)
-                raw_x[a, t0] = loads.tile([P, PACK, tokens], F32, tag=spacer_buffer[a], name="raw_x", align_bytes=64)
-                nc.sync.dma_start(raw_x[a, t0][:], x_view[a][:, :, t0 : t0 + tokens])
+        later = {}
+        for a, t0, tokens, number, byte in ((1, 0, 512, 2, 0), (1, 512, 768, 3, 0), (2, 0, 256, 1, 2048), (2, 256, 512, 5, 0), (2, 768, 512, 6, 0)):
+            later[a, t0] = berth(quay, f"x{a}_{t0}", [P, 1, PACK, tokens], F32, number, byte)
+            nc.sync.dma_start(later[a, t0][:, 0], x_view[a][:, :, t0 : t0 + tokens])
         for r in range(TOP):
             rows = gate_rows[r * scalar_blocks : (r + 1) * scalar_blocks, :]
             nc.sync.dma_start(rows, gate[r, 0, vector_tokens:].rearrange("(c t) -> c t", t=P))
@@ -147,105 +135,155 @@ def tile_moe_tk_lin_bias_kernel(tc, xT, w, b, gate, offs, pos1, pos2, pos3, out)
                 quantize_tokens(0, 0, first[:, : units[0][1], :])
         for t0, tokens in units[1:]:
             quantize_tokens(0, t0, first[:, t0 : t0 + tokens, :])
+        gather(0, 0, S // 2)
+        gather(0, S // 2, S // 2)
 
-        def interleave(dst, src):
-            nc.scalar.copy(dst.rearrange("p m (c i) j -> p m c j i", i=RUN), src.rearrange("p m j (c i) -> p m c j i", i=RUN))
+        second = held.tile([P, 1, T, PACK], BF16, tag="gates", name="second", align_bytes=64)
+        for t0, tokens in ((0, 512), (512, 768)):
+            interleave(second[:, :, t0 : t0 + tokens, :], later[1, t0][:])
+        for t0, tokens in ((0, 1024), (1024, 256)):
+            quantize_tokens(1, t0, second[:, 0, t0 : t0 + tokens, :])
 
-        for a in range(passes):
-            if a > 0:
-                for t0, tokens in spans(LATER_PIECES):
-                    rounded = rounds.tile([P, 1, tokens, PACK], BF16, name="rounded", align_bytes=64)
-                    interleave(rounded[:], raw_x[a, t0][:].unsqueeze(1))
-                    quantize_tokens(a, t0, rounded[:, 0])
-                gather(*SPACERS[a], loads, spacer_buffer[a])
-            for sort, s0, slots in FREE_GATHERS[a]:
-                gather(sort, s0, slots, held, f"words{sort}_{s0}")
+        for t0, tokens, number, byte in ((0, 256, 0, 0), (256, 512, 1, 0), (768, 512, 1, BERTH // 2)):
+            rounded = berth(rounds, f"third{t0}", [P, 1, tokens, PACK], BF16, number, byte)
+            interleave(rounded[:], later[2, t0][:])
+            quantize_tokens(2, t0, rounded[:, 0])
+            if t0 == 0:
+                gather(1, 0, S // 2, 1)
+        gather(1, S // 2, 640, 6)
+        gather(SCALES, 0, T)
 
         gates_turned = bank(7, [P, P])
         nc.tensor.transpose(gates_turned[:], gate_rows[:], ident[:])
         nc.scalar.copy(gate_columns[:], gates_turned[:, : TOP * scalar_blocks])
 
         y = held.tile([P, S], F32, tag="y", name="y", align_bytes=64)
-        w_words = []
-        w_scales = []
+        matrices = {}
         products = {}
         passes_done = [0] * E
+        pair_bank = {0: 0, 2: 1, 5: 3, 8: 5, 10: 6}
+        paired = [e + 1 for e in pair_bank]
+        bias = {}
 
         def open_product(e):
             if e == E - 1:
-                products[e] = [(bank(i, [P, C // 2])[:], i * C // 2, (i + 1) * C // 2) for i in range(2)]
-            elif e >= PAIRED:
-                products[e] = [(bank(e - PAIRED // 2, [P, C])[:], 0, C)]
-            elif e % 2 == 0:
-                pair_bank = bank(e // 2, [P, 2, C])
-                products[e], products[e + 1] = [(pair_bank[:, 0, :], 0, C)], [(pair_bank[:, 1, :], 0, C)]
+                products[e] = [(bank(number, [P, C // 2])[:], i * C // 2, (i + 1) * C // 2) for i, number in enumerate((0, 1))]
+            elif e in pair_bank:
+                both = bank(pair_bank[e], [P, 2, C])
+                products[e], products[e + 1] = [(both[:, 0, :], 0, C)], [(both[:, 1, :], 0, C)]
+            elif e not in paired:
+                products[e] = [(bank({4: 2, 7: 4, 12: 2, 13: 7}[e], [P, C])[:], 0, C)]
+
+        def operand(sort, s0, s1):
+            gathered, base = by_expert[sort, s0 // P]
+            return gathered, s0 - base, s1 - base
 
         def multiply():
             for e in range(E):
-                second_in_bank = e < PAIRED and e % 2 == 1
                 while passes_done[e] < passes:
                     a = passes_done[e]
-                    ready = (SCALES, e) in by_expert and (a, e) in by_expert and len(w_words) > passes * e + a
-                    if not ready or (second_in_bank and passes_done[e - 1] < passes):
+                    halves = (2 * e, 2 * e + 1)
+                    ready = all((sort, h) in by_expert for sort in (SCALES, a) for h in halves) and passes * e + a in matrices
+                    if not ready or (e in paired and passes_done[e - 1] < passes):
                         break
                     if a == 0:
                         open_product(e)
+                    words, scales = matrices[passes * e + a]
                     for dst, c0, c1 in products[e]:
-                        nc.tensor.matmul_mx(
-                            out=dst,
-                            lhsT=w_words[passes * e + a].bitcast(FP8X4),
-                            lhsT_scale=w_scales[passes * e + a],
-                            rhs=by_expert[a, e][:, c0:c1].bitcast(FP8X4),
-                            rhs_scale=by_expert[SCALES, e][4 * a : P, c0:c1],
-                            start=(a == 0),
-                            stop=(a == passes - 1),
-                        )
+                        cut = [c0, c1]
+                        if by_expert[a, halves[0]][1] != by_expert[a, halves[1]][1]:
+                            cut = [c0, (c0 + c1) // 2, c1]
+                        for d0, d1 in zip(cut, cut[1:]):
+                            slot_words, w0, w1 = operand(a, e * C + d0, e * C + d1)
+                            slot_scales, b0, b1 = operand(SCALES, e * C + d0, e * C + d1)
+                            nc.tensor.matmul_mx(
+                                out=dst[:, d0 - c0 : d1 - c0],
+                                lhsT=words.bitcast(FP8X4),
+                                lhsT_scale=scales,
+                                rhs=slot_words[:, w0:w1].bitcast(FP8X4),
+                                rhs_scale=slot_scales[PLANE[a] : P, b0:b1],
+                                start=(a == 0 and d0 == c0),
+                                stop=(a == passes - 1 and d1 == c1),
+                            )
                     passes_done[e] += 1
 
-        for piece, (m0, count) in enumerate(spans(WEIGHT_PIECES)):
-            buffer = take(keep=piece in BEHIND_WEIGHTS)
-            raw = loads.tile([P, count, PACK, N], F32, tag=buffer, name="raw_w", align_bytes=64)
+        def empty_on_scalar(e):
+            for product, c0, c1 in products[e]:
+                nc.scalar.activation(y[:, e * C + c0 : e * C + c1], product, IDENTITY, bias=bias[e])
+
+        def round_weights(m0, count, number, byte, dst):
+            raw = berth(quay, f"w{m0}", [P, count, PACK, N], F32, number, byte)
             nc.sync.dma_start(raw[:].rearrange("p m j n -> p m (j n)"), w_view[:, m0 : m0 + count, :])
-            rounded = rounds.tile([P, count, N, PACK], BF16, name="rounded", align_bytes=64)
+            if m0 in bias_behind:
+                e0, e1 = bias_behind[m0]
+                columns = held.tile([P, e1 - e0], F32, name=f"bias{e0}")
+                nc.sync.dma_start(columns[:], b[:, e0:e1])
+                for e in range(e0, e1):
+                    bias[e] = columns[:, e - e0 : e - e0 + 1]
+            interleave(dst, raw[:])
+
+        def quantize_weights(m0, rounded):
+            count = rounded.shape[1]
             words = held.tile([P, count, N], U32, name=f"w_words{m0}", align_bytes=64)
             scales = held.tile([P, count, N], U8, name=f"w_scales{m0}", align_bytes=64)
-            w_words.extend(words[:, i, :] for i in range(count))
-            w_scales.extend(scales[:, i, :] for i in range(count))
-            interleave(rounded[:], raw[:])
             nc.vector.quantize_mx(
                 out=words[:].rearrange("p m n -> p (m n)").bitcast(FP8X4),
                 scales=scales[:].rearrange("p m n -> p (m n)"),
-                in_=rounded[:].rearrange("p m n j -> p (m n j)"),
+                in_=rounded.rearrange("p m n j -> p (m n j)"),
             )
-            if piece in BEHIND_WEIGHTS:
-                gather(*BEHIND_WEIGHTS[piece], loads, buffer)
+            for i in range(count):
+                matrices[m0 + i] = (words[:, i, :], scales[:, i, :])
+
+        piece_berth = (7, 8, 9, 10, 11, 12, 13, 0, 2, 3)
+        gathers_behind = (
+            ((2, 0, T, 0),),
+            ((SCALES, T, T, 5120), (2, T, T, 0)),
+            ((1, 2 * T, T, 0),),
+            ((SCALES, 2 * T, T, 0),),
+            ((2, 2 * T, 2 * C, 0),),
+        )
+        bias_behind = {16: (0, 2), 24: (2, 5), 36: (5, 8), 44: (8, E)}
+        for group in range(5):
+            rounded = berth(rounds, f"w_rounded{group}", [P, 8, N, PACK], BF16, (group + 2) % 3)
+            for half in range(2):
+                piece = 2 * group + half
+                round_weights(4 * piece, 4, piece_berth[piece], 0, rounded[:, 4 * half : 4 * half + 4])
+                for e in range(*bias_behind.get(4 * piece, (0, 0))):
+                    empty_on_scalar(e)
+            quantize_weights(8 * group, rounded[:])
+            for sort, s0, slots, byte in gathers_behind[group]:
+                gather(sort, s0, slots, piece_berth[2 * group + 1], byte)
             multiply()
-            if piece in BIAS_BEHIND:
-                e0, e1 = BIAS_BEHIND[piece]
-                bias = held.tile([P, e1 - e0], F32, name=f"bias{e0}")
-                nc.sync.dma_start(bias[:], b[:, e0:e1])
-                for e in range(e0, e1):
-                    for product, c0, c1 in products[e]:
-                        nc.scalar.activation(y[:, e * C + c0 : e * C + c1], product, IDENTITY, bias=bias[:, e - e0 : e - e0 + 1])
+        rounded = berth(rounds, "w_rounded5", [P, 4, N, PACK], BF16, 1)
+        round_weights(40, 4, 5, 0, rounded[:])
+        quantize_weights(40, rounded[:])
+        gather(2, S - 3 * C, 2 * C, 5)
+        multiply()
+        gather(2, S - C, C, 5, BERTH // 2)
+        multiply()
+        in_y = y[:, 13 * C : 14 * C].bitcast(BF16).rearrange("p (m n j) -> p m n j", m=1, j=PACK)
+        round_weights(44, 1, 4, BERTH // 2, in_y)
+        quantize_weights(44, in_y)
+        multiply()
+        for e in (8, 9, 10, 11, 12, 14):
+            empty_on_scalar(e)
+        nc.vector.tensor_scalar_add(y[:, 13 * C : 14 * C], products[13][0][0], bias[13])
 
         for pos_tile, pos in zip(pos_sb, (pos1, pos2, pos3)):
             nc.sync.dma_start(pos_tile[:], pos)
         gates = held.tile([P, TOP, vector_tokens], F32, tag="gates", name="gates", align_bytes=64)
         nc.sync.dma_start(gates[:], gate[:, :, :vector_tokens].rearrange("r p t -> p r t"))
 
-        free.extend(lent)
-
         def entries(r, c0, c1):
             return pos_sb[r][:, c0 * P // STRIPE : c1 * P // STRIPE]
 
         turned = {}
-        ring = [take(keep=True) for i in range(LAG)]
-        weighed = loads.tile([P, TOP, scalar_blocks, P], F32, tag=take(), name="weighed", align_bytes=64)
+        weighed = berth(quay, "weighed", [P, TOP, scalar_blocks, P], F32, 7)
         back = {c: bank(4 + c - VECTOR_BLOCKS, [P, P]) for c in range(VECTOR_BLOCKS, blocks)}
 
         def fetch(step):
             r, c0, c1 = FETCHES[step]
-            plain = loads.tile([P, c1 - c0, P], F32, tag=ring[step % LAG], name="plain", align_bytes=64)
+            plain = berth(quay, f"plain{step}", [P, c1 - c0, P], F32, 9, step % LAG * 2048)
             nc.scalar.activation(plain[:].rearrange("p c t -> p (c t)"), y[:].indirect(entries(r, c0, c1)), COPY)
             tile = bank(step % 4, [P, c1 - c0, P])
             for c in range(c0, c1):
@@ -266,7 +304,7 @@ def tile_moe_tk_lin_bias_kernel(tc, xT, w, b, gate, offs, pos1, pos2, pos3, out)
                 weigh_turned(step - LAG)
             if step <= last:
                 fetch(step)
-        handed = loads.tile([P, scalar_blocks, P], F32, tag=ring[(last - 1) % LAG], name="handed", align_bytes=64)
+        handed = berth(quay, "handed", [P, scalar_blocks, P], F32, 9, (last - 1) % LAG * 2048)
         for c in (6, 7):
             nc.scalar.copy(handed[:, c - VECTOR_BLOCKS, :], back[c][:])
         weigh_turned(last)
@@ -275,9 +313,9 @@ def tile_moe_tk_lin_bias_kernel(tc, xT, w, b, gate, offs, pos1, pos2, pos3, out)
         nc.scalar.copy(handed[:, 3, :], back[9][:])
         nc.scalar.dma_start(out[:, 9 * P :], handed[:, 3, :])
 
-        terms = [loads.tile([P, vector_tokens], F32, tag=take(), name="term", align_bytes=64) for r in range(TOP)]
-        pair = loads.tile([P, vector_tokens], F32, tag=take(), name="pair", align_bytes=64)
-        result = loads.tile([P, vector_tokens], F32, tag=take(), name="result", align_bytes=64)
+        terms = [berth(quay, f"term{r}", [P, vector_tokens], F32, 11 + 2 * (r // 2), r % 2 * BERTH // 2) for r in range(TOP)]
+        pair = berth(quay, "pair", [P, vector_tokens], F32, 13, BERTH // 2)
+        result = berth(quay, "result", [P, vector_tokens], F32, 6, BERTH // 2)
 
         def weigh(r, c0, c1):
             columns = slice(c0 * P, c1 * P)

@@ -27,7 +27,7 @@ FIRST_UNITS = (256, 512, 256, 256)
 HIGH_PIECES = ((512, 256), (512, 256), (256, 192))
 PLANE = (4, 0, 8)
 SCALES = 3
-SCALE_WINDOW = 1792
+SHORT_WINDOW = 1792
 VECTOR_BLOCKS = 6
 FETCHES = ((2, 6, 8), (1, 6, 8), (0, 6, 8), (2, 8, 10), (1, 8, 9), (0, 8, 9), (1, 9, 10), (0, 9, 10))
 LAG = 3
@@ -64,7 +64,7 @@ def tile_moe_tk_lin_bias_kernel(tc, xT, w, b, gate, offs, pos1, pos2, pos3, out)
         offs_sb = held.tile([P, S // STRIPE], U16, name="offs_sb")
         pos_sb = [held.tile([P, T // STRIPE], U16, name=f"pos{r}_sb") for r in range(TOP)]
         token_words = held.tile([P, (passes - 1) * T + S], U32, name="token_words", align_bytes=64)
-        token_scales = held.tile([P, SCALE_WINDOW], U8, name="token_scales", align_bytes=64)
+        token_scales = held.tile([P, S], U8, name="token_scales", align_bytes=64)
         gate_rows = held.tile([P, P], F32, name="gate_rows", align_bytes=64)
         gate_columns = held.tile([P, TOP * scalar_blocks], F32, name="gate_columns")
         ident = held.tile([P, P], F32, name="ident", align_bytes=64)
@@ -95,7 +95,7 @@ def tile_moe_tk_lin_bias_kernel(tc, xT, w, b, gate, offs, pos1, pos2, pos3, out)
                 window = token_scales[:]
             else:
                 first_word = (passes - 1 - sort) * T
-                window = token_words[:, first_word : first_word + (S if slots > T else SCALE_WINDOW)]
+                window = token_words[:, first_word : first_word + (S if slots > T else SHORT_WINDOW)]
             nc.vector.tensor_copy(gathered[:], window.indirect(offs_sb[:, s0 // STRIPE : (s0 + slots) // STRIPE]))
             for h in range(s0 // P, (s0 + slots) // P):
                 by_expert[sort, h] = (gathered, s0)
@@ -112,7 +112,7 @@ def tile_moe_tk_lin_bias_kernel(tc, xT, w, b, gate, offs, pos1, pos2, pos3, out)
             high.append((t0, raw))
         nc.sync.dma_start(offs_sb[:], offs)
         later = {}
-        for a, t0, tokens, number, byte in ((1, 0, 512, 2, 0), (1, 512, 768, 3, 0), (2, 0, 256, 1, 2048), (2, 256, 512, 5, 0), (2, 768, 512, 6, 0)):
+        for a, t0, tokens, number, byte in ((1, 0, 640, 1, 2048), (1, 640, 640, 2, 4096), (2, 0, 512, 4, 0), (2, 512, 768, 5, 0)):
             later[a, t0] = berth(quay, f"x{a}_{t0}", [P, 1, PACK, tokens], F32, number, byte)
             nc.sync.dma_start(later[a, t0][:, 0], x_view[a][:, :, t0 : t0 + tokens])
         for r in range(TOP):
@@ -139,19 +139,25 @@ def tile_moe_tk_lin_bias_kernel(tc, xT, w, b, gate, offs, pos1, pos2, pos3, out)
         gather(0, S // 2, S // 2)
 
         second = held.tile([P, 1, T, PACK], BF16, tag="gates", name="second", align_bytes=64)
-        for t0, tokens in ((0, 512), (512, 768)):
+        for t0, tokens in ((0, 640), (640, 640)):
             interleave(second[:, :, t0 : t0 + tokens, :], later[1, t0][:])
         for t0, tokens in ((0, 1024), (1024, 256)):
             quantize_tokens(1, t0, second[:, 0, t0 : t0 + tokens, :])
 
-        for t0, tokens, number, byte in ((0, 256, 0, 0), (256, 512, 1, 0), (768, 512, 1, BERTH // 2)):
-            rounded = berth(rounds, f"third{t0}", [P, 1, tokens, PACK], BF16, number, byte)
-            interleave(rounded[:], later[2, t0][:])
-            quantize_tokens(2, t0, rounded[:, 0])
-            if t0 == 0:
-                gather(1, 0, S // 2, 1)
-        gather(1, S // 2, 640, 6)
-        gather(SCALES, 0, T)
+        third = berth(rounds, "third", [P, 1, T, PACK], BF16, 0)
+
+        def round_third(piece, t0, t1):
+            interleave(third[:, :, t0:t1, :], later[2, piece][:, :, :, t0 - piece : t1 - piece])
+
+        round_third(0, 0, 256)
+        quantize_tokens(2, 0, third[:, 0, :256, :])
+        round_third(0, 256, 512)
+        gather(1, 0, S // 2, 4)
+        round_third(512, 512, 768)
+        quantize_tokens(2, 256, third[:, 0, 256:768, :])
+        round_third(512, 768, T)
+        quantize_tokens(2, 768, third[:, 0, 768:, :])
+        gather(1, S // 2, S // 2, 5)
 
         gates_turned = bank(7, [P, P])
         nc.tensor.transpose(gates_turned[:], gate_rows[:], ident[:])
@@ -161,7 +167,7 @@ def tile_moe_tk_lin_bias_kernel(tc, xT, w, b, gate, offs, pos1, pos2, pos3, out)
         matrices = {}
         products = {}
         passes_done = [0] * E
-        pair_bank = {0: 0, 2: 1, 5: 3, 8: 5, 10: 6}
+        pair_bank = {0: 0, 2: 1, 4: 2, 6: 3, 8: 4, 10: 5}
         paired = [e + 1 for e in pair_bank]
         bias = {}
 
@@ -172,7 +178,7 @@ def tile_moe_tk_lin_bias_kernel(tc, xT, w, b, gate, offs, pos1, pos2, pos3, out)
                 both = bank(pair_bank[e], [P, 2, C])
                 products[e], products[e + 1] = [(both[:, 0, :], 0, C)], [(both[:, 1, :], 0, C)]
             elif e not in paired:
-                products[e] = [(bank({4: 2, 7: 4, 12: 2, 13: 7}[e], [P, C])[:], 0, C)]
+                products[e] = [(bank({12: 6, 13: 7}[e], [P, C])[:], 0, C)]
 
         def operand(sort, s0, s1):
             gathered, base = by_expert[sort, s0 // P]
@@ -191,7 +197,7 @@ def tile_moe_tk_lin_bias_kernel(tc, xT, w, b, gate, offs, pos1, pos2, pos3, out)
                     words, scales = matrices[passes * e + a]
                     for dst, c0, c1 in products[e]:
                         cut = [c0, c1]
-                        if by_expert[a, halves[0]][1] != by_expert[a, halves[1]][1]:
+                        if any(by_expert[sort, halves[0]][1] != by_expert[sort, halves[1]][1] for sort in (SCALES, a)):
                             cut = [c0, (c0 + c1) // 2, c1]
                         for d0, d1 in zip(cut, cut[1:]):
                             slot_words, w0, w1 = operand(a, e * C + d0, e * C + d1)
@@ -234,15 +240,9 @@ def tile_moe_tk_lin_bias_kernel(tc, xT, w, b, gate, offs, pos1, pos2, pos3, out)
             for i in range(count):
                 matrices[m0 + i] = (words[:, i, :], scales[:, i, :])
 
-        piece_berth = (7, 8, 9, 10, 11, 12, 13, 0, 2, 3)
-        gathers_behind = (
-            ((2, 0, T, 0),),
-            ((SCALES, T, T, 5120), (2, T, T, 0)),
-            ((1, 2 * T, T, 0),),
-            ((SCALES, 2 * T, T, 0),),
-            ((2, 2 * T, 2 * C, 0),),
-        )
-        bias_behind = {16: (0, 2), 24: (2, 5), 36: (5, 8), 44: (8, E)}
+        piece_berth = (7, 8, 9, 10, 11, 12, 13, 0, 1, 2)
+        gathers_behind = ((SCALES, 0, S // 2), (2, 0, S // 2), (SCALES, S // 2, S // 2), (2, S // 2, 11 * C - S // 2), (2, 11 * C, 2 * C))
+        bias_behind = {28: (0, 4), 44: (4, E)}
         for group in range(5):
             rounded = berth(rounds, f"w_rounded{group}", [P, 8, N, PACK], BF16, (group + 2) % 3)
             for half in range(2):
@@ -251,21 +251,20 @@ def tile_moe_tk_lin_bias_kernel(tc, xT, w, b, gate, offs, pos1, pos2, pos3, out)
                 for e in range(*bias_behind.get(4 * piece, (0, 0))):
                     empty_on_scalar(e)
             quantize_weights(8 * group, rounded[:])
-            for sort, s0, slots, byte in gathers_behind[group]:
-                gather(sort, s0, slots, piece_berth[2 * group + 1], byte)
+            gather(*gathers_behind[group], piece_berth[2 * group + 1])
             multiply()
         rounded = berth(rounds, "w_rounded5", [P, 4, N, PACK], BF16, 1)
-        round_weights(40, 4, 5, 0, rounded[:])
+        round_weights(40, 4, 3, 0, rounded[:])
         quantize_weights(40, rounded[:])
-        gather(2, S - 3 * C, 2 * C, 5)
+        gather(2, S - 2 * C, C, 3)
         multiply()
-        gather(2, S - C, C, 5, BERTH // 2)
+        gather(2, S - C, C, 3, BERTH // 2)
         multiply()
         in_y = y[:, 13 * C : 14 * C].bitcast(BF16).rearrange("p (m n j) -> p m n j", m=1, j=PACK)
-        round_weights(44, 1, 4, BERTH // 2, in_y)
+        round_weights(44, 1, 6, BERTH // 2, in_y)
         quantize_weights(44, in_y)
         multiply()
-        for e in (8, 9, 10, 11, 12, 14):
+        for e in (4, 5, 6, 7, 8, 9, 10, 11, 12, 14):
             empty_on_scalar(e)
         nc.vector.tensor_scalar_add(y[:, 13 * C : 14 * C], products[13][0][0], bias[13])
 
@@ -315,7 +314,7 @@ def tile_moe_tk_lin_bias_kernel(tc, xT, w, b, gate, offs, pos1, pos2, pos3, out)
 
         terms = [berth(quay, f"term{r}", [P, vector_tokens], F32, 11 + 2 * (r // 2), r % 2 * BERTH // 2) for r in range(TOP)]
         pair = berth(quay, "pair", [P, vector_tokens], F32, 13, BERTH // 2)
-        result = berth(quay, "result", [P, vector_tokens], F32, 6, BERTH // 2)
+        result = berth(quay, "result", [P, vector_tokens], F32, 1)
 
         def weigh(r, c0, c1):
             columns = slice(c0 * P, c1 * P)

@@ -112,7 +112,7 @@ def tile_moe_tk_lin_bias_kernel(tc, xT, w, b, gate, offs, pos1, pos2, pos3, out)
             high.append((t0, raw))
         nc.sync.dma_start(offs_sb[:], offs)
         later = {}
-        for a, t0, tokens, number, byte in ((1, 0, 640, 1, 2048), (1, 640, 640, 2, 4096), (2, 0, 512, 4, 0), (2, 512, 768, 5, 0)):
+        for a, t0, tokens, number, byte in ((1, 0, 1024, 2, 0), (1, 1024, 256, 1, 2048), (2, 0, 256, 4, 0), (2, 256, 512, 5, 0), (2, 768, 512, 6, 0)):
             later[a, t0] = berth(quay, f"x{a}_{t0}", [P, 1, PACK, tokens], F32, number, byte)
             nc.sync.dma_start(later[a, t0][:, 0], x_view[a][:, :, t0 : t0 + tokens])
         for r in range(TOP):
@@ -139,25 +139,16 @@ def tile_moe_tk_lin_bias_kernel(tc, xT, w, b, gate, offs, pos1, pos2, pos3, out)
         gather(0, S // 2, S // 2)
 
         second = held.tile([P, 1, T, PACK], BF16, tag="gates", name="second", align_bytes=64)
-        for t0, tokens in ((0, 640), (640, 640)):
-            interleave(second[:, :, t0 : t0 + tokens, :], later[1, t0][:])
         for t0, tokens in ((0, 1024), (1024, 256)):
+            interleave(second[:, :, t0 : t0 + tokens, :], later[1, t0][:])
             quantize_tokens(1, t0, second[:, 0, t0 : t0 + tokens, :])
 
         third = berth(rounds, "third", [P, 1, T, PACK], BF16, 0)
-
-        def round_third(piece, t0, t1):
-            interleave(third[:, :, t0:t1, :], later[2, piece][:, :, :, t0 - piece : t1 - piece])
-
-        round_third(0, 0, 256)
-        quantize_tokens(2, 0, third[:, 0, :256, :])
-        round_third(0, 256, 512)
-        gather(1, 0, S // 2, 4)
-        round_third(512, 512, 768)
-        quantize_tokens(2, 256, third[:, 0, 256:768, :])
-        round_third(512, 768, T)
-        quantize_tokens(2, 768, third[:, 0, 768:, :])
-        gather(1, S // 2, S // 2, 5)
+        for t0, tokens, number in ((0, 256, 4), (256, 512, None), (768, 512, 6)):
+            interleave(third[:, :, t0 : t0 + tokens, :], later[2, t0][:])
+            quantize_tokens(2, t0, third[:, 0, t0 : t0 + tokens, :])
+            if number is not None:
+                gather(1, t0 // 768 * S // 2, S // 2, number)
 
         gates_turned = bank(7, [P, P])
         nc.tensor.transpose(gates_turned[:], gate_rows[:], ident[:])
@@ -261,7 +252,7 @@ def tile_moe_tk_lin_bias_kernel(tc, xT, w, b, gate, offs, pos1, pos2, pos3, out)
         gather(2, S - C, C, 3, BERTH // 2)
         multiply()
         in_y = y[:, 13 * C : 14 * C].bitcast(BF16).rearrange("p (m n j) -> p m n j", m=1, j=PACK)
-        round_weights(44, 1, 6, BERTH // 2, in_y)
+        round_weights(44, 1, 5, 0, in_y)
         quantize_weights(44, in_y)
         multiply()
         for e in (4, 5, 6, 7, 8, 9, 10, 11, 12, 14):

@@ -22,12 +22,9 @@ RUN = 4
 FLOPS = 2 * 1536 * 128 * 3840
 
 BERTH = 8192
-LOW_ON_VECTOR = 704
-FIRST_UNITS = (256, 512, 256, 256)
-HIGH_PIECES = ((512, 256), (512, 256), (256, 192))
-PLANE = (4, 0, 8)
+PLANE = (0, 4, 8)
 SCALES = 3
-SHORT_WINDOW = 1792
+WINDOW = 1792
 VECTOR_BLOCKS = 6
 FETCHES = ((2, 6, 8), (1, 6, 8), (0, 6, 8), (2, 8, 10), (1, 8, 9), (0, 8, 9), (1, 9, 10), (0, 9, 10))
 LAG = 3
@@ -46,9 +43,6 @@ def tile_moe_tk_lin_bias_kernel(tc, xT, w, b, gate, offs, pos1, pos2, pos3, out)
     x_view = xT.rearrange("(a p j) t -> a p j t", p=P, j=PACK)
     w_view = w.rearrange("e (a p j) n -> p (e a) (j n)", p=P, j=PACK)
 
-    def spans(widths):
-        return [(sum(widths[:i]), width) for i, width in enumerate(widths)]
-
     with ExitStack() as ctx:
         held = ctx.enter_context(tc.tile_pool(name="held", bufs=1))
         quay = ctx.enter_context(tc.tile_pool(name="quay", bufs=1))
@@ -63,8 +57,8 @@ def tile_moe_tk_lin_bias_kernel(tc, xT, w, b, gate, offs, pos1, pos2, pos3, out)
 
         offs_sb = held.tile([P, S // STRIPE], U16, name="offs_sb")
         pos_sb = [held.tile([P, T // STRIPE], U16, name=f"pos{r}_sb") for r in range(TOP)]
-        token_words = held.tile([P, (passes - 1) * T + S], U32, name="token_words", align_bytes=64)
-        token_scales = held.tile([P, S], U8, name="token_scales", align_bytes=64)
+        token_words = held.tile([P, (passes - 1) * T + WINDOW], U32, name="token_words", align_bytes=64)
+        token_scales = held.tile([P, WINDOW], U8, name="token_scales", align_bytes=64)
         gate_rows = held.tile([P, P], F32, name="gate_rows", align_bytes=64)
         gate_columns = held.tile([P, TOP * scalar_blocks], F32, name="gate_columns")
         ident = held.tile([P, P], F32, name="ident", align_bytes=64)
@@ -95,7 +89,7 @@ def tile_moe_tk_lin_bias_kernel(tc, xT, w, b, gate, offs, pos1, pos2, pos3, out)
                 window = token_scales[:]
             else:
                 first_word = (passes - 1 - sort) * T
-                window = token_words[:, first_word : first_word + (S if slots > T else SHORT_WINDOW)]
+                window = token_words[:, first_word : first_word + WINDOW]
             nc.vector.tensor_copy(gathered[:], window.indirect(offs_sb[:, s0 // STRIPE : (s0 + slots) // STRIPE]))
             for h in range(s0 // P, (s0 + slots) // P):
                 by_expert[sort, h] = (gathered, s0)
@@ -103,16 +97,19 @@ def tile_moe_tk_lin_bias_kernel(tc, xT, w, b, gate, offs, pos1, pos2, pos3, out)
         def interleave(dst, src):
             nc.scalar.copy(dst.rearrange("p m (c i) j -> p m c j i", i=RUN), src.rearrange("p m j (c i) -> p m c j i", i=RUN))
 
-        low = held.tile([P, 2, T], F32, tag="y", name="low", align_bytes=64)
-        nc.sync.dma_start(low[:], x_view[0][:, 0:2, :])
-        high = []
-        for i, (t0, tokens) in enumerate(spans([tokens for tokens, on_vector in HIGH_PIECES])):
-            raw = berth(quay, f"high{i}", [P, 2, tokens], F32, 0, i * BERTH // 2)
-            nc.sync.dma_start(raw[:], x_view[0][:, 2:4, t0 : t0 + tokens])
-            high.append((t0, raw))
+        raw_first = berth(quay, "raw_first", [P, PACK * T], F32, 8)
+        x_first = xT[: P * PACK].rearrange("(p j) t -> p (j t)", j=PACK)
+        for c0, c1 in ((0, 2048), (2048, 3072), (3 * T, 3 * T + 512)):
+            nc.sync.dma_start(raw_first[:, c0:c1], x_first[:, c0:c1])
+        rows_first = raw_first[:].rearrange("p (j t) -> p j t", j=PACK)
+        upper = {0: rows_first[:, 2:4, :512]}
+        for i, (t0, t1) in enumerate(((512, 1024), (1024, T))):
+            raw = berth(quay, f"upper{t0}", [P, 2, t1 - t0], F32, 0, i * BERTH // 2)
+            nc.sync.dma_start(raw[:], x_view[0][:, 2:4, t0:t1])
+            upper[t0] = raw[:]
         nc.sync.dma_start(offs_sb[:], offs)
         later = {}
-        for a, t0, tokens, number, byte in ((1, 0, 1024, 2, 0), (1, 1024, 256, 1, 2048), (2, 0, 256, 4, 0), (2, 256, 512, 5, 0), (2, 768, 512, 6, 0)):
+        for a, t0, tokens, number, byte in ((1, 0, 512, 2, 0), (1, 512, 512, 3, 0), (1, 1024, 256, 1, 2048), (2, 0, 256, 4, 3072), (2, 256, 1024, 5, 2048)):
             later[a, t0] = berth(quay, f"x{a}_{t0}", [P, 1, PACK, tokens], F32, number, byte)
             nc.sync.dma_start(later[a, t0][:, 0], x_view[a][:, :, t0 : t0 + tokens])
         for r in range(TOP):
@@ -121,40 +118,52 @@ def tile_moe_tk_lin_bias_kernel(tc, xT, w, b, gate, offs, pos1, pos2, pos3, out)
 
         first = held.tile([P, T, PACK], BF16, tag="gates", name="first", align_bytes=64)
 
-        def round_half(copy, half, t0, src):
-            dst = first[:, t0 : t0 + src.shape[2], 2 * half : 2 * half + 2]
+        def round_half(copy, half, t0, t1):
+            dst = first[:, t0:t1, 2 * half : 2 * half + 2]
+            piece = t0 // 512 * 512
+            src = upper[piece][:, :, t0 - piece : t1 - piece] if half else rows_first[:, 0:2, t0:t1]
             copy(dst.rearrange("p (c i) e -> p c e i", i=RUN), src.rearrange("p e (c i) -> p c e i", i=RUN))
 
-        round_half(nc.vector.tensor_copy, 0, 0, low[:, :, :LOW_ON_VECTOR])
-        round_half(nc.scalar.copy, 0, LOW_ON_VECTOR, low[:, :, LOW_ON_VECTOR:])
-        units = spans(FIRST_UNITS)
-        for (t0, raw), (tokens, on_vector) in zip(high, HIGH_PIECES):
-            round_half(nc.vector.tensor_copy, 1, t0, raw[:, :, :on_vector])
-            round_half(nc.scalar.copy, 1, t0 + on_vector, raw[:, :, on_vector:])
-            if t0 == 0:
-                quantize_tokens(0, 0, first[:, : units[0][1], :])
-        for t0, tokens in units[1:]:
-            quantize_tokens(0, t0, first[:, t0 : t0 + tokens, :])
-        gather(0, 0, S // 2)
-        gather(0, S // 2, S // 2)
+        def share(half, t0, middle, t1):
+            round_half(nc.vector.tensor_copy, half, t0, middle)
+            round_half(nc.scalar.copy, half, middle, t1)
+
+        def quantize_first(t0, t1):
+            quantize_tokens(0, t0, first[:, t0:t1, :])
+
+        share(0, 0, 512, 768)
+        share(0, 768, 1088, T)
+        share(1, 0, 256, 512)
+        quantize_first(0, 256)
+        quantize_first(256, 512)
+        share(1, 512, 768, 1024)
+        share(1, 1024, 1152, T)
+        quantize_first(512, 768)
+        quantize_first(768, 1024)
+        quantize_first(1024, T)
+        for s0 in range(0, S, T):
+            gather(0, s0, T)
 
         second = held.tile([P, 1, T, PACK], BF16, tag="gates", name="second", align_bytes=64)
-        for t0, tokens in ((0, 1024), (1024, 256)):
+        for t0, tokens in ((0, 512), (512, 512), (1024, 256)):
             interleave(second[:, :, t0 : t0 + tokens, :], later[1, t0][:])
             quantize_tokens(1, t0, second[:, 0, t0 : t0 + tokens, :])
 
         third = berth(rounds, "third", [P, 1, T, PACK], BF16, 0)
-        for t0, tokens, number in ((0, 256, 4), (256, 512, None), (768, 512, 6)):
-            interleave(third[:, :, t0 : t0 + tokens, :], later[2, t0][:])
-            quantize_tokens(2, t0, third[:, 0, t0 : t0 + tokens, :])
-            if number is not None:
-                gather(1, t0 // 768 * S // 2, S // 2, number)
+        for piece, t0, t1 in ((0, 0, 256), (256, 256, 768), (256, 768, T)):
+            interleave(third[:, :, t0:t1, :], later[2, piece][:, :, :, t0 - piece : t1 - piece])
+            quantize_tokens(2, t0, third[:, 0, t0:t1, :])
+            if t0 == 0:
+                gather(1, 0, T, 4)
+                gather(1, T, T, 4, 4 * T)
+        gather(1, 2 * T, T, 5, 2048)
+        gather(SCALES, 0, T)
 
         gates_turned = bank(7, [P, P])
         nc.tensor.transpose(gates_turned[:], gate_rows[:], ident[:])
         nc.scalar.copy(gate_columns[:], gates_turned[:, : TOP * scalar_blocks])
 
-        y = held.tile([P, S], F32, tag="y", name="y", align_bytes=64)
+        y = held.tile([P, S], F32, name="y", align_bytes=64)
         matrices = {}
         products = {}
         passes_done = [0] * E
@@ -231,9 +240,9 @@ def tile_moe_tk_lin_bias_kernel(tc, xT, w, b, gate, offs, pos1, pos2, pos3, out)
             for i in range(count):
                 matrices[m0 + i] = (words[:, i, :], scales[:, i, :])
 
-        piece_berth = (7, 8, 9, 10, 11, 12, 13, 0, 1, 2)
-        gathers_behind = ((SCALES, 0, S // 2), (2, 0, S // 2), (SCALES, S // 2, S // 2), (2, S // 2, 11 * C - S // 2), (2, 11 * C, 2 * C))
-        bias_behind = {28: (0, 4), 44: (4, E)}
+        piece_berth = (8, 9, 10, 11, 12, 13, 0, 1, 2, 3)
+        gathers_behind = ((2, 0, T), (SCALES, T, T), (2, T, T), (SCALES, 2 * T, T), (2, 2 * T, 2 * C))
+        bias_behind = {24: (0, 4), 44: (4, E)}
         for group in range(5):
             rounded = berth(rounds, f"w_rounded{group}", [P, 8, N, PACK], BF16, (group + 2) % 3)
             for half in range(2):
@@ -241,18 +250,19 @@ def tile_moe_tk_lin_bias_kernel(tc, xT, w, b, gate, offs, pos1, pos2, pos3, out)
                 round_weights(4 * piece, 4, piece_berth[piece], 0, rounded[:, 4 * half : 4 * half + 4])
                 for e in range(*bias_behind.get(4 * piece, (0, 0))):
                     empty_on_scalar(e)
-            quantize_weights(8 * group, rounded[:])
+            for half in range(2):
+                quantize_weights(8 * group + 4 * half, rounded[:, 4 * half : 4 * half + 4])
             gather(*gathers_behind[group], piece_berth[2 * group + 1])
             multiply()
         rounded = berth(rounds, "w_rounded5", [P, 4, N, PACK], BF16, 1)
-        round_weights(40, 4, 3, 0, rounded[:])
-        quantize_weights(40, rounded[:])
-        gather(2, S - 2 * C, C, 3)
-        multiply()
-        gather(2, S - C, C, 3, BERTH // 2)
-        multiply()
+        for half, (s0, slots) in enumerate(((S - 3 * C, 2 * C), (S - C, C))):
+            round_weights(40 + 2 * half, 2, 6, half * BERTH // 2, rounded[:, 2 * half : 2 * half + 2])
+            quantize_weights(40 + 2 * half, rounded[:, 2 * half : 2 * half + 2])
+            multiply()
+            gather(2, s0, slots, 6, half * BERTH // 2)
+            multiply()
         in_y = y[:, 13 * C : 14 * C].bitcast(BF16).rearrange("p (m n j) -> p m n j", m=1, j=PACK)
-        round_weights(44, 1, 5, 0, in_y)
+        round_weights(44, 1, 7, BERTH // 2, in_y)
         quantize_weights(44, in_y)
         multiply()
         for e in (4, 5, 6, 7, 8, 9, 10, 11, 12, 14):
@@ -262,18 +272,19 @@ def tile_moe_tk_lin_bias_kernel(tc, xT, w, b, gate, offs, pos1, pos2, pos3, out)
         for pos_tile, pos in zip(pos_sb, (pos1, pos2, pos3)):
             nc.sync.dma_start(pos_tile[:], pos)
         gates = held.tile([P, TOP, vector_tokens], F32, tag="gates", name="gates", align_bytes=64)
-        nc.sync.dma_start(gates[:], gate[:, :, :vector_tokens].rearrange("r p t -> p r t"))
+        for r in range(TOP):
+            nc.sync.dma_start(gates[:, r, :], gate[r, :, :vector_tokens])
 
         def entries(r, c0, c1):
             return pos_sb[r][:, c0 * P // STRIPE : c1 * P // STRIPE]
 
         turned = {}
-        weighed = berth(quay, "weighed", [P, TOP, scalar_blocks, P], F32, 7)
+        weighed = berth(quay, "weighed", [P, TOP, scalar_blocks, P], F32, 8)
         back = {c: bank(4 + c - VECTOR_BLOCKS, [P, P]) for c in range(VECTOR_BLOCKS, blocks)}
 
         def fetch(step):
             r, c0, c1 = FETCHES[step]
-            plain = berth(quay, f"plain{step}", [P, c1 - c0, P], F32, 9, step % LAG * 2048)
+            plain = berth(quay, f"plain{step}", [P, c1 - c0, P], F32, 10, step % LAG * 2048)
             nc.scalar.activation(plain[:].rearrange("p c t -> p (c t)"), y[:].indirect(entries(r, c0, c1)), COPY)
             tile = bank(step % 4, [P, c1 - c0, P])
             for c in range(c0, c1):
@@ -294,7 +305,7 @@ def tile_moe_tk_lin_bias_kernel(tc, xT, w, b, gate, offs, pos1, pos2, pos3, out)
                 weigh_turned(step - LAG)
             if step <= last:
                 fetch(step)
-        handed = berth(quay, "handed", [P, scalar_blocks, P], F32, 9, (last - 1) % LAG * 2048)
+        handed = berth(quay, "handed", [P, scalar_blocks, P], F32, 10, (last - 1) % LAG * 2048)
         for c in (6, 7):
             nc.scalar.copy(handed[:, c - VECTOR_BLOCKS, :], back[c][:])
         weigh_turned(last)
@@ -303,9 +314,9 @@ def tile_moe_tk_lin_bias_kernel(tc, xT, w, b, gate, offs, pos1, pos2, pos3, out)
         nc.scalar.copy(handed[:, 3, :], back[9][:])
         nc.scalar.dma_start(out[:, 9 * P :], handed[:, 3, :])
 
-        terms = [berth(quay, f"term{r}", [P, vector_tokens], F32, 11 + 2 * (r // 2), r % 2 * BERTH // 2) for r in range(TOP)]
-        pair = berth(quay, "pair", [P, vector_tokens], F32, 13, BERTH // 2)
-        result = berth(quay, "result", [P, vector_tokens], F32, 1)
+        terms = [berth(quay, f"term{r}", [P, vector_tokens], F32, (12, 12, 0)[r], r % 2 * BERTH // 2) for r in range(TOP)]
+        pair = berth(quay, "pair", [P, vector_tokens], F32, 0, BERTH // 2)
+        result = berth(quay, "result", [P, vector_tokens], F32, 2)
 
         def weigh(r, c0, c1):
             columns = slice(c0 * P, c1 * P)
@@ -321,13 +332,13 @@ def tile_moe_tk_lin_bias_kernel(tc, xT, w, b, gate, offs, pos1, pos2, pos3, out)
             nc.sync.dma_start(out[:, columns], result[:, columns])
 
         weigh(0, 0, 6)
-        weigh(1, 0, 3)
-        weigh(2, 0, 3)
-        add_pair(0, 3)
-        weigh(1, 3, 6)
-        finish(0, 3)
-        add_pair(3, 6)
-        weigh(2, 3, 5)
-        weigh(2, 5, 6)
-        finish(3, 5)
+        weigh(1, 0, 4)
+        weigh(2, 0, 4)
+        add_pair(0, 4)
+        weigh(1, 4, 6)
+        finish(0, 4)
+        weigh(2, 4, 6)
+        add_pair(4, 5)
+        add_pair(5, 6)
+        finish(4, 5)
         finish(5, 6)

@@ -242,7 +242,7 @@ def tile_moe_tk_lin_bias_kernel(tc, xT, w, b, gate, offs, pos1, pos2, pos3, out)
 
         piece_berth = (8, 9, 10, 11, 12, 13, 0, 1, 2, 3)
         gathers_behind = ((2, 0, T), (SCALES, T, T), (2, T, T), (SCALES, 2 * T, T), (2, 2 * T, 2 * C))
-        bias_behind = {24: (0, 4), 44: (4, E)}
+        bias_behind = {20: (0, 2), 28: (2, 4), 44: (4, E)}
         for group in range(5):
             rounded = berth(rounds, f"w_rounded{group}", [P, 8, N, PACK], BF16, (group + 2) % 3)
             for half in range(2):

@@ -59,8 +59,8 @@ def tile_moe_tk_lin_bias_kernel(tc, xT, w, b, gate, offs, pos1, pos2, pos3, out)
         pos_sb = [held.tile([P, T // STRIPE], U16, name=f"pos{r}_sb") for r in range(TOP)]
         token_words = held.tile([P, (passes - 1) * T + WINDOW], U32, name="token_words", align_bytes=64)
         token_scales = held.tile([P, WINDOW], U8, name="token_scales", align_bytes=64)
-        gate_rows = held.tile([P, P], F32, name="gate_rows", align_bytes=64)
-        gate_columns = held.tile([P, TOP * scalar_blocks], F32, name="gate_columns")
+        gate_rows = held.tile([P, TOP, P], F32, name="gate_rows", align_bytes=64)
+        gate_columns = held.tile([P, TOP, scalar_blocks], F32, name="gate_columns")
         ident = held.tile([P, P], F32, name="ident", align_bytes=64)
 
         nc.vector.memset(token_scales[:, :T].bitcast(U32), 0)
@@ -112,9 +112,7 @@ def tile_moe_tk_lin_bias_kernel(tc, xT, w, b, gate, offs, pos1, pos2, pos3, out)
         for a, t0, tokens, number, byte in ((1, 0, 512, 2, 0), (1, 512, 512, 3, 0), (1, 1024, 256, 1, 2048), (2, 0, 256, 4, 3072), (2, 256, 1024, 5, 2048)):
             later[a, t0] = berth(quay, f"x{a}_{t0}", [P, 1, PACK, tokens], F32, number, byte)
             nc.sync.dma_start(later[a, t0][:, 0], x_view[a][:, :, t0 : t0 + tokens])
-        for r in range(TOP):
-            rows = gate_rows[r * scalar_blocks : (r + 1) * scalar_blocks, :]
-            nc.sync.dma_start(rows, gate[r, 0, vector_tokens:].rearrange("(c t) -> c t", t=P))
+        nc.sync.dma_start(gate_rows[:scalar_blocks], gate[:, 0, vector_tokens:].rearrange("r (c t) -> c r t", t=P))
 
         first = held.tile([P, T, PACK], BF16, tag="gates", name="first", align_bytes=64)
 
@@ -159,9 +157,10 @@ def tile_moe_tk_lin_bias_kernel(tc, xT, w, b, gate, offs, pos1, pos2, pos3, out)
         gather(1, 2 * T, T, 5, 2048)
         gather(SCALES, 0, T)
 
-        gates_turned = bank(7, [P, P])
-        nc.tensor.transpose(gates_turned[:], gate_rows[:], ident[:])
-        nc.scalar.copy(gate_columns[:], gates_turned[:, : TOP * scalar_blocks])
+        gates_turned = bank(7, [P, TOP, P])
+        for r in range(TOP):
+            nc.tensor.transpose(gates_turned[:, r, :], gate_rows[:, r, :], ident[:])
+        nc.scalar.copy(gate_columns[:], gates_turned[:, :, :scalar_blocks])
 
         y = held.tile([P, S], F32, name="y", align_bytes=64)
         matrices = {}
@@ -272,8 +271,8 @@ def tile_moe_tk_lin_bias_kernel(tc, xT, w, b, gate, offs, pos1, pos2, pos3, out)
         for pos_tile, pos in zip(pos_sb, (pos1, pos2, pos3)):
             nc.sync.dma_start(pos_tile[:], pos)
         gates = held.tile([P, TOP, vector_tokens], F32, tag="gates", name="gates", align_bytes=64)
-        for r in range(TOP):
-            nc.sync.dma_start(gates[:, r, :], gate[r, :, :vector_tokens])
+        for r, c0, c1 in ((0, 0, 6), (1, 0, 4), (2, 0, 4), (1, 4, 6), (2, 4, 6)):
+            nc.sync.dma_start(gates[:, r, c0 * P : c1 * P], gate[r, :, c0 * P : c1 * P])
 
         def entries(r, c0, c1):
             return pos_sb[r][:, c0 * P // STRIPE : c1 * P // STRIPE]
@@ -294,9 +293,9 @@ def tile_moe_tk_lin_bias_kernel(tc, xT, w, b, gate, offs, pos1, pos2, pos3, out)
         def weigh_turned(step):
             r, c0, c1 = FETCHES[step]
             for c in range(c0, c1):
-                column = r * scalar_blocks + c - VECTOR_BLOCKS
+                column = c - VECTOR_BLOCKS
                 term = weighed[:, r, c - VECTOR_BLOCKS, :]
-                nc.scalar.activation(term, turned[r, c], COPY, scale=gate_columns[:, column : column + 1])
+                nc.scalar.activation(term, turned[r, c], COPY, scale=gate_columns[:, r, column : column + 1])
                 nc.tensor.matmul(back[c][:], term, ident[:], start=(r == 2), stop=(r == 0), is_transpose=True)
 
         last = len(FETCHES) - 1

from contextlib import ExitStack

import concourse.mybir as mybir
from concourse.masks import make_identity

F32 = mybir.dt.float32
BF16 = mybir.dt.bfloat16
U32 = mybir.dt.uint32
U16 = mybir.dt.uint16
U8 = mybir.dt.uint8
FP8X4 = mybir.dt.float8_e4m3fn_x4
IDENTITY = mybir.ActivationFunctionType.Identity
COPY = mybir.ActivationFunctionType.Copy
MULT = mybir.AluOpType.mult
ADD = mybir.AluOpType.add

P = 128
PACK = 4
TOP = 3
STRIPE = 16
RUN = 4
FLOPS = 2 * 1536 * 128 * 3840

BERTH = 8192
PLANE = (0, 4, 8)
SCALES = 3
WINDOW = 1792
VECTOR_BLOCKS = 6
FETCHES = ((2, 6, 8), (1, 6, 8), (0, 6, 8), (2, 8, 10), (1, 8, 9), (0, 8, 9), (1, 9, 10), (0, 9, 10))
LAG = 3


def tile_moe_tk_lin_bias_kernel(tc, xT, w, b, gate, offs, pos1, pos2, pos3, out):
    nc = tc.nc
    K, T = xT.shape
    E, N = w.shape[0], w.shape[2]
    S = offs.shape[1] * STRIPE
    C = S // E
    passes = K // (P * PACK)
    blocks = T // P
    scalar_blocks = blocks - VECTOR_BLOCKS
    vector_tokens = VECTOR_BLOCKS * P
    x_view = xT.rearrange("(a p j) t -> a p j t", p=P, j=PACK)
    w_view = w.rearrange("e (a p j) n -> p (e a) (j n)", p=P, j=PACK)

    with ExitStack() as ctx:
        held = ctx.enter_context(tc.tile_pool(name="held", bufs=1))
        quay = ctx.enter_context(tc.tile_pool(name="quay", bufs=1))
        rounds = ctx.enter_context(tc.tile_pool(name="rounds", bufs=1))
        psum = ctx.enter_context(tc.psum_pool(name="psum", bufs=1))

        def bank(number, shape):
            return psum.tile(shape, F32, tag=f"bank{number}", name="bank")

        def berth(pool, name, shape, dtype, number, byte=0):
            return pool.tile(shape, dtype, name=name, align_bytes=64, offset=number * BERTH + byte)

        offs_sb = held.tile([P, S // STRIPE], U16, name="offs_sb")
        pos_sb = [held.tile([P, T // STRIPE], U16, name=f"pos{r}_sb") for r in range(TOP)]
        token_words = held.tile([P, (passes - 1) * T + WINDOW], U32, name="token_words", align_bytes=64)
        token_scales = held.tile([P, WINDOW], U8, name="token_scales", align_bytes=64)
        gate_rows = held.tile([P, TOP, P], F32, name="gate_rows", align_bytes=64)
        gate_columns = held.tile([P, TOP, scalar_blocks], F32, name="gate_columns")
        ident = held.tile([P, P], F32, name="ident", align_bytes=64)

        nc.vector.memset(token_scales[:, :T].bitcast(U32), 0)
        nc.vector.memset(gate_rows[:], 0.0)
        make_identity(nc, ident[:])

        def quantize_tokens(a, t0, rounded):
            tokens = rounded.shape[1]
            first_word = (passes - 1 - a) * T + t0
            nc.vector.quantize_mx(
                out=token_words[:, first_word : first_word + tokens].bitcast(FP8X4),
                scales=token_scales[PLANE[a] : P, t0 : t0 + tokens],
                in_=rounded.rearrange("p t j -> p (t j)"),
            )

        by_expert = {}

        def gather(sort, s0, slots, number=None, byte=0):
            name = f"gathered{sort}_{s0}"
            dtype = U8 if sort == SCALES else U32
            if number is None:
                gathered = held.tile([P, slots], dtype, name=name, align_bytes=64)
            else:
                gathered = berth(quay, name, [P, slots], dtype, number, byte)
            if sort == SCALES:
                window = token_scales[:]
            else:
                first_word = (passes - 1 - sort) * T
                window = token_words[:, first_word : first_word + WINDOW]
            nc.vector.tensor_copy(gathered[:], window.indirect(offs_sb[:, s0 // STRIPE : (s0 + slots) // STRIPE]))
            for h in range(s0 // P, (s0 + slots) // P):
                by_expert[sort, h] = (gathered, s0)

        def interleave(dst, src):
            nc.scalar.copy(dst.rearrange("p m (c i) j -> p m c j i", i=RUN), src.rearrange("p m j (c i) -> p m c j i", i=RUN))

        raw_first = berth(quay, "raw_first", [P, PACK * T], F32, 8)
        x_first = xT[: P * PACK].rearrange("(p j) t -> p (j t)", j=PACK)
        for c0, c1 in ((0, 2048), (2048, 3072), (3 * T, 3 * T + 512)):
            nc.sync.dma_start(raw_first[:, c0:c1], x_first[:, c0:c1])
        rows_first = raw_first[:].rearrange("p (j t) -> p j t", j=PACK)
        upper = {0: rows_first[:, 2:4, :512]}
        for i, (t0, t1) in enumerate(((512, 1024), (1024, T))):
            raw = berth(quay, f"upper{t0}", [P, 2, t1 - t0], F32, 0, i * BERTH // 2)
            nc.sync.dma_start(raw[:], x_view[0][:, 2:4, t0:t1])
            upper[t0] = raw[:]
        nc.sync.dma_start(offs_sb[:], offs)
        later = {}
        for a, t0, tokens, number, byte in ((1, 0, 512, 2, 0), (1, 512, 512, 3, 0), (1, 1024, 256, 1, 2048), (2, 0, 256, 4, 3072), (2, 256, 1024, 5, 2048)):
            later[a, t0] = berth(quay, f"x{a}_{t0}", [P, 1, PACK, tokens], F32, number, byte)
            nc.sync.dma_start(later[a, t0][:, 0], x_view[a][:, :, t0 : t0 + tokens])
        nc.sync.dma_start(gate_rows[:scalar_blocks], gate[:, 0, vector_tokens:].rearrange("r (c t) -> c r t", t=P))

        first = held.tile([P, T, PACK], BF16, tag="gates", name="first", align_bytes=64)

        def round_half(copy, half, t0, t1):
            dst = first[:, t0:t1, 2 * half : 2 * half + 2]
            piece = t0 // 512 * 512
            src = upper[piece][:, :, t0 - piece : t1 - piece] if half else rows_first[:, 0:2, t0:t1]
            copy(dst.rearrange("p (c i) e -> p c e i", i=RUN), src.rearrange("p e (c i) -> p c e i", i=RUN))

        def share(half, t0, middle, t1):
            round_half(nc.vector.tensor_copy, half, t0, middle)
            round_half(nc.scalar.copy, half, middle, t1)

        def quantize_first(t0, t1):
            quantize_tokens(0, t0, first[:, t0:t1, :])

        share(0, 0, 512, 768)
        share(0, 768, 1088, T)
        share(1, 0, 256, 512)
        quantize_first(0, 256)
        quantize_first(256, 512)
        share(1, 512, 768, 1024)
        share(1, 1024, 1152, T)
        quantize_first(512, 768)
        quantize_first(768, 1024)
        quantize_first(1024, T)
        for s0 in range(0, S, T):
            gather(0, s0, T)

        second = held.tile([P, 1, T, PACK], BF16, tag="gates", name="second", align_bytes=64)
        for t0, tokens in ((0, 512), (512, 512), (1024, 256)):
            interleave(second[:, :, t0 : t0 + tokens, :], later[1, t0][:])
            quantize_tokens(1, t0, second[:, 0, t0 : t0 + tokens, :])

        third = berth(rounds, "third", [P, 1, T, PACK], BF16, 0)
        for piece, t0, t1 in ((0, 0, 256), (256, 256, 768), (256, 768, T)):
            interleave(third[:, :, t0:t1, :], later[2, piece][:, :, :, t0 - piece : t1 - piece])
            quantize_tokens(2, t0, third[:, 0, t0:t1, :])
            if t0 == 0:
                gather(1, 0, T, 4)
                gather(1, T, T, 4, 4 * T)
        gather(1, 2 * T, T, 5, 2048)
        gather(SCALES, 0, T)

        gates_turned = bank(7, [P, TOP, P])
        for r in range(TOP):
            nc.tensor.transpose(gates_turned[:, r, :], gate_rows[:, r, :], ident[:])
        nc.scalar.copy(gate_columns[:], gates_turned[:, :, :scalar_blocks])

        y = held.tile([P, S], F32, name="y", align_bytes=64)
        matrices = {}
        products = {}
        passes_done = [0] * E
        pair_bank = {0: 0, 2: 1, 4: 2, 6: 3, 8: 4, 10: 5}
        paired = [e + 1 for e in pair_bank]
        bias = {}

        def open_product(e):
            if e == E - 1:
                products[e] = [(bank(number, [P, C // 2])[:], i * C // 2, (i + 1) * C // 2) for i, number in enumerate((0, 1))]
            elif e in pair_bank:
                both = bank(pair_bank[e], [P, 2, C])
                products[e], products[e + 1] = [(both[:, 0, :], 0, C)], [(both[:, 1, :], 0, C)]
            elif e not in paired:
                products[e] = [(bank({12: 6, 13: 7}[e], [P, C])[:], 0, C)]

        def operand(sort, s0, s1):
            gathered, base = by_expert[sort, s0 // P]
            return gathered, s0 - base, s1 - base

        def multiply():
            for e in range(E):
                while passes_done[e] < passes:
                    a = passes_done[e]
                    halves = (2 * e, 2 * e + 1)
                    ready = all((sort, h) in by_expert for sort in (SCALES, a) for h in halves) and passes * e + a in matrices
                    if not ready or (e in paired and passes_done[e - 1] < passes):
                        break
                    if a == 0:
                        open_product(e)
                    words, scales = matrices[passes * e + a]
                    for dst, c0, c1 in products[e]:
                        cut = [c0, c1]
                        if any(by_expert[sort, halves[0]][1] != by_expert[sort, halves[1]][1] for sort in (SCALES, a)):
                            cut = [c0, (c0 + c1) // 2, c1]
                        for d0, d1 in zip(cut, cut[1:]):
                            slot_words, w0, w1 = operand(a, e * C + d0, e * C + d1)
                            slot_scales, b0, b1 = operand(SCALES, e * C + d0, e * C + d1)
                            nc.tensor.matmul_mx(
                                out=dst[:, d0 - c0 : d1 - c0],
                                lhsT=words.bitcast(FP8X4),
                                lhsT_scale=scales,
                                rhs=slot_words[:, w0:w1].bitcast(FP8X4),
                                rhs_scale=slot_scales[PLANE[a] : P, b0:b1],
                                start=(a == 0 and d0 == c0),
                                stop=(a == passes - 1 and d1 == c1),
                            )
                    passes_done[e] += 1

        def empty_on_scalar(e):
            for product, c0, c1 in products[e]:
                nc.scalar.activation(y[:, e * C + c0 : e * C + c1], product, IDENTITY, bias=bias[e])

        def round_weights(m0, count, number, byte, dst):
            raw = berth(quay, f"w{m0}", [P, count, PACK, N], F32, number, byte)
            nc.sync.dma_start(raw[:].rearrange("p m j n -> p m (j n)"), w_view[:, m0 : m0 + count, :])
            if m0 in bias_behind:
                e0, e1 = bias_behind[m0]
                columns = held.tile([P, e1 - e0], F32, name=f"bias{e0}")
                nc.sync.dma_start(columns[:], b[:, e0:e1])
                for e in range(e0, e1):
                    bias[e] = columns[:, e - e0 : e - e0 + 1]
            interleave(dst, raw[:])

        def quantize_weights(m0, rounded):
            count = rounded.shape[1]
            words = held.tile([P, count, N], U32, name=f"w_words{m0}", align_bytes=64)
            scales = held.tile([P, count, N], U8, name=f"w_scales{m0}", align_bytes=64)
            nc.vector.quantize_mx(
                out=words[:].rearrange("p m n -> p (m n)").bitcast(FP8X4),
                scales=scales[:].rearrange("p m n -> p (m n)"),
                in_=rounded.rearrange("p m n j -> p (m n j)"),
            )
            for i in range(count):
                matrices[m0 + i] = (words[:, i, :], scales[:, i, :])

        piece_berth = (8, 9, 10, 11, 12, 13, 0, 1, 2, 3)
        gathers_behind = ((2, 0, T), (SCALES, T, T), (2, T, T), (SCALES, 2 * T, T), (2, 2 * T, 2 * C))
        bias_behind = {20: (0, 2), 28: (2, 4), 44: (4, E)}
        for group in range(5):
            rounded = berth(rounds, f"w_rounded{group}", [P, 8, N, PACK], BF16, (group + 2) % 3)
            for half in range(2):
                piece = 2 * group + half
                round_weights(4 * piece, 4, piece_berth[piece], 0, rounded[:, 4 * half : 4 * half + 4])
                for e in range(*bias_behind.get(4 * piece, (0, 0))):
                    empty_on_scalar(e)
            for half in range(2):
                quantize_weights(8 * group + 4 * half, rounded[:, 4 * half : 4 * half + 4])
            gather(*gathers_behind[group], piece_berth[2 * group + 1])
            multiply()
        rounded = berth(rounds, "w_rounded5", [P, 4, N, PACK], BF16, 1)
        for half, (s0, slots) in enumerate(((S - 3 * C, 2 * C), (S - C, C))):
            round_weights(40 + 2 * half, 2, 6, half * BERTH // 2, rounded[:, 2 * half : 2 * half + 2])
            quantize_weights(40 + 2 * half, rounded[:, 2 * half : 2 * half + 2])
            multiply()
            gather(2, s0, slots, 6, half * BERTH // 2)
            multiply()
        in_y = y[:, 13 * C : 14 * C].bitcast(BF16).rearrange("p (m n j) -> p m n j", m=1, j=PACK)
        round_weights(44, 1, 7, BERTH // 2, in_y)
        quantize_weights(44, in_y)
        multiply()
        for e in (4, 5, 6, 7, 8, 9, 10, 11, 12, 14):
            empty_on_scalar(e)
        nc.vector.tensor_scalar_add(y[:, 13 * C : 14 * C], products[13][0][0], bias[13])

        for pos_tile, pos in zip(pos_sb, (pos1, pos2, pos3)):
            nc.sync.dma_start(pos_tile[:], pos)
        gates = held.tile([P, TOP, vector_tokens], F32, tag="gates", name="gates", align_bytes=64)
        for r, c0, c1 in ((0, 0, 6), (1, 0, 4), (2, 0, 4), (1, 4, 6), (2, 4, 6)):
            nc.sync.dma_start(gates[:, r, c0 * P : c1 * P], gate[r, :, c0 * P : c1 * P])

        def entries(r, c0, c1):
            return pos_sb[r][:, c0 * P // STRIPE : c1 * P // STRIPE]

        turned = {}
        weighed = berth(quay, "weighed", [P, TOP, scalar_blocks, P], F32, 8)
        back = {c: bank(4 + c - VECTOR_BLOCKS, [P, P]) for c in range(VECTOR_BLOCKS, blocks)}

        def fetch(step):
            r, c0, c1 = FETCHES[step]
            plain = berth(quay, f"plain{step}", [P, c1 - c0, P], F32, 10, step % LAG * 2048)
            nc.scalar.activation(plain[:].rearrange("p c t -> p (c t)"), y[:].indirect(entries(r, c0, c1)), COPY)
            tile = bank(step % 4, [P, c1 - c0, P])
            for c in range(c0, c1):
                turned[r, c] = tile[:, c - c0, :]
                nc.tensor.transpose(turned[r, c], plain[:, c - c0, :], ident[:])

        def weigh_turned(step):
            r, c0, c1 = FETCHES[step]
            for c in range(c0, c1):
                column = c - VECTOR_BLOCKS
                term = weighed[:, r, c - VECTOR_BLOCKS, :]
                nc.scalar.activation(term, turned[r, c], COPY, scale=gate_columns[:, r, column : column + 1])
                nc.tensor.matmul(back[c][:], term, ident[:], start=(r == 2), stop=(r == 0), is_transpose=True)

        last = len(FETCHES) - 1
        for step in range(last + LAG):
            if step >= LAG:
                weigh_turned(step - LAG)
            if step <= last:
                fetch(step)
        handed = berth(quay, "handed", [P, scalar_blocks, P], F32, 10, (last - 1) % LAG * 2048)
        for c in (6, 7):
            nc.scalar.copy(handed[:, c - VECTOR_BLOCKS, :], back[c][:])
        weigh_turned(last)
        nc.scalar.copy(handed[:, 2, :], back[8][:])
        nc.scalar.dma_start(out[:, 6 * P : 9 * P], handed[:, :3, :].rearrange("p c t -> p (c t)"))
        nc.scalar.copy(handed[:, 3, :], back[9][:])
        nc.scalar.dma_start(out[:, 9 * P :], handed[:, 3, :])

        terms = [berth(quay, f"term{r}", [P, vector_tokens], F32, (12, 12, 0)[r], r % 2 * BERTH // 2) for r in range(TOP)]
        pair = berth(quay, "pair", [P, vector_tokens], F32, 0, BERTH // 2)
        result = berth(quay, "result", [P, vector_tokens], F32, 2)

        def weigh(r, c0, c1):
            columns = slice(c0 * P, c1 * P)
            nc.vector.tensor_tensor(terms[r][:, columns], y[:].indirect(entries(r, c0, c1)), gates[:, r, columns], MULT)

        def add_pair(c0, c1):
            columns = slice(c0 * P, c1 * P)
            nc.vector.tensor_tensor(pair[:, columns], terms[0][:, columns], terms[1][:, columns], ADD)

        def finish(c0, c1):
            columns = slice(c0 * P, c1 * P)
            nc.vector.tensor_tensor(result[:, columns], pair[:, columns], terms[2][:, columns], ADD)
            nc.sync.dma_start(out[:, columns], result[:, columns])

        weigh(0, 0, 6)
        weigh(1, 0, 4)
        weigh(2, 0, 4)
        add_pair(0, 4)
        weigh(1, 4, 6)
        finish(0, 4)
        weigh(2, 4, 6)
        add_pair(4, 5)
        add_pair(5, 6)
        finish(4, 5)
        finish(5, 6)
